import numpy as np
import ml_dtypes


def mxq(x, axis, fmt="e4m3"):
    dtype, down = {"e4m3": (ml_dtypes.float8_e4m3fn, 7), "e5m2": (ml_dtypes.float8_e5m2, 14)}[fmt]
    v = np.moveaxis(np.asarray(x, np.float32).astype(ml_dtypes.bfloat16).astype(np.float64), axis, -1)
    blocks = v.reshape(v.shape[:-1] + (-1, 32))
    amax = np.abs(blocks).max(-1, keepdims=True)
    byte = np.maximum(np.where(amax > 0, np.frexp(amax)[1] - 1 + 127, 0) - down, 1)
    scale = np.exp2(byte - 127.0)
    codes = (blocks / scale).astype(np.float32).astype(dtype).astype(np.float64)
    return np.moveaxis((codes * scale).reshape(v.shape), -1, axis)


WIDE = False


def mx_kscale(k):
    if not WIDE:
        return np.ones(k)
    levels = np.array([10, -10, 5, -5, 0])
    if k % 512:
        return np.exp2(np.random.permutation(np.resize(levels, k // 32))).repeat(32)
    a = np.empty((k // 512, 16))
    for p in range(k // 512):
        a[p, :8] = np.random.permutation(np.resize(levels, 8))
        for g in range(8):
            far = levels[np.abs(levels - a[p, g]) >= 10]
            a[p, g + 8] = far[np.random.randint(len(far))]
    return np.exp2(a.ravel()).repeat(32)


def f64(x):
    return np.asarray(x).astype(np.float64)


def striped(idx):
    return np.tile(idx.reshape(-1, 16).T, (8, 1)).astype(np.uint16)


def unstriped(offs):
    return offs[:16].T.reshape(-1).astype(np.int64)


def silu(v):
    return v / (1.0 + np.exp(-np.maximum(v, -700.0)))


K, T, D, S, V, N = 1024, 512, 4, 1024, 256, 128


def setup_inputs():
    n = np.random.standard_normal
    s = mx_kscale(K)[:, None]
    return {
        "xT": (n((K, T)) * s / np.sqrt(D)).astype(ml_dtypes.bfloat16).astype(np.float32),
        "w": (n((K, N)) / np.sqrt(K) / s).astype(np.float32),
        "b": (0.3 * n((N, 1))).astype(np.float32),
        "offs": striped(np.concatenate([np.random.permutation(T)[:V] for _ in range(D)])),
    }


def reference(xT, w, b, offs):
    idx = unstriped(offs)
    x = sum(f64(xT)[:, idx[d * V:(d + 1) * V]] for d in range(D))
    return silu((mxq(f64(w), 0, "e4m3").T @ mxq(x, 0, "e4m3")) + f64(b))

@@ -1,0 +1,130 @@
+from contextlib import ExitStack
+
+import concourse.mybir as mybir
+
+K, T, D, V, N = 1024, 512, 4, 256, 128
+FLOPS = 2 * K * N * V
+
+F32 = mybir.dt.float32
+BF16 = mybir.dt.bfloat16
+U32 = mybir.dt.uint32
+U16 = mybir.dt.uint16
+U8 = mybir.dt.uint8
+FP8X4 = mybir.dt.float8_e4m3fn_x4
+ADD = mybir.AluOpType.add
+SILU = mybir.ActivationFunctionType.Silu
+
+P = 128
+PACK = 4
+PASSES = K // (P * PACK)
+PAIRS = 2 * PASSES
+HALF = V // 2
+COLS = V // 16
+VEC_COLS = 320
+PIECES = (1, 2, 2, 4)
+
+
+def tile_picked_hash_lin_silu_sub_l_kernel(tc, xT, w, b, offs, out):
+    nc = tc.nc
+    with ExitStack() as ctx:
+        keep = ctx.enter_context(tc.tile_pool(name="keep", bufs=1))
+        psum = ctx.enter_context(tc.psum_pool(name="psum", bufs=1))
+
+        offsets = keep.tile([P, D * COLS], U16, name="offsets")
+        x_rows = xT.rearrange("(c p u e) t -> c u p e t", c=PASSES, p=P, u=2, e=2)
+        raw = [keep.tile([P, 2, T], F32, name=f"raw{q}") for q in range(PAIRS)]
+        w_raw = keep.tile([P, PASSES, PACK, N], F32, name="w_raw")
+        bias = keep.tile([P, 1], F32, name="bias")
+
+        nc.sync.dma_start(raw[0][:], x_rows[0, 0])
+        nc.sync.dma_start(offsets[:], offs)
+        for q in range(1, PAIRS):
+            nc.sync.dma_start(raw[q][:], x_rows[q // 2, q % 2])
+        nc.sync.dma_start(w_raw[:], w.rearrange("(c p j) n -> p c j n", c=PASSES, p=P, j=PACK))
+        nc.sync.dma_start(bias[:], b)
+
+        warm = keep.tile([P, 1], F32, name="warm")
+        warm_out = keep.tile([P, 1], F32, name="warm_out")
+        nc.vector.memset(warm[:], 0.0)
+        nc.scalar.activation(warm_out[:], warm[:], SILU)
+
+        tables = keep.tile([P, PAIRS, T, 2], BF16, name="tables", align_bytes=64)
+        words = tables[:].rearrange("p s t e -> p (s t e)").bitcast(U32)
+        table = [tables[:, PAIRS - 1 - q] for q in range(PAIRS)]
+        src = [raw[q][:].rearrange("p e t -> p t e") for q in range(PAIRS)]
+        nc.vector.tensor_copy(table[0][:, :VEC_COLS, :], src[0][:, :VEC_COLS, :])
+        nc.scalar.copy(table[0][:, VEC_COLS:, :], src[0][:, VEC_COLS:, :])
+        for q in range(1, PAIRS):
+            nc.scalar.copy(table[q], src[q])
+        w_grouped = keep.tile([P, PASSES, N, PACK], BF16, name="w_grouped", align_bytes=64)
+        nc.scalar.copy(w_grouped[:], w_raw[:].rearrange("p c j n -> p c n j"))
+
+        picked = [keep.tile([P, D, V], U32, name=f"picked{q}", align_bytes=64) for q in range(PAIRS)]
+        partial = [keep.tile([P, 2, 2, V, 2], F32, name=f"partial{c}", align_bytes=64) for c in range(PASSES)]
+        for q in range(PAIRS):
+            step = PIECES[q]
+            first = (PAIRS - 1 - q) * T
+            window = words[:, first : first + 2 * step * V]
+            for d in range(step - 1, D, step):
+                nc.vector.tensor_copy(
+                    picked[q][:, d + 1 - step : d + 1, :].rearrange("p d v -> p (d v)"),
+                    window.indirect(offsets[:, (d + 1 - step) * COLS : (d + 1) * COLS]),
+                )
+                if d % 2 == 1 and q < PAIRS - 1:
+                    nc.gpsimd.tensor_tensor(
+                        partial[q // 2][:, q % 2, d // 2].rearrange("p v e -> p (v e)"),
+                        picked[q][:, d - 1, :].bitcast(BF16),
+                        picked[q][:, d, :].bitcast(BF16),
+                        ADD,
+                    )
+
+        x_grouped = [keep.tile([P, V, 2, 2], BF16, name=f"x_grouped{c}", align_bytes=64) for c in range(PASSES)]
+        x_codes = keep.tile([P, PASSES, V], U32, name="x_codes", align_bytes=64)
+        x_scales = keep.tile([P, PASSES, V], U8, name="x_scales", align_bytes=64)
+        w_codes = keep.tile([P, PASSES * N], U32, name="w_codes", align_bytes=64)
+        w_scales = keep.tile([P, PASSES * N], U8, name="w_scales", align_bytes=64)
+
+        def final_sum(c, lo, hi):
+            both = partial[c][:, :, :, lo:hi, :].rearrange("p u h v e -> p h v u e")
+            nc.vector.tensor_tensor(x_grouped[c][:, lo:hi], both[:, 0], both[:, 1], ADD)
+
+        def quantize_x(c, lo, hi):
+            nc.vector.quantize_mx(
+                out=x_codes[:, c, lo:hi].bitcast(FP8X4),
+                scales=x_scales[:, c, lo:hi],
+                in_=x_grouped[c][:, lo:hi].rearrange("p v u e -> p (v u e)"),
+            )
+
+        final_sum(0, 0, V)
+        last = picked[PAIRS - 1][:].bitcast(BF16).rearrange("p (h g) m -> p h g m", g=2)
+        nc.vector.tensor_tensor(
+            partial[1][:, 1].rearrange("p h v e -> p h (v e)"), last[:, :, 0, :], last[:, :, 1, :], ADD
+        )
+        nc.vector.quantize_mx(
+            out=w_codes[:].bitcast(FP8X4),
+            scales=w_scales[:],
+            in_=w_grouped[:].rearrange("p c n j -> p (c n j)"),
+        )
+        final_sum(1, 0, HALF)
+        quantize_x(0, 0, V)
+        final_sum(1, HALF, V)
+        quantize_x(1, 0, HALF)
+        quantize_x(1, HALF, V)
+
+        acc = [psum.tile([P, HALF], F32, name=f"acc{h}") for h in range(2)]
+        result = [keep.tile([P, HALF], F32, name=f"result{h}") for h in range(2)]
+        for c in range(PASSES):
+            for h in range(2):
+                cols = slice(h * HALF, (h + 1) * HALF)
+                nc.tensor.matmul_mx(
+                    out=acc[h][:],
+                    lhsT=w_codes[:, c * N : (c + 1) * N].bitcast(FP8X4),
+                    lhsT_scale=w_scales[:, c * N : (c + 1) * N],
+                    rhs=x_codes[:, c, cols].bitcast(FP8X4),
+                    rhs_scale=x_scales[:, c, cols],
+                    start=(c == 0),
+                    stop=(c == PASSES - 1),
+                )
+        for h in range(2):
+            nc.scalar.activation(result[h][:], acc[h][:], SILU, bias=bias[:])
+            nc.sync.dma_start(out[:, h * HALF : (h + 1) * HALF], result[h][:])

@@ -1,6 +1,7 @@
 from contextlib import ExitStack
 
 import concourse.mybir as mybir
+from concourse.masks import make_identity
 
 K, T, D, V, N = 1024, 512, 4, 256, 128
 FLOPS = 2 * K * N * V
@@ -20,7 +21,8 @@ PASSES = K // (P * PACK)
 PAIRS = 2 * PASSES
 HALF = V // 2
 COLS = V // 16
-VEC_COLS = 320
+BLOCKS = 2 * V // P
+VEC_COLS = 416
 PIECES = (1, 2, 2, 4)
 
 
@@ -36,7 +38,8 @@ def tile_picked_hash_lin_silu_sub_l_kernel(tc, xT, w, b, offs, out):
         w_raw = keep.tile([P, PASSES, PACK, N], F32, name="w_raw")
         bias = keep.tile([P, 1], F32, name="bias")
 
-        nc.sync.dma_start(raw[0][:], x_rows[0, 0])
+        for lo in (0, T // 2):
+            nc.sync.dma_start(raw[0][:, :, lo : lo + T // 2], x_rows[0, 0][:, :, lo : lo + T // 2])
         nc.sync.dma_start(offsets[:], offs)
         for q in range(1, PAIRS):
             nc.sync.dma_start(raw[q][:], x_rows[q // 2, q % 2])
@@ -48,11 +51,17 @@ def tile_picked_hash_lin_silu_sub_l_kernel(tc, xT, w, b, offs, out):
         nc.vector.memset(warm[:], 0.0)
         nc.scalar.activation(warm_out[:], warm[:], SILU)
 
+        ident32 = keep.tile([P, P], F32, name="ident32")
+        ident16 = keep.tile([P, P], BF16, name="ident16")
+        make_identity(nc, ident32[:])
+        make_identity(nc, ident16[:])
+
         tables = keep.tile([P, PAIRS, T, 2], BF16, name="tables", align_bytes=64)
         words = tables[:].rearrange("p s t e -> p (s t e)").bitcast(U32)
         table = [tables[:, PAIRS - 1 - q] for q in range(PAIRS)]
         src = [raw[q][:].rearrange("p e t -> p t e") for q in range(PAIRS)]
-        nc.vector.tensor_copy(table[0][:, :VEC_COLS, :], src[0][:, :VEC_COLS, :])
+        nc.vector.tensor_copy(table[0][:, : T // 2, :], src[0][:, : T // 2, :])
+        nc.vector.tensor_copy(table[0][:, T // 2 : VEC_COLS, :], src[0][:, T // 2 : VEC_COLS, :])
         nc.scalar.copy(table[0][:, VEC_COLS:, :], src[0][:, VEC_COLS:, :])
         for q in range(1, PAIRS):
             nc.scalar.copy(table[q], src[q])
@@ -60,7 +69,8 @@ def tile_picked_hash_lin_silu_sub_l_kernel(tc, xT, w, b, offs, out):
         nc.scalar.copy(w_grouped[:], w_raw[:].rearrange("p c j n -> p c n j"))
 
         picked = [keep.tile([P, D, V], U32, name=f"picked{q}", align_bytes=64) for q in range(PAIRS)]
-        partial = [keep.tile([P, 2, 2, V, 2], F32, name=f"partial{c}", align_bytes=64) for c in range(PASSES)]
+        partials = [keep.tile([P, 2, 2, 2 * V], F32, name=f"partials{c}", align_bytes=64) for c in range(PASSES)]
+        partial = [partials[q // 2][:, q % 2] for q in range(PAIRS)]
         for q in range(PAIRS):
             step = PIECES[q]
             first = (PAIRS - 1 - q) * T
@@ -72,7 +82,7 @@ def tile_picked_hash_lin_silu_sub_l_kernel(tc, xT, w, b, offs, out):
                 )
                 if d % 2 == 1 and q < PAIRS - 1:
                     nc.gpsimd.tensor_tensor(
-                        partial[q // 2][:, q % 2, d // 2].rearrange("p v e -> p (v e)"),
+                        partial[q][:, d // 2, :],
                         picked[q][:, d - 1, :].bitcast(BF16),
                         picked[q][:, d, :].bitcast(BF16),
                         ADD,
@@ -84,9 +94,29 @@ def tile_picked_hash_lin_silu_sub_l_kernel(tc, xT, w, b, offs, out):
         w_codes = keep.tile([P, PASSES * N], U32, name="w_codes", align_bytes=64)
         w_scales = keep.tile([P, PASSES * N], U8, name="w_scales", align_bytes=64)
 
-        def final_sum(c, lo, hi):
-            both = partial[c][:, :, :, lo:hi, :].rearrange("p u h v e -> p h v u e")
-            nc.vector.tensor_tensor(x_grouped[c][:, lo:hi], both[:, 0], both[:, 1], ADD)
+        back = psum.tile([P, 2, V, 2], BF16, name="back")
+        for q in range(2):
+            summed = psum.tile([P, BLOCKS, P], F32, name=f"summed{q}")
+            for j in range(BLOCKS):
+                for h in range(2):
+                    nc.tensor.matmul(
+                        summed[:, j, :],
+                        lhsT=partial[q][:, h, j * P : (j + 1) * P],
+                        rhs=ident32[:],
+                        start=(h == 0),
+                        stop=(h == 1),
+                        is_transpose=True,
+                    )
+            turned = keep.tile([P, BLOCKS, P], BF16, name=f"turned{q}")
+            nc.scalar.copy(turned[:], summed[:])
+            flat = back[:, q].rearrange("p v e -> p (v e)")
+            for j in range(BLOCKS):
+                nc.tensor.transpose(flat[:, j * P : (j + 1) * P], turned[:, j, :], ident16[:])
+        nc.scalar.copy(x_grouped[0][:], back[:].rearrange("p u v e -> p v u e"))
+
+        def final_sum(lo, hi):
+            both = partials[1][:].rearrange("p u h (v e) -> p h v u e", e=2)
+            nc.vector.tensor_tensor(x_grouped[1][:, lo:hi], both[:, 0, lo:hi], both[:, 1, lo:hi], ADD)
 
         def quantize_x(c, lo, hi):
             nc.vector.quantize_mx(
@@ -95,25 +125,24 @@ def tile_picked_hash_lin_silu_sub_l_kernel(tc, xT, w, b, offs, out):
                 in_=x_grouped[c][:, lo:hi].rearrange("p v u e -> p (v u e)"),
             )
 
-        final_sum(0, 0, V)
         last = picked[PAIRS - 1][:].bitcast(BF16).rearrange("p (h g) m -> p h g m", g=2)
         nc.vector.tensor_tensor(
-            partial[1][:, 1].rearrange("p h v e -> p h (v e)"), last[:, :, 0, :], last[:, :, 1, :], ADD
+            partial[PAIRS - 1], last[:, :, 0, :], last[:, :, 1, :], ADD
         )
         nc.vector.quantize_mx(
             out=w_codes[:].bitcast(FP8X4),
             scales=w_scales[:],
             in_=w_grouped[:].rearrange("p c n j -> p (c n j)"),
         )
-        final_sum(1, 0, HALF)
-        quantize_x(0, 0, V)
-        final_sum(1, HALF, V)
-        quantize_x(1, 0, HALF)
-        quantize_x(1, HALF, V)
+        final_sum(0, HALF)
+        final_sum(HALF, V)
+        for c in (1, 0):
+            quantize_x(c, 0, HALF)
+            quantize_x(c, HALF, V)
 
         acc = [psum.tile([P, HALF], F32, name=f"acc{h}") for h in range(2)]
         result = [keep.tile([P, HALF], F32, name=f"result{h}") for h in range(2)]
-        for c in range(PASSES):
+        for c in (1, 0):
             for h in range(2):
                 cols = slice(h * HALF, (h + 1) * HALF)
                 nc.tensor.matmul_mx(
@@ -122,8 +151,8 @@ def tile_picked_hash_lin_silu_sub_l_kernel(tc, xT, w, b, offs, out):
                     lhsT_scale=w_scales[:, c * N : (c + 1) * N],
                     rhs=x_codes[:, c, cols].bitcast(FP8X4),
                     rhs_scale=x_scales[:, c, cols],
-                    start=(c == 0),
-                    stop=(c == PASSES - 1),
+                    start=(c == 1),
+                    stop=(c == 0),
                 )
         for h in range(2):
             nc.scalar.activation(result[h][:], acc[h][:], SILU, bias=bias[:])

@@ -21,9 +21,6 @@ PASSES = K // (P * PACK)
 PAIRS = 2 * PASSES
 HALF = V // 2
 COLS = V // 16
-BLOCKS = 2 * V // P
-VEC_COLS = 416
-PIECES = (1, 2, 2, 4)
 
 
 def tile_picked_hash_lin_silu_sub_l_kernel(tc, xT, w, b, offs, out):
@@ -34,15 +31,19 @@ def tile_picked_hash_lin_silu_sub_l_kernel(tc, xT, w, b, offs, out):
 
         offsets = keep.tile([P, D * COLS], U16, name="offsets")
         x_rows = xT.rearrange("(c p u e) t -> c u p e t", c=PASSES, p=P, u=2, e=2)
-        raw = [keep.tile([P, 2, T], F32, name=f"raw{q}") for q in range(PAIRS)]
+        rows = keep.tile([P, T + PAIRS * 2 * T], F32, name="rows", align_bytes=64)
+        A, C, Dd, B = (1, 0), (0, 0), (0, 1), (1, 1)
+        order = [A, C, Dd, B]
+        start = {q: T + (PAIRS - 1 - i) * 2 * T for i, q in enumerate(order)}
+        raw = {q: rows[:, start[q] : start[q] + 2 * T].rearrange("p (e t) -> p e t", e=2) for q in order}
         w_raw = keep.tile([P, PASSES, PACK, N], F32, name="w_raw")
         bias = keep.tile([P, 1], F32, name="bias")
 
         for lo in (0, T // 2):
-            nc.sync.dma_start(raw[0][:, :, lo : lo + T // 2], x_rows[0, 0][:, :, lo : lo + T // 2])
+            nc.sync.dma_start(raw[A][:, :, lo : lo + T // 2], x_rows[A][:, :, lo : lo + T // 2])
         nc.sync.dma_start(offsets[:], offs)
-        for q in range(1, PAIRS):
-            nc.sync.dma_start(raw[q][:], x_rows[q // 2, q % 2])
+        for q in order[1:]:
+            nc.sync.dma_start(raw[q], x_rows[q])
         nc.sync.dma_start(w_raw[:], w.rearrange("(c p j) n -> p c j n", c=PASSES, p=P, j=PACK))
         nc.sync.dma_start(bias[:], b)
 
@@ -56,101 +57,137 @@ def tile_picked_hash_lin_silu_sub_l_kernel(tc, xT, w, b, offs, out):
         make_identity(nc, ident32[:])
         make_identity(nc, ident16[:])
 
-        tables = keep.tile([P, PAIRS, T, 2], BF16, name="tables", align_bytes=64)
-        words = tables[:].rearrange("p s t e -> p (s t e)").bitcast(U32)
-        table = [tables[:, PAIRS - 1 - q] for q in range(PAIRS)]
-        src = [raw[q][:].rearrange("p e t -> p t e") for q in range(PAIRS)]
-        nc.vector.tensor_copy(table[0][:, : T // 2, :], src[0][:, : T // 2, :])
-        nc.vector.tensor_copy(table[0][:, T // 2 : VEC_COLS, :], src[0][:, T // 2 : VEC_COLS, :])
-        nc.scalar.copy(table[0][:, VEC_COLS:, :], src[0][:, VEC_COLS:, :])
-        for q in range(1, PAIRS):
-            nc.scalar.copy(table[q], src[q])
+        words = rows[:].bitcast(U32)
+        values = rows[:].bitcast(BF16)
+        halves = values.rearrange("p (t h) -> p t h", h=2)
+
+        def pack(copy, q, lo, hi):
+            copy(halves[:, start[q] + T + lo : start[q] + T + hi, 0], halves[:, start[q] + lo : start[q] + hi, 1])
+
+        pack(nc.vector.tensor_copy, A, 0, T // 2)
+        pack(nc.vector.tensor_copy, A, T // 2, T)
+        for q in order[1:]:
+            pack(nc.scalar.copy, q, 0, T)
+
+        def gather(dst, q, d, pieces, columns):
+            first = start[q] + T
+            window = words[:, first : first + columns]
+            nc.vector.tensor_copy(dst, window.indirect(offsets[:, d * COLS : (d + pieces) * COLS]))
+
+        def add_two(dst, two):
+            nc.gpsimd.tensor_tensor(dst, two[:, :V].bitcast(BF16), two[:, V:].bitcast(BF16), ADD)
+
+        three = keep.tile([P, 2, 2 * V], F32, name="three", align_bytes=64)
+        two = {q: keep.tile([P, 2 * V], U32, name=f"two{i}", align_bytes=64) for i, q in enumerate(order)}
+        part = {q: keep.tile([P, 2 * V], F32, name=f"part{i}", align_bytes=64) for i, q in enumerate(order)}
+        third = {q: keep.tile([P, V], U32, name=f"third{q[1]}", align_bytes=64) for q in (A, B)}
+
+        gather(two[A][:, :V], A, 0, 1, T)
+        gather(two[A][:, V:], A, 1, 1, T)
+        add_two(part[A][:], two[A])
+        gather(third[A][:], A, 2, 1, T)
+        nc.gpsimd.tensor_tensor(three[:, 0, :], part[A][:], third[A][:].bitcast(BF16), ADD)
+
+        gather(two[C][:], C, 0, 2, 2 * T)
+        add_two(part[C][:], two[C])
+        c_late = keep.tile([P, 2 * V], U32, name="c_late", align_bytes=64)
+        gather(c_late[:], C, 2, 2, 2 * T)
+        c_wide = rows[:, 0 : 2 * T]
+        nc.scalar.copy(c_wide, c_late[:].bitcast(BF16))
         w_grouped = keep.tile([P, PASSES, N, PACK], BF16, name="w_grouped", align_bytes=64)
         nc.scalar.copy(w_grouped[:], w_raw[:].rearrange("p c j n -> p c n j"))
 
-        picked = [keep.tile([P, D, V], U32, name=f"picked{q}", align_bytes=64) for q in range(PAIRS)]
-        partials = [keep.tile([P, 2, 2, 2 * V], F32, name=f"partials{c}", align_bytes=64) for c in range(PASSES)]
-        partial = [partials[q // 2][:, q % 2] for q in range(PAIRS)]
-        for q in range(PAIRS):
-            step = PIECES[q]
-            first = (PAIRS - 1 - q) * T
-            window = words[:, first : first + 2 * step * V]
-            for d in range(step - 1, D, step):
-                nc.vector.tensor_copy(
-                    picked[q][:, d + 1 - step : d + 1, :].rearrange("p d v -> p (d v)"),
-                    window.indirect(offsets[:, (d + 1 - step) * COLS : (d + 1) * COLS]),
-                )
-                if d % 2 == 1 and q < PAIRS - 1:
-                    nc.gpsimd.tensor_tensor(
-                        partial[q][:, d // 2, :],
-                        picked[q][:, d - 1, :].bitcast(BF16),
-                        picked[q][:, d, :].bitcast(BF16),
-                        ADD,
-                    )
+        gather(two[Dd][:], Dd, 0, 2, 2 * T)
+        add_two(part[Dd][:], two[Dd])
+        gather(two[B][:], B, 0, 2, 2 * T)
+        add_two(part[B][:], two[B])
+        d_wide = [keep.tile([P, 2 * V], F32, name=f"d_wide{g}", align_bytes=64) for g in range(2)]
+        for g in range(2):
+            at = start[Dd] + g * V
+            gather(words[:, at : at + V], Dd, 2 + g, 1, 2 * T)
+            nc.scalar.copy(d_wide[g][:], values[:, 2 * at : 2 * (at + V)])
+        gather(third[B][:], B, 2, 1, T)
+        nc.gpsimd.tensor_tensor(three[:, 1, :], part[B][:], third[B][:].bitcast(BF16), ADD)
+        for u, q in enumerate((A, B)):
+            at = start[C] + u * V
+            gather(words[:, at : at + V], q, 3, 1, T)
+        fourth = values[:, 2 * start[C] : 2 * (start[C] + 2 * V)]
 
-        x_grouped = [keep.tile([P, V, 2, 2], BF16, name=f"x_grouped{c}", align_bytes=64) for c in range(PASSES)]
-        x_codes = keep.tile([P, PASSES, V], U32, name="x_codes", align_bytes=64)
-        x_scales = keep.tile([P, PASSES, V], U8, name="x_scales", align_bytes=64)
-        w_codes = keep.tile([P, PASSES * N], U32, name="w_codes", align_bytes=64)
-        w_scales = keep.tile([P, PASSES * N], U8, name="w_scales", align_bytes=64)
-
-        back = psum.tile([P, 2, V, 2], BF16, name="back")
-        for q in range(2):
-            summed = psum.tile([P, BLOCKS, P], F32, name=f"summed{q}")
-            for j in range(BLOCKS):
-                for h in range(2):
+        def sum_turned(name, parts):
+            blocks = 2 * V // P
+            summed = psum.tile([P, blocks, P], F32, name=f"summed_{name}")
+            for i, term in enumerate(parts):
+                for j in range(blocks):
                     nc.tensor.matmul(
                         summed[:, j, :],
-                        lhsT=partial[q][:, h, j * P : (j + 1) * P],
+                        lhsT=term[:, j * P : (j + 1) * P],
                         rhs=ident32[:],
-                        start=(h == 0),
-                        stop=(h == 1),
+                        start=(i == 0 and j == 0),
+                        stop=(i == len(parts) - 1 and j == blocks - 1),
                         is_transpose=True,
                     )
-            turned = keep.tile([P, BLOCKS, P], BF16, name=f"turned{q}")
+            turned = keep.tile([P, blocks, P], BF16, name=f"turned_{name}")
             nc.scalar.copy(turned[:], summed[:])
-            flat = back[:, q].rearrange("p v e -> p (v e)")
-            for j in range(BLOCKS):
-                nc.tensor.transpose(flat[:, j * P : (j + 1) * P], turned[:, j, :], ident16[:])
-        nc.scalar.copy(x_grouped[0][:], back[:].rearrange("p u v e -> p v u e"))
+            return turned
 
-        def final_sum(lo, hi):
-            both = partials[1][:].rearrange("p u h (v e) -> p h v u e", e=2)
-            nc.vector.tensor_tensor(x_grouped[1][:, lo:hi], both[:, 0, lo:hi], both[:, 1, lo:hi], ADD)
-
-        def quantize_x(c, lo, hi):
-            nc.vector.quantize_mx(
-                out=x_codes[:, c, lo:hi].bitcast(FP8X4),
-                scales=x_scales[:, c, lo:hi],
-                in_=x_grouped[c][:, lo:hi].rearrange("p v u e -> p (v u e)"),
+        turned = [
+            sum_turned("c", [part[C][:], c_wide[:, : 2 * V], c_wide[:, 2 * V :]]),
+            sum_turned("d", [part[Dd][:], d_wide[0][:], d_wide[1][:]]),
+        ]
+        grouped0 = keep.tile([P, PACK * V], BF16, name="grouped0", align_bytes=64)
+        backs = [psum.tile([P, 2, 2 * HALF], BF16, name=f"back{h}", tag=f"last{h}") for h in range(2)]
+        for u in range(2):
+            for h in range(2):
+                for j in range(2):
+                    nc.tensor.transpose(backs[h][:, u, j * P : (j + 1) * P], turned[u][:, 2 * h + j, :], ident16[:])
+        for h in range(2):
+            nc.scalar.copy(
+                grouped0[:, h * PACK * HALF : (h + 1) * PACK * HALF].bitcast(F32).rearrange("p (v u) -> p v u", u=2),
+                backs[h][:].bitcast(F32).rearrange("p u v -> p v u"),
             )
 
-        last = picked[PAIRS - 1][:].bitcast(BF16).rearrange("p (h g) m -> p h g m", g=2)
-        nc.vector.tensor_tensor(
-            partial[PAIRS - 1], last[:, :, 0, :], last[:, :, 1, :], ADD
-        )
+        w_codes = keep.tile([P, PASSES * N], U32, name="w_codes", align_bytes=64)
+        x_codes = keep.tile([P, PASSES * V], U32, name="x_codes", align_bytes=64)
+        w_scales = keep.tile([P, PASSES * N], U8, name="w_scales", align_bytes=64)
+        x_scales = keep.tile([P, PASSES * V], U8, name="x_scales", align_bytes=64)
+
+        def quantize_x(c, grouped, h):
+            first = c * V + h * HALF
+            nc.vector.quantize_mx(
+                out=x_codes[:, first : first + HALF].bitcast(FP8X4),
+                scales=x_scales[:, first : first + HALF],
+                in_=grouped[:, h * PACK * HALF : (h + 1) * PACK * HALF],
+            )
+
+        grouped1 = keep.tile([P, PACK * V], BF16, name="grouped1", align_bytes=64)
+        for h in range(2):
+            ids = slice(h * HALF, (h + 1) * HALF)
+            nc.vector.tensor_tensor(
+                grouped1[:].rearrange("p (v u e) -> p v u e", u=2, e=2)[:, ids],
+                three[:].rearrange("p u (v e) -> p v u e", e=2)[:, ids],
+                fourth.rearrange("p (u v e) -> p v u e", u=2, e=2)[:, ids],
+                ADD,
+            )
         nc.vector.quantize_mx(
             out=w_codes[:].bitcast(FP8X4),
             scales=w_scales[:],
             in_=w_grouped[:].rearrange("p c n j -> p (c n j)"),
         )
-        final_sum(0, HALF)
-        final_sum(HALF, V)
-        for c in (1, 0):
-            quantize_x(c, 0, HALF)
-            quantize_x(c, HALF, V)
+        for c, grouped in ((1, grouped1), (0, grouped0)):
+            for h in range(2):
+                quantize_x(c, grouped, h)
 
-        acc = [psum.tile([P, HALF], F32, name=f"acc{h}") for h in range(2)]
+        acc = [psum.tile([P, HALF], F32, name=f"acc{h}", tag=f"last{h}") for h in range(2)]
         result = [keep.tile([P, HALF], F32, name=f"result{h}") for h in range(2)]
         for c in (1, 0):
             for h in range(2):
-                cols = slice(h * HALF, (h + 1) * HALF)
+                cols = slice(c * V + h * HALF, c * V + (h + 1) * HALF)
                 nc.tensor.matmul_mx(
                     out=acc[h][:],
                     lhsT=w_codes[:, c * N : (c + 1) * N].bitcast(FP8X4),
                     lhsT_scale=w_scales[:, c * N : (c + 1) * N],
-                    rhs=x_codes[:, c, cols].bitcast(FP8X4),
-                    rhs_scale=x_scales[:, c, cols],
+                    rhs=x_codes[:, cols].bitcast(FP8X4),
+                    rhs_scale=x_scales[:, cols],
                     start=(c == 1),
                     stop=(c == 0),
                 )

@@ -21,6 +21,9 @@ PASSES = K // (P * PACK)
 PAIRS = 2 * PASSES
 HALF = V // 2
 COLS = V // 16
+VEC_COLS = 416
+WINDOW = {1: T, 2: 704, 3: 2 * T}
+LAST = WINDOW[2] + 4 * V
 
 
 def tile_picked_hash_lin_silu_sub_l_kernel(tc, xT, w, b, offs, out):
@@ -31,20 +34,23 @@ def tile_picked_hash_lin_silu_sub_l_kernel(tc, xT, w, b, offs, out):
 
         offsets = keep.tile([P, D * COLS], U16, name="offsets")
         x_rows = xT.rearrange("(c p u e) t -> c u p e t", c=PASSES, p=P, u=2, e=2)
-        rows = keep.tile([P, T + PAIRS * 2 * T], F32, name="rows", align_bytes=64)
         A, C, Dd, B = (1, 0), (0, 0), (0, 1), (1, 1)
-        order = [A, C, Dd, B]
-        start = {q: T + (PAIRS - 1 - i) * 2 * T for i, q in enumerate(order)}
-        raw = {q: rows[:, start[q] : start[q] + 2 * T].rearrange("p (e t) -> p e t", e=2) for q in order}
-        w_raw = keep.tile([P, PASSES, PACK, N], F32, name="w_raw")
+        order = [C, A, Dd, B]
+        rows = {
+            q: keep.tile([P, LAST if q == B else 2 * T], F32, name=f"rows{i}", align_bytes=64)
+            for i, q in enumerate(order)
+        }
+        raw = {q: rows[q][:, : 2 * T].rearrange("p (e t) -> p e t", e=2) for q in order}
+        w_rows = keep.tile([P, PASSES * PACK * N + V], F32, name="w_rows", align_bytes=64)
+        w_raw = w_rows[:, : PASSES * PACK * N].rearrange("p (c j n) -> p c j n", c=PASSES, j=PACK)
         bias = keep.tile([P, 1], F32, name="bias")
 
         for lo in (0, T // 2):
-            nc.sync.dma_start(raw[A][:, :, lo : lo + T // 2], x_rows[A][:, :, lo : lo + T // 2])
+            nc.sync.dma_start(raw[C][:, :, lo : lo + T // 2], x_rows[C][:, :, lo : lo + T // 2])
         nc.sync.dma_start(offsets[:], offs)
         for q in order[1:]:
             nc.sync.dma_start(raw[q], x_rows[q])
-        nc.sync.dma_start(w_raw[:], w.rearrange("(c p j) n -> p c j n", c=PASSES, p=P, j=PACK))
+        nc.sync.dma_start(w_raw, w.rearrange("(c p j) n -> p c j n", c=PASSES, p=P, j=PACK))
         nc.sync.dma_start(bias[:], b)
 
         warm = keep.tile([P, 1], F32, name="warm")
@@ -57,89 +63,99 @@ def tile_picked_hash_lin_silu_sub_l_kernel(tc, xT, w, b, offs, out):
         make_identity(nc, ident32[:])
         make_identity(nc, ident16[:])
 
-        words = rows[:].bitcast(U32)
-        values = rows[:].bitcast(BF16)
-        halves = values.rearrange("p (t h) -> p t h", h=2)
-
         def pack(copy, q, lo, hi):
-            copy(halves[:, start[q] + T + lo : start[q] + T + hi, 0], halves[:, start[q] + lo : start[q] + hi, 1])
+            halves = rows[q][:, : 2 * T].bitcast(BF16).rearrange("p (t h) -> p t h", h=2)
+            copy(halves[:, lo:hi, 0], halves[:, T + lo : T + hi, 1])
 
-        pack(nc.vector.tensor_copy, A, 0, T // 2)
-        pack(nc.vector.tensor_copy, A, T // 2, T)
+        pack(nc.vector.tensor_copy, C, 0, T // 2)
+        pack(nc.vector.tensor_copy, C, T // 2, VEC_COLS)
+        pack(nc.scalar.copy, C, VEC_COLS, T)
         for q in order[1:]:
             pack(nc.scalar.copy, q, 0, T)
 
-        def gather(dst, q, d, pieces, columns):
-            first = start[q] + T
-            window = words[:, first : first + columns]
+        def gather(dst, q, d, pieces):
+            window = rows[q][:, : WINDOW[pieces]].bitcast(U32)
             nc.vector.tensor_copy(dst, window.indirect(offsets[:, d * COLS : (d + pieces) * COLS]))
 
-        def add_two(dst, two):
-            nc.gpsimd.tensor_tensor(dst, two[:, :V].bitcast(BF16), two[:, V:].bitcast(BF16), ADD)
+        def add(dst, first, second):
+            nc.gpsimd.tensor_tensor(dst, first, second, ADD)
 
+        def add_turned(bank, term, first, last):
+            count = bank.shape[1]
+            for j in range(count):
+                nc.tensor.matmul(
+                    bank[:, j, :],
+                    lhsT=term[:, j * P : (j + 1) * P],
+                    rhs=ident32[:],
+                    start=(first and j == 0),
+                    stop=(last and j == count - 1),
+                    is_transpose=True,
+                )
+
+        blocks = 2 * V // P
         three = keep.tile([P, 2, 2 * V], F32, name="three", align_bytes=64)
-        two = {q: keep.tile([P, 2 * V], U32, name=f"two{i}", align_bytes=64) for i, q in enumerate(order)}
-        part = {q: keep.tile([P, 2 * V], F32, name=f"part{i}", align_bytes=64) for i, q in enumerate(order)}
-        third = {q: keep.tile([P, V], U32, name=f"third{q[1]}", align_bytes=64) for q in (A, B)}
 
-        gather(two[A][:, :V], A, 0, 1, T)
-        gather(two[A][:, V:], A, 1, 1, T)
-        add_two(part[A][:], two[A])
-        gather(third[A][:], A, 2, 1, T)
-        nc.gpsimd.tensor_tensor(three[:, 0, :], part[A][:], third[A][:].bitcast(BF16), ADD)
-
-        gather(two[C][:], C, 0, 2, 2 * T)
-        add_two(part[C][:], two[C])
-        c_late = keep.tile([P, 2 * V], U32, name="c_late", align_bytes=64)
-        gather(c_late[:], C, 2, 2, 2 * T)
-        c_wide = rows[:, 0 : 2 * T]
-        nc.scalar.copy(c_wide, c_late[:].bitcast(BF16))
-        w_grouped = keep.tile([P, PASSES, N, PACK], BF16, name="w_grouped", align_bytes=64)
-        nc.scalar.copy(w_grouped[:], w_raw[:].rearrange("p c j n -> p c n j"))
-
-        gather(two[Dd][:], Dd, 0, 2, 2 * T)
-        add_two(part[Dd][:], two[Dd])
-        gather(two[B][:], B, 0, 2, 2 * T)
-        add_two(part[B][:], two[B])
-        d_wide = [keep.tile([P, 2 * V], F32, name=f"d_wide{g}", align_bytes=64) for g in range(2)]
+        c_sum = psum.tile([P, blocks, P], F32, name="c_sum")
         for g in range(2):
-            at = start[Dd] + g * V
-            gather(words[:, at : at + V], Dd, 2 + g, 1, 2 * T)
-            nc.scalar.copy(d_wide[g][:], values[:, 2 * at : 2 * (at + V)])
-        gather(third[B][:], B, 2, 1, T)
-        nc.gpsimd.tensor_tensor(three[:, 1, :], part[B][:], third[B][:].bitcast(BF16), ADD)
-        for u, q in enumerate((A, B)):
-            at = start[C] + u * V
-            gather(words[:, at : at + V], q, 3, 1, T)
-        fourth = values[:, 2 * start[C] : 2 * (start[C] + 2 * V)]
+            two = keep.tile([P, 2 * V], U32, name=f"c_two{g}", align_bytes=64)
+            gather(two[:], C, 2 * g, 2)
+            part = keep.tile([P, 2 * V], F32, name=f"c_part{g}", align_bytes=64)
+            add(part[:], two[:, :V].bitcast(BF16), two[:, V:].bitcast(BF16))
+            add_turned(c_sum[:], part[:], g == 0, g == 1)
 
-        def sum_turned(name, parts):
-            blocks = 2 * V // P
-            summed = psum.tile([P, blocks, P], F32, name=f"summed_{name}")
-            for i, term in enumerate(parts):
-                for j in range(blocks):
-                    nc.tensor.matmul(
-                        summed[:, j, :],
-                        lhsT=term[:, j * P : (j + 1) * P],
-                        rhs=ident32[:],
-                        start=(i == 0 and j == 0),
-                        stop=(i == len(parts) - 1 and j == blocks - 1),
-                        is_transpose=True,
-                    )
-            turned = keep.tile([P, blocks, P], BF16, name=f"turned_{name}")
-            nc.scalar.copy(turned[:], summed[:])
-            return turned
+        a_picked = keep.tile([P, 3 * V], U32, name="a_picked", align_bytes=64)
+        gather(a_picked[:], A, 0, 3)
+        a_part = keep.tile([P, 2 * V], F32, name="a_part", tag="part", align_bytes=64)
+        add(a_part[:], a_picked[:, :V].bitcast(BF16), a_picked[:, V : 2 * V].bitcast(BF16))
+        add(three[:, 0, :], a_part[:], a_picked[:, 2 * V :].bitcast(BF16))
 
-        turned = [
-            sum_turned("c", [part[C][:], c_wide[:, : 2 * V], c_wide[:, 2 * V :]]),
-            sum_turned("d", [part[Dd][:], d_wide[0][:], d_wide[1][:]]),
-        ]
-        grouped0 = keep.tile([P, PACK * V], BF16, name="grouped0", align_bytes=64)
+        w_grouped = keep.tile([P, PASSES, N, 2, 2], BF16, name="w_grouped", align_bytes=64)
+        c_turned = w_rows[:, :V].bitcast(BF16)
+        for c in range(PASSES):
+            nc.scalar.copy(w_grouped[:, c], w_raw[:, c].rearrange("p (u e) n -> p n u e", e=2)[:, :, :, ::-1])
+        nc.scalar.copy(c_turned, c_sum[:].rearrange("p j m -> p (j m)"))
         backs = [psum.tile([P, 2, 2 * HALF], BF16, name=f"back{h}", tag=f"last{h}") for h in range(2)]
-        for u in range(2):
+        for h in range(2):
+            for j in range(2):
+                at = (2 * h + j) * P
+                nc.tensor.transpose(backs[h][:, 0, j * P : (j + 1) * P], c_turned[:, at : at + P], ident16[:])
+
+        d_two = keep.tile([P, 2 * V], U32, name="d_two", tag="d_terms", align_bytes=64)
+        gather(d_two[:], Dd, 0, 2)
+        d_early = w_rows[:, V:]
+        nc.scalar.copy(d_early, d_two[:].bitcast(BF16))
+        d_sum = [psum.tile([P, blocks // 2, P], F32, name=f"d_sum{h}") for h in range(2)]
+        for g in range(2):
             for h in range(2):
-                for j in range(2):
-                    nc.tensor.transpose(backs[h][:, u, j * P : (j + 1) * P], turned[u][:, 2 * h + j, :], ident16[:])
+                add_turned(d_sum[h][:], d_early[:, g * 2 * V + h * V : g * 2 * V + (h + 1) * V], g == 0, False)
+
+        b_two = keep.tile([P, 2 * V], U32, name="b_two", align_bytes=64)
+        gather(b_two[:], B, 0, 2)
+        b_part = keep.tile([P, 2 * V], F32, name="b_part", tag="part", align_bytes=64)
+        add(b_part[:], b_two[:, :V].bitcast(BF16), b_two[:, V:].bitcast(BF16))
+
+        held = rows[B][:, WINDOW[2] :]
+        gather(held[:, V : 3 * V].bitcast(U32), Dd, 2, 2)
+        d_picked = held[:, V : 3 * V].bitcast(BF16).rearrange("p (g h m) -> p h g m", g=2, h=2)
+        d_late = keep.tile([P, 2, 2, V], F32, name="d_late", tag="d_terms", align_bytes=64)
+        for h in range(2):
+            nc.scalar.copy(d_late[:, h], d_picked[:, h])
+            for g in range(2):
+                add_turned(d_sum[h][:], d_late[:, h, g], False, g == 1)
+
+        b_third = keep.tile([P, V], U32, name="b_third", align_bytes=64)
+        gather(b_third[:], B, 2, 1)
+        add(three[:, 1, :], b_part[:], b_third[:].bitcast(BF16))
+        for u, q in enumerate((A, B)):
+            gather(held[:, 3 * u * V : (3 * u + 1) * V].bitcast(U32), q, 3, 1)
+        fourth = held.bitcast(BF16).rearrange("p (u v e) -> p v u e", u=4, e=2)[:, :, ::3]
+
+        grouped0 = keep.tile([P, PACK * V], BF16, name="grouped0", align_bytes=64)
+        d_turned = [keep.tile([P, blocks // 2, P], BF16, name=f"d_turned{h}") for h in range(2)]
+        for h in range(2):
+            nc.scalar.copy(d_turned[h][:], d_sum[h][:])
+            for j in range(2):
+                nc.tensor.transpose(backs[h][:, 1, j * P : (j + 1) * P], d_turned[h][:, j, :], ident16[:])
         for h in range(2):
             nc.scalar.copy(
                 grouped0[:, h * PACK * HALF : (h + 1) * PACK * HALF].bitcast(F32).rearrange("p (v u) -> p v u", u=2),
@@ -165,13 +181,13 @@ def tile_picked_hash_lin_silu_sub_l_kernel(tc, xT, w, b, offs, out):
             nc.vector.tensor_tensor(
                 grouped1[:].rearrange("p (v u e) -> p v u e", u=2, e=2)[:, ids],
                 three[:].rearrange("p u (v e) -> p v u e", e=2)[:, ids],
-                fourth.rearrange("p (u v e) -> p v u e", u=2, e=2)[:, ids],
+                fourth[:, ids],
                 ADD,
             )
         nc.vector.quantize_mx(
             out=w_codes[:].bitcast(FP8X4),
             scales=w_scales[:],
-            in_=w_grouped[:].rearrange("p c n j -> p (c n j)"),
+            in_=w_grouped[:].rearrange("p c n u e -> p (c n u e)"),
         )
         for c, grouped in ((1, grouped1), (0, grouped0)):
             for h in range(2):

@@ -23,7 +23,7 @@ HALF = V // 2
 COLS = V // 16
 VEC_COLS = 416
 WINDOW = {1: T, 2: 704, 3: 2 * T}
-LAST = WINDOW[2] + 4 * V
+LAST = 2 * T
 
 
 def tile_picked_hash_lin_silu_sub_l_kernel(tc, xT, w, b, offs, out):
@@ -93,7 +93,7 @@ def tile_picked_hash_lin_silu_sub_l_kernel(tc, xT, w, b, offs, out):
                 )
 
         blocks = 2 * V // P
-        three = keep.tile([P, 2, 2 * V], F32, name="three", align_bytes=64)
+        parts = keep.tile([P, 2, 2, 2 * V], F32, name="parts", align_bytes=64)
 
         c_sum = psum.tile([P, blocks, P], F32, name="c_sum")
         for g in range(2):
@@ -103,11 +103,17 @@ def tile_picked_hash_lin_silu_sub_l_kernel(tc, xT, w, b, offs, out):
             add(part[:], two[:, :V].bitcast(BF16), two[:, V:].bitcast(BF16))
             add_turned(c_sum[:], part[:], g == 0, g == 1)
 
-        a_picked = keep.tile([P, 3 * V], U32, name="a_picked", align_bytes=64)
-        gather(a_picked[:], A, 0, 3)
-        a_part = keep.tile([P, 2 * V], F32, name="a_part", tag="part", align_bytes=64)
-        add(a_part[:], a_picked[:, :V].bitcast(BF16), a_picked[:, V : 2 * V].bitcast(BF16))
-        add(three[:, 0, :], a_part[:], a_picked[:, 2 * V :].bitcast(BF16))
+        def sum_two(q, g):
+            two = keep.tile([P, 2 * V], U32, name=f"two{q[1]}{g}", align_bytes=64)
+            gather(two[:], q, 2 * g, 2)
+            add(parts[:, q[1], g, :], two[:, :V].bitcast(BF16), two[:, V:].bitcast(BF16))
+
+        sum_two(A, 0)
+        sum_two(A, 1)
+        d_three = keep.tile([P, 3 * V], U32, name="d_three", tag="d_terms", align_bytes=64)
+        gather(d_three[:], Dd, 0, 3)
+        d_part = keep.tile([P, 2 * V], F32, name="d_part", align_bytes=64)
+        add(d_part[:], d_three[:, :V].bitcast(BF16), d_three[:, V : 2 * V].bitcast(BF16))
 
         w_grouped = keep.tile([P, PASSES, N, 2, 2], BF16, name="w_grouped", align_bytes=64)
         c_turned = w_rows[:, :V].bitcast(BF16)
@@ -120,35 +126,25 @@ def tile_picked_hash_lin_silu_sub_l_kernel(tc, xT, w, b, offs, out):
                 at = (2 * h + j) * P
                 nc.tensor.transpose(backs[h][:, 0, j * P : (j + 1) * P], c_turned[:, at : at + P], ident16[:])
 
-        d_two = keep.tile([P, 2 * V], U32, name="d_two", tag="d_terms", align_bytes=64)
-        gather(d_two[:], Dd, 0, 2)
-        d_early = w_rows[:, V:]
-        nc.scalar.copy(d_early, d_two[:].bitcast(BF16))
+        d_early = w_rows[:, V : 3 * V]
+        nc.scalar.copy(d_early, d_three[:, 2 * V :].bitcast(BF16))
         d_sum = [psum.tile([P, blocks // 2, P], F32, name=f"d_sum{h}") for h in range(2)]
-        for g in range(2):
+        for g, term in enumerate((d_early, d_part[:])):
             for h in range(2):
-                add_turned(d_sum[h][:], d_early[:, g * 2 * V + h * V : g * 2 * V + (h + 1) * V], g == 0, False)
+                add_turned(d_sum[h][:], term[:, h * V : (h + 1) * V], g == 0, False)
 
-        b_two = keep.tile([P, 2 * V], U32, name="b_two", align_bytes=64)
-        gather(b_two[:], B, 0, 2)
-        b_part = keep.tile([P, 2 * V], F32, name="b_part", tag="part", align_bytes=64)
-        add(b_part[:], b_two[:, :V].bitcast(BF16), b_two[:, V:].bitcast(BF16))
+        sum_two(B, 0)
 
-        held = rows[B][:, WINDOW[2] :]
-        gather(held[:, V : 3 * V].bitcast(U32), Dd, 2, 2)
-        d_picked = held[:, V : 3 * V].bitcast(BF16).rearrange("p (g h m) -> p h g m", g=2, h=2)
-        d_late = keep.tile([P, 2, 2, V], F32, name="d_late", tag="d_terms", align_bytes=64)
+        held = rows[B][:, WINDOW[2] : WINDOW[2] + V]
+        gather(held.bitcast(U32), Dd, 3, 1)
+        d_late = keep.tile([P, 2 * V], F32, name="d_late", tag="d_terms", align_bytes=64)
         for h in range(2):
-            nc.scalar.copy(d_late[:, h], d_picked[:, h])
-            for g in range(2):
-                add_turned(d_sum[h][:], d_late[:, h, g], False, g == 1)
+            cols = slice(h * V, (h + 1) * V)
+            nc.scalar.copy(d_late[:, cols], held.bitcast(BF16)[:, cols])
+            add_turned(d_sum[h][:], d_late[:, cols], False, True)
 
-        b_third = keep.tile([P, V], U32, name="b_third", align_bytes=64)
-        gather(b_third[:], B, 2, 1)
-        add(three[:, 1, :], b_part[:], b_third[:].bitcast(BF16))
-        for u, q in enumerate((A, B)):
-            gather(held[:, 3 * u * V : (3 * u + 1) * V].bitcast(U32), q, 3, 1)
-        fourth = held.bitcast(BF16).rearrange("p (u v e) -> p v u e", u=4, e=2)[:, :, ::3]
+        last = keep.tile([P, 2 * V], U32, name="last", align_bytes=64)
+        gather(last[:], B, 2, 2)
 
         grouped0 = keep.tile([P, PACK * V], BF16, name="grouped0", align_bytes=64)
         d_turned = [keep.tile([P, blocks // 2, P], BF16, name=f"d_turned{h}") for h in range(2)]
@@ -176,19 +172,21 @@ def tile_picked_hash_lin_silu_sub_l_kernel(tc, xT, w, b, offs, out):
             )
 
         grouped1 = keep.tile([P, PACK * V], BF16, name="grouped1", align_bytes=64)
-        for h in range(2):
-            ids = slice(h * HALF, (h + 1) * HALF)
-            nc.vector.tensor_tensor(
-                grouped1[:].rearrange("p (v u e) -> p v u e", u=2, e=2)[:, ids],
-                three[:].rearrange("p u (v e) -> p v u e", e=2)[:, ids],
-                fourth[:, ids],
-                ADD,
-            )
+        nc.vector.tensor_tensor(parts[:, 1, 1, :], last[:, :V].bitcast(BF16), last[:, V:].bitcast(BF16), ADD)
         nc.vector.quantize_mx(
             out=w_codes[:].bitcast(FP8X4),
             scales=w_scales[:],
             in_=w_grouped[:].rearrange("p c n u e -> p (c n u e)"),
         )
+        both = parts[:].rearrange("p u g (v e) -> p g v u e", e=2)
+        for h in range(2):
+            ids = slice(h * HALF, (h + 1) * HALF)
+            nc.vector.tensor_tensor(
+                grouped1[:].rearrange("p (v u e) -> p v u e", u=2, e=2)[:, ids],
+                both[:, 0, ids],
+                both[:, 1, ids],
+                ADD,
+            )
         for c, grouped in ((1, grouped1), (0, grouped0)):
             for h in range(2):
                 quantize_x(c, grouped, h)

@@ -13,6 +13,7 @@ U16 = mybir.dt.uint16
 U8 = mybir.dt.uint8
 FP8X4 = mybir.dt.float8_e4m3fn_x4
 ADD = mybir.AluOpType.add
+COPY = mybir.ActivationFunctionType.Copy
 SILU = mybir.ActivationFunctionType.Silu
 
 P = 128
@@ -21,9 +22,9 @@ PASSES = K // (P * PACK)
 PAIRS = 2 * PASSES
 HALF = V // 2
 COLS = V // 16
-VEC_COLS = 416
-WINDOW = {1: T, 2: 704, 3: 2 * T}
-LAST = 2 * T
+PIECES = ((0, 256), (256, 448), (448, T))
+HALVES = ((0, T // 2), (T // 2, T))
+WINDOW = 704
 
 
 def tile_picked_hash_lin_silu_sub_l_kernel(tc, xT, w, b, offs, out):
@@ -35,22 +36,24 @@ def tile_picked_hash_lin_silu_sub_l_kernel(tc, xT, w, b, offs, out):
         offsets = keep.tile([P, D * COLS], U16, name="offsets")
         x_rows = xT.rearrange("(c p u e) t -> c u p e t", c=PASSES, p=P, u=2, e=2)
         A, C, Dd, B = (1, 0), (0, 0), (0, 1), (1, 1)
-        order = [C, A, Dd, B]
-        rows = {
-            q: keep.tile([P, LAST if q == B else 2 * T], F32, name=f"rows{i}", align_bytes=64)
-            for i, q in enumerate(order)
-        }
-        raw = {q: rows[q][:, : 2 * T].rearrange("p (e t) -> p e t", e=2) for q in order}
-        w_rows = keep.tile([P, PASSES * PACK * N + V], F32, name="w_rows", align_bytes=64)
-        w_raw = w_rows[:, : PASSES * PACK * N].rearrange("p (c j n) -> p c j n", c=PASSES, j=PACK)
+        order = [C, Dd, A, B]
+        rows = {q: keep.tile([P, 2 * T], F32, name=f"rows{i}", align_bytes=64)[:] for i, q in enumerate(order[:3])}
+        raw = {q: rows[q].rearrange("p (e t) -> p e t", e=2) for q in order[:3]}
+        b_even = keep.tile([P, WINDOW], F32, name="b_even", align_bytes=64)
+        b_odd = keep.tile([P, T], F32, name="b_odd", tag="b_odd", align_bytes=64)
+        rows.update({B: b_even[:]})
+        w_raw = keep.tile([P, PASSES, PACK, N], F32, name="w_raw")
         bias = keep.tile([P, 1], F32, name="bias")
 
-        for lo in (0, T // 2):
-            nc.sync.dma_start(raw[C][:, :, lo : lo + T // 2], x_rows[C][:, :, lo : lo + T // 2])
+        for lo, hi in PIECES:
+            nc.sync.dma_start(raw[C][:, :, lo:hi], x_rows[C][:, :, lo:hi])
         nc.sync.dma_start(offsets[:], offs)
-        for q in order[1:]:
-            nc.sync.dma_start(raw[q], x_rows[q])
-        nc.sync.dma_start(w_raw, w.rearrange("(c p j) n -> p c j n", c=PASSES, p=P, j=PACK))
+        for lo, hi in HALVES:
+            nc.sync.dma_start(raw[Dd][:, :, lo:hi], x_rows[Dd][:, :, lo:hi])
+        nc.sync.dma_start(raw[A], x_rows[A])
+        nc.sync.dma_start(b_even[:, :T], x_rows[B][:, 0])
+        nc.sync.dma_start(b_odd[:], x_rows[B][:, 1])
+        nc.sync.dma_start(w_raw[:], w.rearrange("(c p j) n -> p c j n", c=PASSES, p=P, j=PACK))
         nc.sync.dma_start(bias[:], b)
 
         warm = keep.tile([P, 1], F32, name="warm")
@@ -62,96 +65,95 @@ def tile_picked_hash_lin_silu_sub_l_kernel(tc, xT, w, b, offs, out):
         ident16 = keep.tile([P, P], BF16, name="ident16")
         make_identity(nc, ident32[:])
         make_identity(nc, ident16[:])
+        nc.vector.memset(b_even[:, T:], 0.0)
+
+        def halves(q):
+            return rows[q].bitcast(BF16).rearrange("p (r t h) -> p r t h", r=2, h=2)
 
         def pack(copy, q, lo, hi):
-            halves = rows[q][:, : 2 * T].bitcast(BF16).rearrange("p (t h) -> p t h", h=2)
-            copy(halves[:, lo:hi, 0], halves[:, T + lo : T + hi, 1])
+            copy(halves(q)[:, 0, lo:hi, 0], halves(q)[:, 1, lo:hi, 1])
 
-        pack(nc.vector.tensor_copy, C, 0, T // 2)
-        pack(nc.vector.tensor_copy, C, T // 2, VEC_COLS)
-        pack(nc.scalar.copy, C, VEC_COLS, T)
-        for q in order[1:]:
-            pack(nc.scalar.copy, q, 0, T)
+        planes = [keep.tile([P, T], BF16, name=f"plane{r}", align_bytes=64) for r in range(2)]
+        for lo, hi in PIECES:
+            pack(nc.vector.tensor_copy, C, lo, hi)
+        for lo, hi in HALVES:
+            for r in (1, 0):
+                nc.scalar.copy(planes[r][:, lo:hi], halves(C)[:, r, lo:hi, 1])
+        for lo, hi in HALVES:
+            pack(nc.scalar.copy, Dd, lo, hi)
+        pack(nc.scalar.copy, A, 0, T)
+        nc.scalar.copy(
+            b_even[:, :T].bitcast(BF16).rearrange("p (t h) -> p t h", h=2)[:, :, 0],
+            b_odd[:].bitcast(BF16).rearrange("p (t h) -> p t h", h=2)[:, :, 1],
+        )
 
-        def gather(dst, q, d, pieces):
-            window = rows[q][:, : WINDOW[pieces]].bitcast(U32)
-            nc.vector.tensor_copy(dst, window.indirect(offsets[:, d * COLS : (d + pieces) * COLS]))
+        def gather(q, g):
+            two = keep.tile([P, 2 * V], U32, name=f"two{q[0]}{q[1]}{g}", align_bytes=64)
+            window = rows[q][:, :WINDOW].bitcast(U32)
+            nc.vector.tensor_copy(two[:], window.indirect(offsets[:, 2 * g * COLS : 2 * (g + 1) * COLS]))
+            return two[:, :V].bitcast(BF16), two[:, V:].bitcast(BF16)
 
-        def add(dst, first, second):
-            nc.gpsimd.tensor_tensor(dst, first, second, ADD)
-
-        def add_turned(bank, term, first, last):
-            count = bank.shape[1]
-            for j in range(count):
+        def add_turned(bank, sources, first, last):
+            for j, source in enumerate(sources):
                 nc.tensor.matmul(
                     bank[:, j, :],
-                    lhsT=term[:, j * P : (j + 1) * P],
+                    lhsT=source,
                     rhs=ident32[:],
                     start=(first and j == 0),
-                    stop=(last and j == count - 1),
+                    stop=(last and j == len(sources) - 1),
                     is_transpose=True,
                 )
 
         blocks = 2 * V // P
-        parts = keep.tile([P, 2, 2, 2 * V], F32, name="parts", align_bytes=64)
-
         c_sum = psum.tile([P, blocks, P], F32, name="c_sum")
+        d_sum = psum.tile([P, blocks, P], F32, name="d_sum")
+        c_part = keep.tile([P, 2 * V], F32, name="c_part", align_bytes=64)
+        nc.gpsimd.tensor_tensor(c_part[:], *gather(C, 0), ADD)
+        by_half = c_part[:].rearrange("p (h v e) -> p e h v", h=2, e=2)
+        add_turned(c_sum[:], [by_half[:, e, h] for e in range(2) for h in range(2)], True, False)
         for g in range(2):
-            two = keep.tile([P, 2 * V], U32, name=f"c_two{g}", align_bytes=64)
-            gather(two[:], C, 2 * g, 2)
-            part = keep.tile([P, 2 * V], F32, name=f"c_part{g}", align_bytes=64)
-            add(part[:], two[:, :V].bitcast(BF16), two[:, V:].bitcast(BF16))
-            add_turned(c_sum[:], part[:], g == 0, g == 1)
+            part = keep.tile([P, 2 * V], F32, name=f"d_part{g}", align_bytes=64)
+            nc.gpsimd.tensor_tensor(part[:], *gather(Dd, g), ADD)
+            add_turned(d_sum[:], [part[:, j * P : (j + 1) * P] for j in range(blocks)], g == 0, g == 1)
+        parts = keep.tile([P, 2, 2, 2 * V], F32, name="parts", align_bytes=64)
+        for g in range(2):
+            nc.gpsimd.tensor_tensor(parts[:, 0, g, :], *gather(A, g), ADD)
+        b_terms = [gather(B, g) for g in range(2)]
 
-        def sum_two(q, g):
-            two = keep.tile([P, 2 * V], U32, name=f"two{q[1]}{g}", align_bytes=64)
-            gather(two[:], q, 2 * g, 2)
-            add(parts[:, q[1], g, :], two[:, :V].bitcast(BF16), two[:, V:].bitcast(BF16))
-
-        sum_two(A, 0)
-        sum_two(A, 1)
-        d_three = keep.tile([P, 3 * V], U32, name="d_three", tag="d_terms", align_bytes=64)
-        gather(d_three[:], Dd, 0, 3)
-        d_part = keep.tile([P, 2 * V], F32, name="d_part", align_bytes=64)
-        add(d_part[:], d_three[:, :V].bitcast(BF16), d_three[:, V : 2 * V].bitcast(BF16))
+        c_picked = keep.tile([P, 2, 2 * V], BF16, name="c_picked", tag="b_odd", align_bytes=64)
+        c_wide = keep.tile([P, 2, 2 * V], F32, name="c_wide", align_bytes=64)
+        for e in range(2):
+            for g in range(2):
+                entries = offsets[:, (2 + g) * COLS : (3 + g) * COLS]
+                nc.scalar.activation(c_picked[:, e, g * V : (g + 1) * V], planes[1 - e][:].indirect(entries), COPY)
+            nc.scalar.copy(c_wide[:, e, :], c_picked[:, e, :])
+            for g in range(2):
+                for h in range(2):
+                    nc.tensor.matmul(
+                        c_sum[:, 2 * e + h, :],
+                        lhsT=c_wide[:, e, g * V + h * HALF : g * V + (h + 1) * HALF],
+                        rhs=ident32[:],
+                        start=False,
+                        stop=(e == 1 and g == 1 and h == 1),
+                        is_transpose=True,
+                    )
 
         w_grouped = keep.tile([P, PASSES, N, 2, 2], BF16, name="w_grouped", align_bytes=64)
-        c_turned = w_rows[:, :V].bitcast(BF16)
         for c in range(PASSES):
             nc.scalar.copy(w_grouped[:, c], w_raw[:, c].rearrange("p (u e) n -> p n u e", e=2)[:, :, :, ::-1])
-        nc.scalar.copy(c_turned, c_sum[:].rearrange("p j m -> p (j m)"))
+
         backs = [psum.tile([P, 2, 2 * HALF], BF16, name=f"back{h}", tag=f"last{h}") for h in range(2)]
-        for h in range(2):
-            for j in range(2):
-                at = (2 * h + j) * P
-                nc.tensor.transpose(backs[h][:, 0, j * P : (j + 1) * P], c_turned[:, at : at + P], ident16[:])
-
-        d_early = w_rows[:, V : 3 * V]
-        nc.scalar.copy(d_early, d_three[:, 2 * V :].bitcast(BF16))
-        d_sum = [psum.tile([P, blocks // 2, P], F32, name=f"d_sum{h}") for h in range(2)]
-        for g, term in enumerate((d_early, d_part[:])):
-            for h in range(2):
-                add_turned(d_sum[h][:], term[:, h * V : (h + 1) * V], g == 0, False)
-
-        sum_two(B, 0)
-
-        held = rows[B][:, WINDOW[2] : WINDOW[2] + V]
-        gather(held.bitcast(U32), Dd, 3, 1)
-        d_late = keep.tile([P, 2 * V], F32, name="d_late", tag="d_terms", align_bytes=64)
-        for h in range(2):
-            cols = slice(h * V, (h + 1) * V)
-            nc.scalar.copy(d_late[:, cols], held.bitcast(BF16)[:, cols])
-            add_turned(d_sum[h][:], d_late[:, cols], False, True)
-
-        last = keep.tile([P, 2 * V], U32, name="last", align_bytes=64)
-        gather(last[:], B, 2, 2)
-
+        d_turned = keep.tile([P, blocks, P], BF16, name="d_turned")
+        nc.scalar.copy(d_turned[:], d_sum[:])
+        for j in range(blocks):
+            nc.tensor.transpose(backs[j // 2][:, 1, (j % 2) * P : (j % 2 + 1) * P], d_turned[:, j, :], ident16[:])
+        c_turned = keep.tile([P, 2, 2 * P], BF16, name="c_turned")
+        nc.scalar.copy(
+            c_turned[:].rearrange("v h (p e) -> v h p e", e=2), c_sum[:].rearrange("v (e h) p -> v h p e", e=2)
+        )
         grouped0 = keep.tile([P, PACK * V], BF16, name="grouped0", align_bytes=64)
-        d_turned = [keep.tile([P, blocks // 2, P], BF16, name=f"d_turned{h}") for h in range(2)]
         for h in range(2):
-            nc.scalar.copy(d_turned[h][:], d_sum[h][:])
-            for j in range(2):
-                nc.tensor.transpose(backs[h][:, 1, j * P : (j + 1) * P], d_turned[h][:, j, :], ident16[:])
+            nc.tensor.transpose(backs[h][:].bitcast(F32)[:, 0, :], c_turned[:, h, :].bitcast(F32), ident32[:])
         for h in range(2):
             nc.scalar.copy(
                 grouped0[:, h * PACK * HALF : (h + 1) * PACK * HALF].bitcast(F32).rearrange("p (v u) -> p v u", u=2),
@@ -172,7 +174,8 @@ def tile_picked_hash_lin_silu_sub_l_kernel(tc, xT, w, b, offs, out):
             )
 
         grouped1 = keep.tile([P, PACK * V], BF16, name="grouped1", align_bytes=64)
-        nc.vector.tensor_tensor(parts[:, 1, 1, :], last[:, :V].bitcast(BF16), last[:, V:].bitcast(BF16), ADD)
+        for g in range(2):
+            nc.vector.tensor_tensor(parts[:, 1, g, :], *b_terms[g], ADD)
         nc.vector.quantize_mx(
             out=w_codes[:].bitcast(FP8X4),
             scales=w_scales[:],

@@ -36,12 +36,11 @@ def tile_picked_hash_lin_silu_sub_l_kernel(tc, xT, w, b, offs, out):
         offsets = keep.tile([P, D * COLS], U16, name="offsets")
         x_rows = xT.rearrange("(c p u e) t -> c u p e t", c=PASSES, p=P, u=2, e=2)
         A, C, Dd, B = (1, 0), (0, 0), (0, 1), (1, 1)
-        order = [C, Dd, A, B]
-        rows = {q: keep.tile([P, 2 * T], F32, name=f"rows{i}", align_bytes=64)[:] for i, q in enumerate(order[:3])}
-        raw = {q: rows[q].rearrange("p (e t) -> p e t", e=2) for q in order[:3]}
-        b_even = keep.tile([P, WINDOW], F32, name="b_even", align_bytes=64)
-        b_odd = keep.tile([P, T], F32, name="b_odd", tag="b_odd", align_bytes=64)
-        rows.update({B: b_even[:]})
+        rows = {q: keep.tile([P, 2 * T], F32, name=f"rows{i}", align_bytes=64)[:] for i, q in enumerate((C, Dd, B))}
+        raw = {q: rows[q].rearrange("p (e t) -> p e t", e=2) for q in (C, Dd, B)}
+        a_even = keep.tile([P, WINDOW], F32, name="a_even", align_bytes=64)
+        a_odd = keep.tile([P, T], F32, name="a_odd", tag="a_odd", align_bytes=64)
+        rows.update({A: a_even[:]})
         w_raw = keep.tile([P, PASSES, PACK, N], F32, name="w_raw")
         bias = keep.tile([P, 1], F32, name="bias")
 
@@ -50,9 +49,9 @@ def tile_picked_hash_lin_silu_sub_l_kernel(tc, xT, w, b, offs, out):
         nc.sync.dma_start(offsets[:], offs)
         for lo, hi in HALVES:
             nc.sync.dma_start(raw[Dd][:, :, lo:hi], x_rows[Dd][:, :, lo:hi])
-        nc.sync.dma_start(raw[A], x_rows[A])
-        nc.sync.dma_start(b_even[:, :T], x_rows[B][:, 0])
-        nc.sync.dma_start(b_odd[:], x_rows[B][:, 1])
+        nc.sync.dma_start(a_even[:, :T], x_rows[A][:, 0])
+        nc.sync.dma_start(a_odd[:], x_rows[A][:, 1])
+        nc.sync.dma_start(raw[B], x_rows[B])
         nc.sync.dma_start(w_raw[:], w.rearrange("(c p j) n -> p c j n", c=PASSES, p=P, j=PACK))
         nc.sync.dma_start(bias[:], b)
 
@@ -65,7 +64,7 @@ def tile_picked_hash_lin_silu_sub_l_kernel(tc, xT, w, b, offs, out):
         ident16 = keep.tile([P, P], BF16, name="ident16")
         make_identity(nc, ident32[:])
         make_identity(nc, ident16[:])
-        nc.vector.memset(b_even[:, T:], 0.0)
+        nc.vector.memset(a_even[:, T:], 0.0)
 
         def halves(q):
             return rows[q].bitcast(BF16).rearrange("p (r t h) -> p r t h", r=2, h=2)
@@ -73,7 +72,9 @@ def tile_picked_hash_lin_silu_sub_l_kernel(tc, xT, w, b, offs, out):
         def pack(copy, q, lo, hi):
             copy(halves(q)[:, 0, lo:hi, 0], halves(q)[:, 1, lo:hi, 1])
 
-        planes = [keep.tile([P, T], BF16, name=f"plane{r}", align_bytes=64) for r in range(2)]
+        planes = [keep.tile([P, 2 * T], BF16, name=f"plane{r}", align_bytes=64) for r in range(2)]
+        for r in range(2):
+            nc.vector.memset(planes[r][:, T:], 0.0)
         for lo, hi in PIECES:
             pack(nc.vector.tensor_copy, C, lo, hi)
         for lo, hi in HALVES:
@@ -81,14 +82,14 @@ def tile_picked_hash_lin_silu_sub_l_kernel(tc, xT, w, b, offs, out):
                 nc.scalar.copy(planes[r][:, lo:hi], halves(C)[:, r, lo:hi, 1])
         for lo, hi in HALVES:
             pack(nc.scalar.copy, Dd, lo, hi)
-        pack(nc.scalar.copy, A, 0, T)
         nc.scalar.copy(
-            b_even[:, :T].bitcast(BF16).rearrange("p (t h) -> p t h", h=2)[:, :, 0],
-            b_odd[:].bitcast(BF16).rearrange("p (t h) -> p t h", h=2)[:, :, 1],
+            a_even[:, :T].bitcast(BF16).rearrange("p (t h) -> p t h", h=2)[:, :, 0],
+            a_odd[:].bitcast(BF16).rearrange("p (t h) -> p t h", h=2)[:, :, 1],
         )
+        pack(nc.scalar.copy, B, 0, T)
 
         def gather(q, g):
-            two = keep.tile([P, 2 * V], U32, name=f"two{q[0]}{q[1]}{g}", align_bytes=64)
+            two = keep.tile([P, 2 * V], U32, name=f"two{q[0]}{q[1]}{g}", tag=f"two{q[0]}{q[1]}{g}", align_bytes=64)
             window = rows[q][:, :WINDOW].bitcast(U32)
             nc.vector.tensor_copy(two[:], window.indirect(offsets[:, 2 * g * COLS : 2 * (g + 1) * COLS]))
             return two[:, :V].bitcast(BF16), two[:, V:].bitcast(BF16)
@@ -115,42 +116,43 @@ def tile_picked_hash_lin_silu_sub_l_kernel(tc, xT, w, b, offs, out):
             part = keep.tile([P, 2 * V], F32, name=f"d_part{g}", align_bytes=64)
             nc.gpsimd.tensor_tensor(part[:], *gather(Dd, g), ADD)
             add_turned(d_sum[:], [part[:, j * P : (j + 1) * P] for j in range(blocks)], g == 0, g == 1)
-        parts = keep.tile([P, 2, 2, 2 * V], F32, name="parts", align_bytes=64)
+        parts = keep.tile([P, 2, 2, 2 * V], F32, name="parts", tag="parts", align_bytes=64)
         for g in range(2):
             nc.gpsimd.tensor_tensor(parts[:, 0, g, :], *gather(A, g), ADD)
         b_terms = [gather(B, g) for g in range(2)]
 
-        c_picked = keep.tile([P, 2, 2 * V], BF16, name="c_picked", tag="b_odd", align_bytes=64)
-        c_wide = keep.tile([P, 2, 2 * V], F32, name="c_wide", align_bytes=64)
+        c_picked = keep.tile([P, 2, 2 * V], BF16, name="c_picked", tag="a_odd", align_bytes=64)
         for e in range(2):
-            for g in range(2):
-                entries = offsets[:, (2 + g) * COLS : (3 + g) * COLS]
-                nc.scalar.activation(c_picked[:, e, g * V : (g + 1) * V], planes[1 - e][:].indirect(entries), COPY)
-            nc.scalar.copy(c_wide[:, e, :], c_picked[:, e, :])
+            nc.scalar.activation(c_picked[:, e, :], planes[1 - e][:].indirect(offsets[:, 2 * COLS :]), COPY)
+            c_wide = keep.tile([P, 2 * V], F32, name=f"c_wide{e}", tag=f"c_wide{e}", align_bytes=64)
+            nc.scalar.copy(c_wide[:], c_picked[:, e, :])
             for g in range(2):
                 for h in range(2):
                     nc.tensor.matmul(
                         c_sum[:, 2 * e + h, :],
-                        lhsT=c_wide[:, e, g * V + h * HALF : g * V + (h + 1) * HALF],
+                        lhsT=c_wide[:, g * V + h * HALF : g * V + (h + 1) * HALF],
                         rhs=ident32[:],
                         start=False,
                         stop=(e == 1 and g == 1 and h == 1),
                         is_transpose=True,
                     )
 
-        w_grouped = keep.tile([P, PASSES, N, 2, 2], BF16, name="w_grouped", align_bytes=64)
-        for c in range(PASSES):
-            nc.scalar.copy(w_grouped[:, c], w_raw[:, c].rearrange("p (u e) n -> p n u e", e=2)[:, :, :, ::-1])
+        def cast_w(c, tag):
+            grouped = keep.tile([P, N, 2, 2], BF16, name=f"w_grouped{c}", tag=tag, align_bytes=64)
+            nc.scalar.copy(grouped[:], w_raw[:, c].rearrange("p (u e) n -> p n u e", e=2)[:, :, :, ::-1])
+            return grouped
 
         backs = [psum.tile([P, 2, 2 * HALF], BF16, name=f"back{h}", tag=f"last{h}") for h in range(2)]
         d_turned = keep.tile([P, blocks, P], BF16, name="d_turned")
         nc.scalar.copy(d_turned[:], d_sum[:])
         for j in range(blocks):
             nc.tensor.transpose(backs[j // 2][:, 1, (j % 2) * P : (j % 2 + 1) * P], d_turned[:, j, :], ident16[:])
+        w_grouped = {1: cast_w(1, "c_wide0")}
         c_turned = keep.tile([P, 2, 2 * P], BF16, name="c_turned")
         nc.scalar.copy(
             c_turned[:].rearrange("v h (p e) -> v h p e", e=2), c_sum[:].rearrange("v (e h) p -> v h p e", e=2)
         )
+        w_grouped.update({0: cast_w(0, "c_wide1")})
         grouped0 = keep.tile([P, PACK * V], BF16, name="grouped0", align_bytes=64)
         for h in range(2):
             nc.tensor.transpose(backs[h][:].bitcast(F32)[:, 0, :], c_turned[:, h, :].bitcast(F32), ident32[:])
@@ -160,27 +162,29 @@ def tile_picked_hash_lin_silu_sub_l_kernel(tc, xT, w, b, offs, out):
                 backs[h][:].bitcast(F32).rearrange("p u v -> p v u"),
             )
 
-        w_codes = keep.tile([P, PASSES * N], U32, name="w_codes", align_bytes=64)
-        x_codes = keep.tile([P, PASSES * V], U32, name="x_codes", align_bytes=64)
         w_scales = keep.tile([P, PASSES * N], U8, name="w_scales", align_bytes=64)
         x_scales = keep.tile([P, PASSES * V], U8, name="x_scales", align_bytes=64)
 
-        def quantize_x(c, grouped, h):
-            first = c * V + h * HALF
+        def quantize_w(c, tag):
+            codes = keep.tile([P, N], U32, name=f"w_codes{c}", tag=tag, align_bytes=64)
             nc.vector.quantize_mx(
-                out=x_codes[:, first : first + HALF].bitcast(FP8X4),
-                scales=x_scales[:, first : first + HALF],
+                out=codes[:].bitcast(FP8X4),
+                scales=w_scales[:, c * N : (c + 1) * N],
+                in_=w_grouped[c][:].rearrange("p n u e -> p (n u e)"),
+            )
+            return codes
+
+        def quantize_x(c, codes, grouped, h):
+            nc.vector.quantize_mx(
+                out=codes[:, h * HALF : (h + 1) * HALF].bitcast(FP8X4),
+                scales=x_scales[:, c * V + h * HALF : c * V + (h + 1) * HALF],
                 in_=grouped[:, h * PACK * HALF : (h + 1) * PACK * HALF],
             )
 
         grouped1 = keep.tile([P, PACK * V], BF16, name="grouped1", align_bytes=64)
         for g in range(2):
             nc.vector.tensor_tensor(parts[:, 1, g, :], *b_terms[g], ADD)
-        nc.vector.quantize_mx(
-            out=w_codes[:].bitcast(FP8X4),
-            scales=w_scales[:],
-            in_=w_grouped[:].rearrange("p c n u e -> p (c n u e)"),
-        )
+        w_codes = {1: quantize_w(1, "two110"), 0: quantize_w(0, "two111")}
         both = parts[:].rearrange("p u g (v e) -> p g v u e", e=2)
         for h in range(2):
             ids = slice(h * HALF, (h + 1) * HALF)
@@ -190,24 +194,26 @@ def tile_picked_hash_lin_silu_sub_l_kernel(tc, xT, w, b, offs, out):
                 both[:, 1, ids],
                 ADD,
             )
-        for c, grouped in ((1, grouped1), (0, grouped0)):
-            for h in range(2):
-                quantize_x(c, grouped, h)
+        x_codes = {
+            1: keep.tile([P, V], U32, name="x_codes1", align_bytes=64),
+            0: keep.tile([P, V], U32, name="x_codes0", tag="parts", align_bytes=64),
+        }
+        for h in range(2):
+            quantize_x(1, x_codes[1], grouped1, h)
+            quantize_x(0, x_codes[0], grouped0, h)
 
         acc = [psum.tile([P, HALF], F32, name=f"acc{h}", tag=f"last{h}") for h in range(2)]
         result = [keep.tile([P, HALF], F32, name=f"result{h}") for h in range(2)]
-        for c in (1, 0):
-            for h in range(2):
-                cols = slice(c * V + h * HALF, c * V + (h + 1) * HALF)
+        for h in range(2):
+            for c in (1, 0):
                 nc.tensor.matmul_mx(
                     out=acc[h][:],
-                    lhsT=w_codes[:, c * N : (c + 1) * N].bitcast(FP8X4),
+                    lhsT=w_codes[c][:].bitcast(FP8X4),
                     lhsT_scale=w_scales[:, c * N : (c + 1) * N],
-                    rhs=x_codes[:, cols].bitcast(FP8X4),
-                    rhs_scale=x_scales[:, cols],
+                    rhs=x_codes[c][:, h * HALF : (h + 1) * HALF].bitcast(FP8X4),
+                    rhs_scale=x_scales[:, c * V + h * HALF : c * V + (h + 1) * HALF],
                     start=(c == 1),
                     stop=(c == 0),
                 )
-        for h in range(2):
             nc.scalar.activation(result[h][:], acc[h][:], SILU, bias=bias[:])
             nc.sync.dma_start(out[:, h * HALF : (h + 1) * HALF], result[h][:])

@@ -22,7 +22,6 @@ PASSES = K // (P * PACK)
 PAIRS = 2 * PASSES
 HALF = V // 2
 COLS = V // 16
-PIECES = ((0, 256), (256, 448), (448, T))
 HALVES = ((0, T // 2), (T // 2, T))
 WINDOW = 704
 
@@ -44,7 +43,7 @@ def tile_picked_hash_lin_silu_sub_l_kernel(tc, xT, w, b, offs, out):
         w_raw = keep.tile([P, PASSES, PACK, N], F32, name="w_raw")
         bias = keep.tile([P, 1], F32, name="bias")
 
-        for lo, hi in PIECES:
+        for lo, hi in HALVES:
             nc.sync.dma_start(raw[C][:, :, lo:hi], x_rows[C][:, :, lo:hi])
         nc.sync.dma_start(offsets[:], offs)
         for lo, hi in HALVES:
@@ -72,14 +71,11 @@ def tile_picked_hash_lin_silu_sub_l_kernel(tc, xT, w, b, offs, out):
         def pack(copy, q, lo, hi):
             copy(halves(q)[:, 0, lo:hi, 0], halves(q)[:, 1, lo:hi, 1])
 
-        planes = [keep.tile([P, 2 * T], BF16, name=f"plane{r}", align_bytes=64) for r in range(2)]
-        for r in range(2):
-            nc.vector.memset(planes[r][:, T:], 0.0)
-        for lo, hi in PIECES:
+        planes = [keep.tile([P, T], BF16, name=f"plane{r}", align_bytes=64) for r in range(2)]
+        for (lo, hi), copy in zip(HALVES, (nc.scalar.copy, nc.vector.tensor_copy)):
             pack(nc.vector.tensor_copy, C, lo, hi)
-        for lo, hi in HALVES:
             for r in (1, 0):
-                nc.scalar.copy(planes[r][:, lo:hi], halves(C)[:, r, lo:hi, 1])
+                copy(planes[r][:, lo:hi], halves(C)[:, r, lo:hi, 1])
         for lo, hi in HALVES:
             pack(nc.scalar.copy, Dd, lo, hi)
         nc.scalar.copy(
@@ -123,7 +119,9 @@ def tile_picked_hash_lin_silu_sub_l_kernel(tc, xT, w, b, offs, out):
 
         c_picked = keep.tile([P, 2, 2 * V], BF16, name="c_picked", tag="a_odd", align_bytes=64)
         for e in range(2):
-            nc.scalar.activation(c_picked[:, e, :], planes[1 - e][:].indirect(offsets[:, 2 * COLS :]), COPY)
+            for g in range(2):
+                entries = offsets[:, (2 + g) * COLS : (3 + g) * COLS]
+                nc.scalar.activation(c_picked[:, e, g * V : (g + 1) * V], planes[1 - e][:].indirect(entries), COPY)
             c_wide = keep.tile([P, 2 * V], F32, name=f"c_wide{e}", tag=f"c_wide{e}", align_bytes=64)
             nc.scalar.copy(c_wide[:], c_picked[:, e, :])
             for g in range(2):

@@ -13,17 +13,19 @@ U16 = mybir.dt.uint16
 U8 = mybir.dt.uint8
 FP8X4 = mybir.dt.float8_e4m3fn_x4
 ADD = mybir.AluOpType.add
+MULT = mybir.AluOpType.mult
 COPY = mybir.ActivationFunctionType.Copy
 SILU = mybir.ActivationFunctionType.Silu
 
 P = 128
 PACK = 4
 PASSES = K // (P * PACK)
-PAIRS = 2 * PASSES
 HALF = V // 2
 COLS = V // 16
 HALVES = ((0, T // 2), (T // 2, T))
 WINDOW = 704
+SPARE = 16
+SHARE = 256
 
 
 def tile_picked_hash_lin_silu_sub_l_kernel(tc, xT, w, b, offs, out):
@@ -34,24 +36,23 @@ def tile_picked_hash_lin_silu_sub_l_kernel(tc, xT, w, b, offs, out):
 
         offsets = keep.tile([P, D * COLS], U16, name="offsets")
         x_rows = xT.rearrange("(c p u e) t -> c u p e t", c=PASSES, p=P, u=2, e=2)
-        A, C, Dd, B = (1, 0), (0, 0), (0, 1), (1, 1)
-        rows = {q: keep.tile([P, 2 * T], F32, name=f"rows{i}", align_bytes=64)[:] for i, q in enumerate((C, Dd, B))}
-        raw = {q: rows[q].rearrange("p (e t) -> p e t", e=2) for q in (C, Dd, B)}
-        a_even = keep.tile([P, WINDOW], F32, name="a_even", align_bytes=64)
-        a_odd = keep.tile([P, T], F32, name="a_odd", tag="a_odd", align_bytes=64)
-        rows.update({A: a_even[:]})
-        w_raw = keep.tile([P, PASSES, PACK, N], F32, name="w_raw")
+        w_rows = w.rearrange("(c p j) n -> c p j n", c=PASSES, p=P, j=PACK)
+        A, S, B, C = (0, 0), (0, 1), (1, 0), (1, 1)
+        rows = {q: keep.tile([P, T + WINDOW], F32, name=f"rows{i}", align_bytes=64) for i, q in enumerate((A, B, C))}
+        raw = {q: rows[q][:, : 2 * T].rearrange("p (e t) -> p e t", e=2) for q in rows}
+        single = [keep.tile([P, T + SPARE], F32, name=f"single{e}", align_bytes=64) for e in range(2)]
+        w_raw = [keep.tile([P, PACK, N], F32, name=f"w_raw{c}") for c in range(PASSES)]
         bias = keep.tile([P, 1], F32, name="bias")
 
         for lo, hi in HALVES:
-            nc.sync.dma_start(raw[C][:, :, lo:hi], x_rows[C][:, :, lo:hi])
+            nc.sync.dma_start(raw[A][:, :, lo:hi], x_rows[A][:, :, lo:hi])
         nc.sync.dma_start(offsets[:], offs)
-        for lo, hi in HALVES:
-            nc.sync.dma_start(raw[Dd][:, :, lo:hi], x_rows[Dd][:, :, lo:hi])
-        nc.sync.dma_start(a_even[:, :T], x_rows[A][:, 0])
-        nc.sync.dma_start(a_odd[:], x_rows[A][:, 1])
+        nc.sync.dma_start(single[0][:, :T], x_rows[S][:, 0])
+        nc.sync.dma_start(w_raw[0][:], w_rows[0])
         nc.sync.dma_start(raw[B], x_rows[B])
-        nc.sync.dma_start(w_raw[:], w.rearrange("(c p j) n -> p c j n", c=PASSES, p=P, j=PACK))
+        nc.sync.dma_start(raw[C], x_rows[C])
+        nc.sync.dma_start(single[1][:, :T], x_rows[S][:, 1])
+        nc.sync.dma_start(w_raw[1][:], w_rows[1])
         nc.sync.dma_start(bias[:], b)
 
         warm = keep.tile([P, 1], F32, name="warm")
@@ -63,114 +64,93 @@ def tile_picked_hash_lin_silu_sub_l_kernel(tc, xT, w, b, offs, out):
         ident16 = keep.tile([P, P], BF16, name="ident16")
         make_identity(nc, ident32[:])
         make_identity(nc, ident16[:])
-        nc.vector.memset(a_even[:, T:], 0.0)
-
-        def halves(q):
-            return rows[q].bitcast(BF16).rearrange("p (r t h) -> p r t h", r=2, h=2)
+        for e in range(2):
+            nc.vector.memset(single[e][:, T:], 0.0)
+        for q in rows:
+            nc.vector.memset(rows[q][:, 2 * T :], 0.0)
 
         def pack(copy, q, lo, hi):
-            copy(halves(q)[:, 0, lo:hi, 0], halves(q)[:, 1, lo:hi, 1])
+            halves = rows[q][:, : 2 * T].bitcast(BF16).rearrange("p (r t h) -> p r t h", r=2, h=2)
+            copy(halves[:, 1, lo:hi, 0], halves[:, 0, lo:hi, 1])
 
-        planes = [keep.tile([P, T], BF16, name=f"plane{r}", align_bytes=64) for r in range(2)]
-        for (lo, hi), copy in zip(HALVES, (nc.scalar.copy, nc.vector.tensor_copy)):
-            pack(nc.vector.tensor_copy, C, lo, hi)
-            for r in (1, 0):
-                copy(planes[r][:, lo:hi], halves(C)[:, r, lo:hi, 1])
         for lo, hi in HALVES:
-            pack(nc.scalar.copy, Dd, lo, hi)
-        nc.scalar.copy(
-            a_even[:, :T].bitcast(BF16).rearrange("p (t h) -> p t h", h=2)[:, :, 0],
-            a_odd[:].bitcast(BF16).rearrange("p (t h) -> p t h", h=2)[:, :, 1],
-        )
+            pack(nc.vector.tensor_copy, A, lo, hi)
         pack(nc.scalar.copy, B, 0, T)
+        pack(nc.scalar.copy, C, 0, T)
+
+        w_grouped = [keep.tile([P, N, PACK], BF16, name=f"w_grouped{c}", align_bytes=64) for c in range(PASSES)]
+        nc.gpsimd.tensor_scalar(w_grouped[0][:], w_raw[0][:].rearrange("p j n -> p n j"), 1.0, 0.0, MULT, ADD)
 
         def gather(q, g):
-            two = keep.tile([P, 2 * V], U32, name=f"two{q[0]}{q[1]}{g}", tag=f"two{q[0]}{q[1]}{g}", align_bytes=64)
-            window = rows[q][:, :WINDOW].bitcast(U32)
+            two = keep.tile([P, 2 * V], U32, name=f"two{q[0]}{q[1]}{g}", align_bytes=64)
+            window = rows[q][:, T:].bitcast(U32)
             nc.vector.tensor_copy(two[:], window.indirect(offsets[:, 2 * g * COLS : 2 * (g + 1) * COLS]))
             return two[:, :V].bitcast(BF16), two[:, V:].bitcast(BF16)
 
-        def add_turned(bank, sources, first, last):
-            for j, source in enumerate(sources):
-                nc.tensor.matmul(
-                    bank[:, j, :],
-                    lhsT=source,
-                    rhs=ident32[:],
-                    start=(first and j == 0),
-                    stop=(last and j == len(sources) - 1),
-                    is_transpose=True,
-                )
-
         blocks = 2 * V // P
-        c_sum = psum.tile([P, blocks, P], F32, name="c_sum")
-        d_sum = psum.tile([P, blocks, P], F32, name="d_sum")
-        c_part = keep.tile([P, 2 * V], F32, name="c_part", align_bytes=64)
-        nc.gpsimd.tensor_tensor(c_part[:], *gather(C, 0), ADD)
-        by_half = c_part[:].rearrange("p (h v e) -> p e h v", h=2, e=2)
-        add_turned(c_sum[:], [by_half[:, e, h] for e in range(2) for h in range(2)], True, False)
+        a_sum = psum.tile([P, blocks, P], F32, name="a_sum")
+        s_sum = psum.tile([P, blocks, P], F32, name="s_sum")
+
+        def add_turned(bank, j, source, start, stop):
+            nc.tensor.matmul(bank[:, j, :], lhsT=source, rhs=ident32[:], start=start, stop=stop, is_transpose=True)
+
         for g in range(2):
-            part = keep.tile([P, 2 * V], F32, name=f"d_part{g}", align_bytes=64)
-            nc.gpsimd.tensor_tensor(part[:], *gather(Dd, g), ADD)
-            add_turned(d_sum[:], [part[:, j * P : (j + 1) * P] for j in range(blocks)], g == 0, g == 1)
+            part = keep.tile([P, 2 * V], F32, name=f"a_part{g}", align_bytes=64)
+            nc.gpsimd.tensor_tensor(part[:], *gather(A, g), ADD)
+            for j in range(blocks):
+                add_turned(a_sum, j, part[:, j * P : (j + 1) * P], g == 0 and j == 0, g == 1 and j == blocks - 1)
         parts = keep.tile([P, 2, 2, 2 * V], F32, name="parts", tag="parts", align_bytes=64)
         for g in range(2):
-            nc.gpsimd.tensor_tensor(parts[:, 0, g, :], *gather(A, g), ADD)
-        b_terms = [gather(B, g) for g in range(2)]
+            nc.gpsimd.tensor_tensor(parts[:, 0, g, :], *gather(B, g), ADD)
+        c_terms = [gather(C, g) for g in range(2)]
+        nc.gpsimd.tensor_tensor(parts[:, 1, 0, :SHARE], c_terms[0][0][:, :SHARE], c_terms[0][1][:, :SHARE], ADD)
+        nc.vector.tensor_tensor(parts[:, 1, 0, SHARE:], c_terms[0][0][:, SHARE:], c_terms[0][1][:, SHARE:], ADD)
+        nc.vector.tensor_tensor(parts[:, 1, 1, :], *c_terms[1], ADD)
 
-        c_picked = keep.tile([P, 2, 2 * V], BF16, name="c_picked", tag="a_odd", align_bytes=64)
-        for e in range(2):
-            for g in range(2):
-                entries = offsets[:, (2 + g) * COLS : (3 + g) * COLS]
-                nc.scalar.activation(c_picked[:, e, g * V : (g + 1) * V], planes[1 - e][:].indirect(entries), COPY)
-            c_wide = keep.tile([P, 2 * V], F32, name=f"c_wide{e}", tag=f"c_wide{e}", align_bytes=64)
-            nc.scalar.copy(c_wide[:], c_picked[:, e, :])
-            for g in range(2):
-                for h in range(2):
-                    nc.tensor.matmul(
-                        c_sum[:, 2 * e + h, :],
-                        lhsT=c_wide[:, g * V + h * HALF : g * V + (h + 1) * HALF],
-                        rhs=ident32[:],
-                        start=False,
-                        stop=(e == 1 and g == 1 and h == 1),
-                        is_transpose=True,
-                    )
-
-        def cast_w(c, tag):
-            grouped = keep.tile([P, N, 2, 2], BF16, name=f"w_grouped{c}", tag=tag, align_bytes=64)
-            nc.scalar.copy(grouped[:], w_raw[:, c].rearrange("p (u e) n -> p n u e", e=2)[:, :, :, ::-1])
-            return grouped
+        runs = ((0, 0, 2), (0, 2, 4), (1, 0, 2), (1, 2, 3), (1, 3, 4))
+        for i, (e, d0, d1) in enumerate(runs):
+            if (e, d0) == (0, 2):
+                picked = rows[B][:, :T]
+            else:
+                picked = keep.tile([P, (d1 - d0) * V], F32, name=f"picked{e}{d0}", align_bytes=64)[:]
+            nc.scalar.activation(picked, single[e][:].indirect(offsets[:, d0 * COLS : d1 * COLS]), COPY)
+            for j in range(2 * (d1 - d0)):
+                add_turned(
+                    s_sum,
+                    2 * e + j % 2,
+                    picked[:, j * HALF : (j + 1) * HALF],
+                    i == 0 and j == 0,
+                    i == len(runs) - 1 and j == 1,
+                )
 
         backs = [psum.tile([P, 2, 2 * HALF], BF16, name=f"back{h}", tag=f"last{h}") for h in range(2)]
-        d_turned = keep.tile([P, blocks, P], BF16, name="d_turned")
-        nc.scalar.copy(d_turned[:], d_sum[:])
-        for j in range(blocks):
-            nc.tensor.transpose(backs[j // 2][:, 1, (j % 2) * P : (j % 2 + 1) * P], d_turned[:, j, :], ident16[:])
-        w_grouped = {1: cast_w(1, "c_wide0")}
-        c_turned = keep.tile([P, 2, 2 * P], BF16, name="c_turned")
+        s_turned = keep.tile([P, 2, 2 * P], BF16, name="s_turned")
         nc.scalar.copy(
-            c_turned[:].rearrange("v h (p e) -> v h p e", e=2), c_sum[:].rearrange("v (e h) p -> v h p e", e=2)
+            s_turned[:].rearrange("v h (p e) -> v h p e", e=2), s_sum[:].rearrange("v (e h) p -> v h p e", e=2)
         )
-        w_grouped.update({0: cast_w(0, "c_wide1")})
-        grouped0 = keep.tile([P, PACK * V], BF16, name="grouped0", align_bytes=64)
+        a_turned = keep.tile([P, blocks, P], BF16, name="a_turned")
+        nc.scalar.copy(a_turned[:], a_sum[:])
+        for j in range(blocks):
+            nc.tensor.transpose(backs[j // 2][:, 0, (j % 2) * P : (j % 2 + 1) * P], a_turned[:, j, :], ident16[:])
         for h in range(2):
-            nc.tensor.transpose(backs[h][:].bitcast(F32)[:, 0, :], c_turned[:, h, :].bitcast(F32), ident32[:])
+            nc.tensor.transpose(backs[h][:].bitcast(F32)[:, 1, :], s_turned[:, h, :].bitcast(F32), ident32[:])
+        grouped0 = keep.tile([P, PACK * V], BF16, name="grouped0", align_bytes=64)
         for h in range(2):
             nc.scalar.copy(
                 grouped0[:, h * PACK * HALF : (h + 1) * PACK * HALF].bitcast(F32).rearrange("p (v u) -> p v u", u=2),
                 backs[h][:].bitcast(F32).rearrange("p u v -> p v u"),
             )
+        nc.scalar.copy(w_grouped[1][:], w_raw[1][:].rearrange("p j n -> p n j"))
 
         w_scales = keep.tile([P, PASSES * N], U8, name="w_scales", align_bytes=64)
         x_scales = keep.tile([P, PASSES * V], U8, name="x_scales", align_bytes=64)
 
-        def quantize_w(c, tag):
-            codes = keep.tile([P, N], U32, name=f"w_codes{c}", tag=tag, align_bytes=64)
+        def quantize_w(c, codes):
             nc.vector.quantize_mx(
-                out=codes[:].bitcast(FP8X4),
+                out=codes.bitcast(FP8X4),
                 scales=w_scales[:, c * N : (c + 1) * N],
-                in_=w_grouped[c][:].rearrange("p n u e -> p (n u e)"),
+                in_=w_grouped[c][:].rearrange("p n j -> p (n j)"),
             )
-            return codes
 
         def quantize_x(c, codes, grouped, h):
             nc.vector.quantize_mx(
@@ -180,11 +160,11 @@ def tile_picked_hash_lin_silu_sub_l_kernel(tc, xT, w, b, offs, out):
             )
 
         grouped1 = keep.tile([P, PACK * V], BF16, name="grouped1", align_bytes=64)
-        for g in range(2):
-            nc.vector.tensor_tensor(parts[:, 1, g, :], *b_terms[g], ADD)
-        w_codes = {1: quantize_w(1, "two110"), 0: quantize_w(0, "two111")}
         both = parts[:].rearrange("p u g (v e) -> p g v u e", e=2)
+        w_words = keep.tile([P, PASSES, N], U32, name="w_words", tag="two110", align_bytes=64)
+        w_codes = [w_words[:, c, :] for c in range(PASSES)]
         for h in range(2):
+            quantize_w(h, w_codes[h])
             ids = slice(h * HALF, (h + 1) * HALF)
             nc.vector.tensor_tensor(
                 grouped1[:].rearrange("p (v u e) -> p v u e", u=2, e=2)[:, ids],
@@ -206,7 +186,7 @@ def tile_picked_hash_lin_silu_sub_l_kernel(tc, xT, w, b, offs, out):
             for c in (1, 0):
                 nc.tensor.matmul_mx(
                     out=acc[h][:],
-                    lhsT=w_codes[c][:].bitcast(FP8X4),
+                    lhsT=w_codes[c].bitcast(FP8X4),
                     lhsT_scale=w_scales[:, c * N : (c + 1) * N],
                     rhs=x_codes[c][:, h * HALF : (h + 1) * HALF].bitcast(FP8X4),
                     rhs_scale=x_scales[:, c * V + h * HALF : c * V + (h + 1) * HALF],

@@ -25,7 +25,6 @@ COLS = V // 16
 HALVES = ((0, T // 2), (T // 2, T))
 WINDOW = 704
 SPARE = 16
-SHARE = 256
 
 
 def tile_picked_hash_lin_silu_sub_l_kernel(tc, xT, w, b, offs, out):
@@ -38,18 +37,23 @@ def tile_picked_hash_lin_silu_sub_l_kernel(tc, xT, w, b, offs, out):
         x_rows = xT.rearrange("(c p u e) t -> c u p e t", c=PASSES, p=P, u=2, e=2)
         w_rows = w.rearrange("(c p j) n -> c p j n", c=PASSES, p=P, j=PACK)
         A, S, B, C = (0, 0), (0, 1), (1, 0), (1, 1)
-        rows = {q: keep.tile([P, T + WINDOW], F32, name=f"rows{i}", align_bytes=64) for i, q in enumerate((A, B, C))}
+        rows = {q: keep.tile([P, T + WINDOW], F32, name=f"rows{i}", align_bytes=64) for i, q in enumerate((B, C))}
         raw = {q: rows[q][:, : 2 * T].rearrange("p (e t) -> p e t", e=2) for q in rows}
+        a_even = keep.tile([P, T + SPARE], F32, name="a_even", align_bytes=64)
+        a_odd = keep.tile([P, WINDOW], F32, name="a_odd", align_bytes=64)
+        even = {A: a_even[:, :T], B: rows[B][:, :T], C: rows[C][:, :T]}
+        table = {A: a_odd[:], B: rows[B][:, T:], C: rows[C][:, T:]}
         single = [keep.tile([P, T + SPARE], F32, name=f"single{e}", align_bytes=64) for e in range(2)]
         w_raw = [keep.tile([P, PACK, N], F32, name=f"w_raw{c}") for c in range(PASSES)]
         bias = keep.tile([P, 1], F32, name="bias")
 
-        for lo, hi in HALVES:
-            nc.sync.dma_start(raw[A][:, :, lo:hi], x_rows[A][:, :, lo:hi])
         nc.sync.dma_start(offsets[:], offs)
-        nc.sync.dma_start(single[0][:, :T], x_rows[S][:, 0])
+        nc.sync.dma_start(a_odd[:, :T], x_rows[A][:, 1])
+        nc.sync.dma_start(a_even[:, :T], x_rows[A][:, 0])
         nc.sync.dma_start(w_raw[0][:], w_rows[0])
-        nc.sync.dma_start(raw[B], x_rows[B])
+        for lo, hi in HALVES:
+            nc.sync.dma_start(raw[B][:, :, lo:hi], x_rows[B][:, :, lo:hi])
+        nc.sync.dma_start(single[0][:, :T], x_rows[S][:, 0])
         nc.sync.dma_start(raw[C], x_rows[C])
         nc.sync.dma_start(single[1][:, :T], x_rows[S][:, 1])
         nc.sync.dma_start(w_raw[1][:], w_rows[1])
@@ -61,31 +65,13 @@ def tile_picked_hash_lin_silu_sub_l_kernel(tc, xT, w, b, offs, out):
         nc.scalar.activation(warm_out[:], warm[:], SILU)
 
         ident32 = keep.tile([P, P], F32, name="ident32")
-        ident16 = keep.tile([P, P], BF16, name="ident16")
         make_identity(nc, ident32[:])
-        make_identity(nc, ident16[:])
+        nc.vector.memset(a_odd[:, T:], 0.0)
+        nc.vector.memset(a_even[:, T:], 0.0)
         for e in range(2):
             nc.vector.memset(single[e][:, T:], 0.0)
         for q in rows:
             nc.vector.memset(rows[q][:, 2 * T :], 0.0)
-
-        def pack(copy, q, lo, hi):
-            halves = rows[q][:, : 2 * T].bitcast(BF16).rearrange("p (r t h) -> p r t h", r=2, h=2)
-            copy(halves[:, 1, lo:hi, 0], halves[:, 0, lo:hi, 1])
-
-        for lo, hi in HALVES:
-            pack(nc.vector.tensor_copy, A, lo, hi)
-        pack(nc.scalar.copy, B, 0, T)
-        pack(nc.scalar.copy, C, 0, T)
-
-        w_grouped = [keep.tile([P, N, PACK], BF16, name=f"w_grouped{c}", align_bytes=64) for c in range(PASSES)]
-        nc.gpsimd.tensor_scalar(w_grouped[0][:], w_raw[0][:].rearrange("p j n -> p n j"), 1.0, 0.0, MULT, ADD)
-
-        def gather(q, g):
-            two = keep.tile([P, 2 * V], U32, name=f"two{q[0]}{q[1]}{g}", align_bytes=64)
-            window = rows[q][:, T:].bitcast(U32)
-            nc.vector.tensor_copy(two[:], window.indirect(offsets[:, 2 * g * COLS : 2 * (g + 1) * COLS]))
-            return two[:, :V].bitcast(BF16), two[:, V:].bitcast(BF16)
 
         blocks = 2 * V // P
         a_sum = psum.tile([P, blocks, P], F32, name="a_sum")
@@ -94,51 +80,83 @@ def tile_picked_hash_lin_silu_sub_l_kernel(tc, xT, w, b, offs, out):
         def add_turned(bank, j, source, start, stop):
             nc.tensor.matmul(bank[:, j, :], lhsT=source, rhs=ident32[:], start=start, stop=stop, is_transpose=True)
 
-        for g in range(2):
-            part = keep.tile([P, 2 * V], F32, name=f"a_part{g}", align_bytes=64)
-            nc.gpsimd.tensor_tensor(part[:], *gather(A, g), ADD)
-            for j in range(blocks):
-                add_turned(a_sum, j, part[:, j * P : (j + 1) * P], g == 0 and j == 0, g == 1 and j == blocks - 1)
+        made = []
+
+        def pick(engine, bank, row, e, d0, d1, start, stop, picked=None):
+            if picked is None:
+                picked = keep.tile([P, (d1 - d0) * V], F32, name=f"picked{len(made)}", align_bytes=64)[:]
+            made.append(picked)
+            looked_up = row[:].indirect(offsets[:, d0 * COLS : d1 * COLS])
+            if engine == "vector":
+                nc.vector.tensor_copy(picked, looked_up)
+            else:
+                nc.scalar.activation(picked, looked_up, COPY)
+            for j in range(2 * (d1 - d0)):
+                last = j == 2 * (d1 - d0) - 1
+                add_turned(bank, 2 * e + j % 2, picked[:, j * HALF : (j + 1) * HALF], start and j == 0, stop and last)
+
+        def pack(copy, q, lo, hi):
+            low = table[q][:, lo:hi].bitcast(BF16).rearrange("p (t h) -> p t h", h=2)[:, :, 0]
+            copy(low, even[q][:, lo:hi].bitcast(BF16).rearrange("p (t h) -> p t h", h=2)[:, :, 1])
+
+        pick("vector", a_sum, a_odd, 1, 2, 3, True, False)
+        pick("scalar", a_sum, a_odd, 1, 3, 4, False, False)
+        pack(nc.vector.tensor_copy, A, 0, T)
+        pick("scalar", a_sum, a_even, 0, 2, 4, False, False)
+        for lo, hi in HALVES:
+            pack(nc.scalar.copy, B, lo, hi)
+        pack(nc.scalar.copy, C, 0, T)
+
+        w_grouped = [keep.tile([P, N, PACK], BF16, name=f"w_grouped{c}", align_bytes=64) for c in range(PASSES)]
+        nc.gpsimd.tensor_scalar(w_grouped[0][:], w_raw[0][:].rearrange("p j n -> p n j"), 1.0, 0.0, MULT, ADD)
+
+        def gather(q, g, two=None):
+            if two is None:
+                two = keep.tile([P, 2 * V], U32, name=f"two{q[0]}{q[1]}{g}", align_bytes=64)[:]
+            nc.vector.tensor_copy(two, table[q].bitcast(U32).indirect(offsets[:, 2 * g * COLS : 2 * (g + 1) * COLS]))
+            return two[:, :V].bitcast(BF16), two[:, V:].bitcast(BF16)
+
+        a_part = keep.tile([P, 2 * V], F32, name="a_part", align_bytes=64)
+        nc.gpsimd.tensor_tensor(a_part[:], *gather(A, 0), ADD)
+        by_row = a_part[:].rearrange("p (h v e) -> p e h v", h=2, e=2)
+        for e in range(2):
+            for h in range(2):
+                add_turned(a_sum, 2 * e + h, by_row[:, e, h], False, e == 1 and h == 1)
         parts = keep.tile([P, 2, 2, 2 * V], F32, name="parts", tag="parts", align_bytes=64)
         for g in range(2):
             nc.gpsimd.tensor_tensor(parts[:, 0, g, :], *gather(B, g), ADD)
-        c_terms = [gather(C, g) for g in range(2)]
-        nc.gpsimd.tensor_tensor(parts[:, 1, 0, :SHARE], c_terms[0][0][:, :SHARE], c_terms[0][1][:, :SHARE], ADD)
-        nc.vector.tensor_tensor(parts[:, 1, 0, SHARE:], c_terms[0][0][:, SHARE:], c_terms[0][1][:, SHARE:], ADD)
-        nc.vector.tensor_tensor(parts[:, 1, 1, :], *c_terms[1], ADD)
+        nc.gpsimd.tensor_tensor(parts[:, 1, 0, :], *gather(C, 0, parts[:, 1, 1, :].bitcast(U32)), ADD)
+        last_terms = gather(C, 1)
 
-        runs = ((0, 0, 2), (0, 2, 4), (1, 0, 2), (1, 2, 3), (1, 3, 4))
-        for i, (e, d0, d1) in enumerate(runs):
-            if (e, d0) == (0, 2):
-                picked = rows[B][:, :T]
-            else:
-                picked = keep.tile([P, (d1 - d0) * V], F32, name=f"picked{e}{d0}", align_bytes=64)[:]
-            nc.scalar.activation(picked, single[e][:].indirect(offsets[:, d0 * COLS : d1 * COLS]), COPY)
-            for j in range(2 * (d1 - d0)):
-                add_turned(
-                    s_sum,
-                    2 * e + j % 2,
-                    picked[:, j * HALF : (j + 1) * HALF],
-                    i == 0 and j == 0,
-                    i == len(runs) - 1 and j == 1,
-                )
+        def round_turned(copy, turned, bank, hs):
+            copy(
+                turned[:].rearrange("v h (p e) -> v h p e", e=2)[:, hs],
+                bank[:].rearrange("v (e h) p -> v h p e", e=2)[:, hs],
+            )
 
-        backs = [psum.tile([P, 2, 2 * HALF], BF16, name=f"back{h}", tag=f"last{h}") for h in range(2)]
-        s_turned = keep.tile([P, 2, 2 * P], BF16, name="s_turned")
-        nc.scalar.copy(
-            s_turned[:].rearrange("v h (p e) -> v h p e", e=2), s_sum[:].rearrange("v (e h) p -> v h p e", e=2)
-        )
-        a_turned = keep.tile([P, blocks, P], BF16, name="a_turned")
-        nc.scalar.copy(a_turned[:], a_sum[:])
-        for j in range(blocks):
-            nc.tensor.transpose(backs[j // 2][:, 0, (j % 2) * P : (j % 2 + 1) * P], a_turned[:, j, :], ident16[:])
+        a_turned = keep.tile([P, 2, 2 * P], BF16, name="a_turned", tag="two100", align_bytes=64)
+        round_turned(nc.vector.tensor_copy, a_turned, a_sum, slice(0, 2))
         for h in range(2):
-            nc.tensor.transpose(backs[h][:].bitcast(F32)[:, 1, :], s_turned[:, h, :].bitcast(F32), ident32[:])
+            cols = slice(h * V, (h + 1) * V)
+            nc.vector.tensor_tensor(parts[:, 1, 1, cols], last_terms[0][:, cols], last_terms[1][:, cols], ADD)
+
+        pick("scalar", s_sum, single[0], 0, 0, 2, True, False)
+        pick("scalar", s_sum, single[1], 1, 0, 2, False, False)
+        pick("scalar", s_sum, single[0], 0, 2, 4, False, False, rows[C][:, :T])
+        pick("scalar", s_sum, single[1], 1, 2, 3, False, False)
+        pick("scalar", s_sum, single[1], 1, 3, 4, False, True)
+
+        backs = [psum.tile([P, 2, HALF], F32, name=f"back{h}", tag=f"last{h}") for h in range(2)]
+        s_turned = keep.tile([P, 2, 2 * P], BF16, name="s_turned")
+        for h in range(2):
+            round_turned(nc.scalar.copy, s_turned, s_sum, slice(h, h + 1))
         grouped0 = keep.tile([P, PACK * V], BF16, name="grouped0", align_bytes=64)
         for h in range(2):
+            for u, turned in enumerate((a_turned, s_turned)):
+                nc.tensor.transpose(backs[h][:, u, :], turned[:, h, :].bitcast(F32), ident32[:])
             nc.scalar.copy(
                 grouped0[:, h * PACK * HALF : (h + 1) * PACK * HALF].bitcast(F32).rearrange("p (v u) -> p v u", u=2),
-                backs[h][:].bitcast(F32).rearrange("p u v -> p v u"),
+                backs[h][:].rearrange("p u v -> p v u"),
             )
         nc.scalar.copy(w_grouped[1][:], w_raw[1][:].rearrange("p j n -> p n j"))
 
@@ -161,10 +179,12 @@ def tile_picked_hash_lin_silu_sub_l_kernel(tc, xT, w, b, offs, out):
 
         grouped1 = keep.tile([P, PACK * V], BF16, name="grouped1", align_bytes=64)
         both = parts[:].rearrange("p u g (v e) -> p g v u e", e=2)
-        w_words = keep.tile([P, PASSES, N], U32, name="w_words", tag="two110", align_bytes=64)
-        w_codes = [w_words[:, c, :] for c in range(PASSES)]
+        w_codes = [
+            keep.tile([P, N], U32, name="w_codes0", tag="two101", align_bytes=64)[:],
+            keep.tile([P, N], U32, name="w_codes1", tag="two111", align_bytes=64)[:],
+        ]
+        quantize_w(0, w_codes[0])
         for h in range(2):
-            quantize_w(h, w_codes[h])
             ids = slice(h * HALF, (h + 1) * HALF)
             nc.vector.tensor_tensor(
                 grouped1[:].rearrange("p (v u e) -> p v u e", u=2, e=2)[:, ids],
@@ -172,6 +192,8 @@ def tile_picked_hash_lin_silu_sub_l_kernel(tc, xT, w, b, offs, out):
                 both[:, 1, ids],
                 ADD,
             )
+            if h == 0:
+                quantize_w(1, w_codes[1])
         x_codes = {
             1: keep.tile([P, V], U32, name="x_codes1", align_bytes=64),
             0: keep.tile([P, V], U32, name="x_codes0", tag="parts", align_bytes=64),

@@ -34,28 +34,31 @@ def tile_picked_hash_lin_silu_sub_l_kernel(tc, xT, w, b, offs, out):
         psum = ctx.enter_context(tc.psum_pool(name="psum", bufs=1))
 
         offsets = keep.tile([P, D * COLS], U16, name="offsets")
-        x_rows = xT.rearrange("(c p u e) t -> c u p e t", c=PASSES, p=P, u=2, e=2)
+        x_rows = xT.rearrange("(c p j) t -> c p j t", c=PASSES, p=P, j=PACK)
         w_rows = w.rearrange("(c p j) n -> c p j n", c=PASSES, p=P, j=PACK)
-        A, S, B, C = (0, 0), (0, 1), (1, 0), (1, 1)
-        rows = {q: keep.tile([P, T + WINDOW], F32, name=f"rows{i}", align_bytes=64) for i, q in enumerate((B, C))}
-        raw = {q: rows[q][:, : 2 * T].rearrange("p (e t) -> p e t", e=2) for q in rows}
-        a_even = keep.tile([P, T + SPARE], F32, name="a_even", align_bytes=64)
-        a_odd = keep.tile([P, WINDOW], F32, name="a_odd", align_bytes=64)
-        even = {A: a_even[:, :T], B: rows[B][:, :T], C: rows[C][:, :T]}
-        table = {A: a_odd[:], B: rows[B][:, T:], C: rows[C][:, T:]}
-        single = [keep.tile([P, T + SPARE], F32, name=f"single{e}", align_bytes=64) for e in range(2)]
+        single = [keep.tile([P, T + SPARE], F32, name=f"single{j}", align_bytes=64) for j in range(PACK)]
+        first_pair = keep.tile([P, T + WINDOW], F32, name="first_pair", align_bytes=64)
+        last_even = keep.tile([P, T], F32, name="last_even", tag="last_even", align_bytes=64)
+        last_odd = keep.tile([P, WINDOW], F32, name="last_odd", align_bytes=64)
+        even = [first_pair[:, :T], last_even[:]]
+        table = [first_pair[:, T:], last_odd[:]]
         w_raw = [keep.tile([P, PACK, N], F32, name=f"w_raw{c}") for c in range(PASSES)]
         bias = keep.tile([P, 1], F32, name="bias")
 
+        def load_single(j):
+            nc.sync.dma_start(single[j][:, :T], x_rows[0][:, j])
+
         nc.sync.dma_start(offsets[:], offs)
-        nc.sync.dma_start(a_odd[:, :T], x_rows[A][:, 1])
-        nc.sync.dma_start(a_even[:, :T], x_rows[A][:, 0])
-        nc.sync.dma_start(w_raw[0][:], w_rows[0])
+        load_single(0)
         for lo, hi in HALVES:
-            nc.sync.dma_start(raw[B][:, :, lo:hi], x_rows[B][:, :, lo:hi])
-        nc.sync.dma_start(single[0][:, :T], x_rows[S][:, 0])
-        nc.sync.dma_start(raw[C], x_rows[C])
-        nc.sync.dma_start(single[1][:, :T], x_rows[S][:, 1])
+            rows = first_pair[:, : 2 * T].rearrange("p (e t) -> p e t", e=2)
+            nc.sync.dma_start(rows[:, :, lo:hi], x_rows[1][:, 0:2, lo:hi])
+        load_single(1)
+        nc.sync.dma_start(w_raw[0][:], w_rows[0])
+        nc.sync.dma_start(last_even[:], x_rows[1][:, 2])
+        nc.sync.dma_start(last_odd[:, :T], x_rows[1][:, 3])
+        load_single(2)
+        load_single(3)
         nc.sync.dma_start(w_raw[1][:], w_rows[1])
         nc.sync.dma_start(bias[:], b)
 
@@ -64,143 +67,146 @@ def tile_picked_hash_lin_silu_sub_l_kernel(tc, xT, w, b, offs, out):
         nc.vector.memset(warm[:], 0.0)
         nc.scalar.activation(warm_out[:], warm[:], SILU)
 
-        ident32 = keep.tile([P, P], F32, name="ident32")
-        make_identity(nc, ident32[:])
-        nc.vector.memset(a_odd[:, T:], 0.0)
-        nc.vector.memset(a_even[:, T:], 0.0)
-        for e in range(2):
-            nc.vector.memset(single[e][:, T:], 0.0)
-        for q in rows:
-            nc.vector.memset(rows[q][:, 2 * T :], 0.0)
+        identity = keep.tile([P, P], F32, name="identity")
+        make_identity(nc, identity[:])
+        for j in range(PACK):
+            nc.vector.memset(single[j][:, T:], 0.0)
+        for u in range(2):
+            nc.vector.memset(table[u][:, T:], 0.0)
 
-        blocks = 2 * V // P
-        a_sum = psum.tile([P, blocks, P], F32, name="a_sum")
-        s_sum = psum.tile([P, blocks, P], F32, name="s_sum")
+        early_sum = psum.tile([P, 2, 2, P], F32, name="early_sum")
+        late_sums = [psum.tile([P, 2, P], F32, name=f"late_sum{h}") for h in range(2)]
+        sums = [[early_sum[:, h] for h in range(2)], [late_sums[h][:] for h in range(2)]]
 
-        def add_turned(bank, j, source, start, stop):
-            nc.tensor.matmul(bank[:, j, :], lhsT=source, rhs=ident32[:], start=start, stop=stop, is_transpose=True)
-
-        made = []
-
-        def pick(engine, bank, row, e, d0, d1, start, stop, picked=None):
-            if picked is None:
-                picked = keep.tile([P, (d1 - d0) * V], F32, name=f"picked{len(made)}", align_bytes=64)[:]
-            made.append(picked)
-            looked_up = row[:].indirect(offsets[:, d0 * COLS : d1 * COLS])
+        def look_up(engine, j, d0, d1, tag=None):
+            name = f"picked{j}{d0}"
+            picked = keep.tile([P, (d1 - d0) * V], F32, name=name, tag=tag if tag else name, align_bytes=64)[:]
+            looked_up = single[j][:].indirect(offsets[:, d0 * COLS : d1 * COLS])
             if engine == "vector":
                 nc.vector.tensor_copy(picked, looked_up)
             else:
                 nc.scalar.activation(picked, looked_up, COPY)
-            for j in range(2 * (d1 - d0)):
-                last = j == 2 * (d1 - d0) - 1
-                add_turned(bank, 2 * e + j % 2, picked[:, j * HALF : (j + 1) * HALF], start and j == 0, stop and last)
+            return picked
 
-        def pack(copy, q, lo, hi):
-            low = table[q][:, lo:hi].bitcast(BF16).rearrange("p (t h) -> p t h", h=2)[:, :, 0]
-            copy(low, even[q][:, lo:hi].bitcast(BF16).rearrange("p (t h) -> p t h", h=2)[:, :, 1])
+        def add_turned(j, h, piece, start=False, stop=False):
+            nc.tensor.matmul(
+                sums[j // 2][h][:, j % 2, :],
+                lhsT=piece[:, h * HALF : (h + 1) * HALF],
+                rhs=identity[:],
+                start=start,
+                stop=stop,
+                is_transpose=True,
+            )
 
-        pick("vector", a_sum, a_odd, 1, 2, 3, True, False)
-        pick("scalar", a_sum, a_odd, 1, 3, 4, False, False)
-        pack(nc.vector.tensor_copy, A, 0, T)
-        pick("scalar", a_sum, a_even, 0, 2, 4, False, False)
-        for lo, hi in HALVES:
-            pack(nc.scalar.copy, B, lo, hi)
-        pack(nc.scalar.copy, C, 0, T)
+        def pick(engine, j, d0, d1, start=False, stop=False, tag=None):
+            picked = look_up(engine, j, d0, d1, tag)
+            for d in range(d1 - d0):
+                for h in range(2):
+                    opens = start and d == 0 and (h == 0 or j >= 2)
+                    add_turned(j, h, picked[:, d * V : (d + 1) * V], opens, stop and d == d1 - d0 - 1 and h == 1)
 
-        w_grouped = [keep.tile([P, N, PACK], BF16, name=f"w_grouped{c}", align_bytes=64) for c in range(PASSES)]
-        nc.gpsimd.tensor_scalar(w_grouped[0][:], w_raw[0][:].rearrange("p j n -> p n j"), 1.0, 0.0, MULT, ADD)
+        def pack(copy, u, lo, hi):
+            low = table[u][:, lo:hi].bitcast(BF16).rearrange("p (t h) -> p t h", h=2)[:, :, 0]
+            copy(low, even[u][:, lo:hi].bitcast(BF16).rearrange("p (t h) -> p t h", h=2)[:, :, 1])
 
-        def gather(q, g, two=None):
-            if two is None:
-                two = keep.tile([P, 2 * V], U32, name=f"two{q[0]}{q[1]}{g}", align_bytes=64)[:]
-            nc.vector.tensor_copy(two, table[q].bitcast(U32).indirect(offsets[:, 2 * g * COLS : 2 * (g + 1) * COLS]))
+        def gather(u, g):
+            two = keep.tile([P, 2 * V], U32, name=f"two{u}{g}", align_bytes=64)
+            window = table[u].bitcast(U32)
+            nc.vector.tensor_copy(two[:], window.indirect(offsets[:, 2 * g * COLS : 2 * (g + 1) * COLS]))
             return two[:, :V].bitcast(BF16), two[:, V:].bitcast(BF16)
 
-        a_part = keep.tile([P, 2 * V], F32, name="a_part", align_bytes=64)
-        nc.gpsimd.tensor_tensor(a_part[:], *gather(A, 0), ADD)
-        by_row = a_part[:].rearrange("p (h v e) -> p e h v", h=2, e=2)
-        for e in range(2):
-            for h in range(2):
-                add_turned(a_sum, 2 * e + h, by_row[:, e, h], False, e == 1 and h == 1)
+        pick("vector", 0, 0, 1, start=True)
+        for lo, hi in HALVES:
+            pack(nc.vector.tensor_copy, 0, lo, hi)
+        pack(nc.scalar.copy, 1, 0, T)
+        w_grouped = [keep.tile([P, N, PACK], BF16, name="w_grouped0", align_bytes=64)]
+        nc.gpsimd.tensor_scalar(w_grouped[0][:], w_raw[0][:].rearrange("p j n -> p n j"), 1.0, 0.0, MULT, ADD)
         parts = keep.tile([P, 2, 2, 2 * V], F32, name="parts", tag="parts", align_bytes=64)
         for g in range(2):
-            nc.gpsimd.tensor_tensor(parts[:, 0, g, :], *gather(B, g), ADD)
-        nc.gpsimd.tensor_tensor(parts[:, 1, 0, :], *gather(C, 0, parts[:, 1, 1, :].bitcast(U32)), ADD)
-        last_terms = gather(C, 1)
+            nc.gpsimd.tensor_tensor(parts[:, 0, g, :], *gather(0, g), ADD)
+        middle = look_up("vector", 1, 3, 4)
+        for g in range(2):
+            nc.gpsimd.tensor_tensor(parts[:, 1, g, :], *gather(1, g), ADD)
 
-        def round_turned(copy, turned, bank, hs):
-            copy(
-                turned[:].rearrange("v h (p e) -> v h p e", e=2)[:, hs],
-                bank[:].rearrange("v (e h) p -> v h p e", e=2)[:, hs],
-            )
-
-        a_turned = keep.tile([P, 2, 2 * P], BF16, name="a_turned", tag="two100", align_bytes=64)
-        round_turned(nc.vector.tensor_copy, a_turned, a_sum, slice(0, 2))
+        pick("scalar", 0, 1, 3)
+        pick("scalar", 0, 3, 4)
+        pick("scalar", 1, 0, 2)
         for h in range(2):
-            cols = slice(h * V, (h + 1) * V)
-            nc.vector.tensor_tensor(parts[:, 1, 1, cols], last_terms[0][:, cols], last_terms[1][:, cols], ADD)
-
-        pick("scalar", s_sum, single[0], 0, 0, 2, True, False)
-        pick("scalar", s_sum, single[1], 1, 0, 2, False, False)
-        pick("scalar", s_sum, single[0], 0, 2, 4, False, False, rows[C][:, :T])
-        pick("scalar", s_sum, single[1], 1, 2, 3, False, False)
-        pick("scalar", s_sum, single[1], 1, 3, 4, False, True)
-
-        backs = [psum.tile([P, 2, HALF], F32, name=f"back{h}", tag=f"last{h}") for h in range(2)]
-        s_turned = keep.tile([P, 2, 2 * P], BF16, name="s_turned")
+            add_turned(1, h, middle)
+        pick("scalar", 2, 0, 2, start=True)
+        pick("scalar", 1, 2, 3, stop=True, tag="last_even")
+        pick("scalar", 2, 2, 3)
+        pick("scalar", 2, 3, 4)
+        pick("vector", 3, 0, 1)
+        pick("scalar", 3, 2, 3)
+        last = [look_up("vector", 3, 1, 2), look_up("scalar", 3, 3, 4)]
         for h in range(2):
-            round_turned(nc.scalar.copy, s_turned, s_sum, slice(h, h + 1))
-        grouped0 = keep.tile([P, PACK * V], BF16, name="grouped0", align_bytes=64)
+            for i in range(2):
+                add_turned(3, h, last[i], stop=(i == 1))
+
+        turned = [
+            keep.tile([P, 2, 2 * P], BF16, name="turned0", tag="picked23", align_bytes=64),
+            keep.tile([P, 2, 2 * P], BF16, name="turned1", align_bytes=64),
+        ]
+
+        nc.scalar.copy(
+            turned[0][:].rearrange("v h (p e) -> v h p e", e=2), early_sum[:].rearrange("v h e p -> v h p e")
+        )
         for h in range(2):
-            for u, turned in enumerate((a_turned, s_turned)):
-                nc.tensor.transpose(backs[h][:, u, :], turned[:, h, :].bitcast(F32), ident32[:])
             nc.scalar.copy(
-                grouped0[:, h * PACK * HALF : (h + 1) * PACK * HALF].bitcast(F32).rearrange("p (v u) -> p v u", u=2),
+                turned[1][:, h].rearrange("v (p e) -> v p e", e=2), late_sums[h][:].rearrange("v e p -> v p e")
+            )
+        backs = [psum.tile([P, 2, HALF], F32, name=f"back{h}", tag=f"last{h}") for h in range(2)]
+        grouped = [keep.tile([P, PACK * V], BF16, name=f"grouped{c}", align_bytes=64) for c in range(PASSES)]
+        for h in range(2):
+            for u in (1, 0):
+                nc.tensor.transpose(backs[h][:, u, :], turned[u][:, h, :].bitcast(F32), identity[:])
+            nc.scalar.copy(
+                grouped[0][:, h * PACK * HALF : (h + 1) * PACK * HALF].bitcast(F32).rearrange("p (v u) -> p v u", u=2),
                 backs[h][:].rearrange("p u v -> p v u"),
             )
-        nc.scalar.copy(w_grouped[1][:], w_raw[1][:].rearrange("p j n -> p n j"))
 
         w_scales = keep.tile([P, PASSES * N], U8, name="w_scales", align_bytes=64)
         x_scales = keep.tile([P, PASSES * V], U8, name="x_scales", align_bytes=64)
+        w_codes = [
+            keep.tile([P, N], U32, name="w_codes0", tag="two10", align_bytes=64),
+            keep.tile([P, N], U32, name="w_codes1", tag="w_codes1", align_bytes=64),
+        ]
+        x_codes = [
+            keep.tile([P, V], U32, name="x_codes0", tag="parts", align_bytes=64),
+            keep.tile([P, V], U32, name="x_codes1", align_bytes=64),
+        ]
 
-        def quantize_w(c, codes):
+        def quantize_w(c):
             nc.vector.quantize_mx(
-                out=codes.bitcast(FP8X4),
+                out=w_codes[c][:].bitcast(FP8X4),
                 scales=w_scales[:, c * N : (c + 1) * N],
                 in_=w_grouped[c][:].rearrange("p n j -> p (n j)"),
             )
 
-        def quantize_x(c, codes, grouped, h):
+        def quantize_x(c, h):
             nc.vector.quantize_mx(
-                out=codes[:, h * HALF : (h + 1) * HALF].bitcast(FP8X4),
+                out=x_codes[c][:, h * HALF : (h + 1) * HALF].bitcast(FP8X4),
                 scales=x_scales[:, c * V + h * HALF : c * V + (h + 1) * HALF],
-                in_=grouped[:, h * PACK * HALF : (h + 1) * PACK * HALF],
+                in_=grouped[c][:, h * PACK * HALF : (h + 1) * PACK * HALF],
             )
 
-        grouped1 = keep.tile([P, PACK * V], BF16, name="grouped1", align_bytes=64)
+        w_grouped.extend([keep.tile([P, N, PACK], BF16, name="w_grouped1", tag="two11", align_bytes=64)])
+        nc.vector.tensor_copy(w_grouped[1][:], w_raw[1][:].rearrange("p j n -> p n j"))
+        quantize_w(0)
         both = parts[:].rearrange("p u g (v e) -> p g v u e", e=2)
-        w_codes = [
-            keep.tile([P, N], U32, name="w_codes0", tag="two101", align_bytes=64)[:],
-            keep.tile([P, N], U32, name="w_codes1", tag="two111", align_bytes=64)[:],
-        ]
-        quantize_w(0, w_codes[0])
         for h in range(2):
             ids = slice(h * HALF, (h + 1) * HALF)
             nc.vector.tensor_tensor(
-                grouped1[:].rearrange("p (v u e) -> p v u e", u=2, e=2)[:, ids],
+                grouped[1][:].rearrange("p (v u e) -> p v u e", u=2, e=2)[:, ids],
                 both[:, 0, ids],
                 both[:, 1, ids],
                 ADD,
             )
-            if h == 0:
-                quantize_w(1, w_codes[1])
-        x_codes = {
-            1: keep.tile([P, V], U32, name="x_codes1", align_bytes=64),
-            0: keep.tile([P, V], U32, name="x_codes0", tag="parts", align_bytes=64),
-        }
+        quantize_w(1)
         for h in range(2):
-            quantize_x(1, x_codes[1], grouped1, h)
-            quantize_x(0, x_codes[0], grouped0, h)
+            quantize_x(1, h)
+            quantize_x(0, h)
 
         acc = [psum.tile([P, HALF], F32, name=f"acc{h}", tag=f"last{h}") for h in range(2)]
         result = [keep.tile([P, HALF], F32, name=f"result{h}") for h in range(2)]
@@ -208,7 +214,7 @@ def tile_picked_hash_lin_silu_sub_l_kernel(tc, xT, w, b, offs, out):
             for c in (1, 0):
                 nc.tensor.matmul_mx(
                     out=acc[h][:],
-                    lhsT=w_codes[c].bitcast(FP8X4),
+                    lhsT=w_codes[c][:].bitcast(FP8X4),
                     lhsT_scale=w_scales[:, c * N : (c + 1) * N],
                     rhs=x_codes[c][:, h * HALF : (h + 1) * HALF].bitcast(FP8X4),
                     rhs_scale=x_scales[:, c * V + h * HALF : c * V + (h + 1) * HALF],

@@ -25,6 +25,7 @@ COLS = V // 16
 HALVES = ((0, T // 2), (T // 2, T))
 WINDOW = 704
 SPARE = 16
+SHARE = 256
 
 
 def tile_picked_hash_lin_silu_sub_l_kernel(tc, xT, w, b, offs, out):
@@ -37,26 +38,25 @@ def tile_picked_hash_lin_silu_sub_l_kernel(tc, xT, w, b, offs, out):
         x_rows = xT.rearrange("(c p j) t -> c p j t", c=PASSES, p=P, j=PACK)
         w_rows = w.rearrange("(c p j) n -> c p j n", c=PASSES, p=P, j=PACK)
         single = [keep.tile([P, T + SPARE], F32, name=f"single{j}", align_bytes=64) for j in range(PACK)]
-        first_pair = keep.tile([P, T + WINDOW], F32, name="first_pair", align_bytes=64)
-        last_even = keep.tile([P, T], F32, name="last_even", tag="last_even", align_bytes=64)
-        last_odd = keep.tile([P, WINDOW], F32, name="last_odd", align_bytes=64)
-        even = [first_pair[:, :T], last_even[:]]
-        table = [first_pair[:, T:], last_odd[:]]
+        pair = [keep.tile([P, T + WINDOW], F32, name=f"pair{u}", align_bytes=64) for u in range(2)]
+        even = [pair[u][:, :T] for u in range(2)]
+        table = [pair[u][:, T:] for u in range(2)]
         w_raw = [keep.tile([P, PACK, N], F32, name=f"w_raw{c}") for c in range(PASSES)]
         bias = keep.tile([P, 1], F32, name="bias")
 
         def load_single(j):
             nc.sync.dma_start(single[j][:, :T], x_rows[0][:, j])
 
+        def load_pair(u):
+            rows = pair[u][:, : 2 * T].rearrange("p (e t) -> p e t", e=2)
+            nc.sync.dma_start(rows, x_rows[1][:, 2 * u : 2 * u + 2])
+
         nc.sync.dma_start(offsets[:], offs)
         load_single(0)
-        for lo, hi in HALVES:
-            rows = first_pair[:, : 2 * T].rearrange("p (e t) -> p e t", e=2)
-            nc.sync.dma_start(rows[:, :, lo:hi], x_rows[1][:, 0:2, lo:hi])
+        load_pair(0)
         load_single(1)
         nc.sync.dma_start(w_raw[0][:], w_rows[0])
-        nc.sync.dma_start(last_even[:], x_rows[1][:, 2])
-        nc.sync.dma_start(last_odd[:, :T], x_rows[1][:, 3])
+        load_pair(1)
         load_single(2)
         load_single(3)
         nc.sync.dma_start(w_raw[1][:], w_rows[1])
@@ -78,32 +78,32 @@ def tile_picked_hash_lin_silu_sub_l_kernel(tc, xT, w, b, offs, out):
         late_sums = [psum.tile([P, 2, P], F32, name=f"late_sum{h}") for h in range(2)]
         sums = [[early_sum[:, h] for h in range(2)], [late_sums[h][:] for h in range(2)]]
 
-        def look_up(engine, j, d0, d1, tag=None):
-            name = f"picked{j}{d0}"
-            picked = keep.tile([P, (d1 - d0) * V], F32, name=name, tag=tag if tag else name, align_bytes=64)[:]
-            looked_up = single[j][:].indirect(offsets[:, d0 * COLS : d1 * COLS])
+        def look_up(engine, j, b0, b1, picked=None):
+            if picked is None:
+                picked = keep.tile([P, (b1 - b0) * HALF], F32, name=f"picked{j}{b0}", align_bytes=64)[:]
+            looked_up = single[j][:].indirect(offsets[:, b0 * COLS // 2 : b1 * COLS // 2])
             if engine == "vector":
                 nc.vector.tensor_copy(picked, looked_up)
             else:
                 nc.scalar.activation(picked, looked_up, COPY)
-            return picked
+            return [(j, block % 2, picked[:, (block - b0) * HALF : (block - b0 + 1) * HALF]) for block in range(b0, b1)]
 
-        def add_turned(j, h, piece, start=False, stop=False):
-            nc.tensor.matmul(
-                sums[j // 2][h][:, j % 2, :],
-                lhsT=piece[:, h * HALF : (h + 1) * HALF],
-                rhs=identity[:],
-                start=start,
-                stop=stop,
-                is_transpose=True,
-            )
+        done = {}
 
-        def pick(engine, j, d0, d1, start=False, stop=False, tag=None):
-            picked = look_up(engine, j, d0, d1, tag)
-            for d in range(d1 - d0):
-                for h in range(2):
-                    opens = start and d == 0 and (h == 0 or j >= 2)
-                    add_turned(j, h, picked[:, d * V : (d + 1) * V], opens, stop and d == d1 - d0 - 1 and h == 1)
+        def add_turned(blocks):
+            for j, h, block in blocks:
+                bank = (0, 0) if j < 2 else (1, h)
+                total = 4 * D if j < 2 else 2 * D
+                count = done.get(bank, 0)
+                nc.tensor.matmul(
+                    sums[j // 2][h][:, j % 2, :],
+                    lhsT=block,
+                    rhs=identity[:],
+                    start=(count == 0),
+                    stop=(count == total - 1),
+                    is_transpose=True,
+                )
+                done.update({bank: count + 1})
 
         def pack(copy, u, lo, hi):
             low = table[u][:, lo:hi].bitcast(BF16).rearrange("p (t h) -> p t h", h=2)[:, :, 0]
@@ -115,37 +115,33 @@ def tile_picked_hash_lin_silu_sub_l_kernel(tc, xT, w, b, offs, out):
             nc.vector.tensor_copy(two[:], window.indirect(offsets[:, 2 * g * COLS : 2 * (g + 1) * COLS]))
             return two[:, :V].bitcast(BF16), two[:, V:].bitcast(BF16)
 
-        pick("vector", 0, 0, 1, start=True)
-        for lo, hi in HALVES:
-            pack(nc.vector.tensor_copy, 0, lo, hi)
+        head = look_up("vector", 0, 0, 3)
+        pack(nc.vector.tensor_copy, 0, 0, T)
         pack(nc.scalar.copy, 1, 0, T)
         w_grouped = [keep.tile([P, N, PACK], BF16, name="w_grouped0", align_bytes=64)]
         nc.gpsimd.tensor_scalar(w_grouped[0][:], w_raw[0][:].rearrange("p j n -> p n j"), 1.0, 0.0, MULT, ADD)
         parts = keep.tile([P, 2, 2, 2 * V], F32, name="parts", tag="parts", align_bytes=64)
         for g in range(2):
             nc.gpsimd.tensor_tensor(parts[:, 0, g, :], *gather(0, g), ADD)
-        middle = look_up("vector", 1, 3, 4)
-        for g in range(2):
-            nc.gpsimd.tensor_tensor(parts[:, 1, g, :], *gather(1, g), ADD)
+        middle = look_up("vector", 1, 6, 8)
+        nc.gpsimd.tensor_tensor(parts[:, 1, 0, :], *gather(1, 0), ADD)
+        last_terms = gather(1, 1)
+        nc.gpsimd.tensor_tensor(parts[:, 1, 1, :SHARE], last_terms[0][:, :SHARE], last_terms[1][:, :SHARE], ADD)
 
-        pick("scalar", 0, 1, 3)
-        pick("scalar", 0, 3, 4)
-        pick("scalar", 1, 0, 2)
-        for h in range(2):
-            add_turned(1, h, middle)
-        pick("scalar", 2, 0, 2, start=True)
-        pick("scalar", 1, 2, 3, stop=True, tag="last_even")
-        pick("scalar", 2, 2, 3)
-        pick("scalar", 2, 3, 4)
-        pick("vector", 3, 0, 1)
-        pick("scalar", 3, 2, 3)
-        last = [look_up("vector", 3, 1, 2), look_up("scalar", 3, 3, 4)]
-        for h in range(2):
-            for i in range(2):
-                add_turned(3, h, last[i], stop=(i == 1))
-
+        first = look_up("scalar", 0, 3, 5)
+        add_turned(first + head)
+        add_turned(look_up("scalar", 0, 5, 8))
+        add_turned(look_up("scalar", 1, 0, 4))
+        add_turned(middle)
+        add_turned(look_up("scalar", 2, 0, 4))
+        add_turned(look_up("scalar", 1, 4, 6, even[1][:, :V]))
+        add_turned(look_up("scalar", 2, 4, 6))
+        add_turned(look_up("scalar", 2, 6, 8))
+        add_turned(look_up("scalar", 3, 3, 6))
+        add_turned(look_up("vector", 3, 0, 3))
+        add_turned(sorted(look_up("scalar", 3, 6, 8), key=lambda block: block[1]))
         turned = [
-            keep.tile([P, 2, 2 * P], BF16, name="turned0", tag="picked23", align_bytes=64),
+            keep.tile([P, 2, 2 * P], BF16, name="turned0", tag="picked26", align_bytes=64),
             keep.tile([P, 2, 2 * P], BF16, name="turned1", align_bytes=64),
         ]
 
@@ -169,7 +165,7 @@ def tile_picked_hash_lin_silu_sub_l_kernel(tc, xT, w, b, offs, out):
         w_scales = keep.tile([P, PASSES * N], U8, name="w_scales", align_bytes=64)
         x_scales = keep.tile([P, PASSES * V], U8, name="x_scales", align_bytes=64)
         w_codes = [
-            keep.tile([P, N], U32, name="w_codes0", tag="two10", align_bytes=64),
+            keep.tile([P, N], U32, name="w_codes0", tag="two01", align_bytes=64),
             keep.tile([P, N], U32, name="w_codes1", tag="w_codes1", align_bytes=64),
         ]
         x_codes = [
@@ -191,8 +187,9 @@ def tile_picked_hash_lin_silu_sub_l_kernel(tc, xT, w, b, offs, out):
                 in_=grouped[c][:, h * PACK * HALF : (h + 1) * PACK * HALF],
             )
 
-        w_grouped.extend([keep.tile([P, N, PACK], BF16, name="w_grouped1", tag="two11", align_bytes=64)])
+        w_grouped.extend([keep.tile([P, N, PACK], BF16, name="w_grouped1", tag="two10", align_bytes=64)])
         nc.vector.tensor_copy(w_grouped[1][:], w_raw[1][:].rearrange("p j n -> p n j"))
+        nc.vector.tensor_tensor(parts[:, 1, 1, SHARE:], last_terms[0][:, SHARE:], last_terms[1][:, SHARE:], ADD)
         quantize_w(0)
         both = parts[:].rearrange("p u g (v e) -> p g v u e", e=2)
         for h in range(2):

@@ -25,7 +25,6 @@ COLS = V // 16
 HALVES = ((0, T // 2), (T // 2, T))
 WINDOW = 704
 SPARE = 16
-SHARE = 256
 
 
 def tile_picked_hash_lin_silu_sub_l_kernel(tc, xT, w, b, offs, out):
@@ -47,16 +46,17 @@ def tile_picked_hash_lin_silu_sub_l_kernel(tc, xT, w, b, offs, out):
         def load_single(j):
             nc.sync.dma_start(single[j][:, :T], x_rows[0][:, j])
 
-        def load_pair(u):
+        def load_pair(u, lo, hi):
             rows = pair[u][:, : 2 * T].rearrange("p (e t) -> p e t", e=2)
-            nc.sync.dma_start(rows, x_rows[1][:, 2 * u : 2 * u + 2])
+            nc.sync.dma_start(rows[:, :, lo:hi], x_rows[1][:, 2 * u : 2 * u + 2, lo:hi])
 
         nc.sync.dma_start(offsets[:], offs)
         load_single(0)
-        load_pair(0)
+        for lo, hi in HALVES:
+            load_pair(0, lo, hi)
         load_single(1)
         nc.sync.dma_start(w_raw[0][:], w_rows[0])
-        load_pair(1)
+        load_pair(1, 0, T)
         load_single(2)
         load_single(3)
         nc.sync.dma_start(w_raw[1][:], w_rows[1])
@@ -78,9 +78,8 @@ def tile_picked_hash_lin_silu_sub_l_kernel(tc, xT, w, b, offs, out):
         late_sums = [psum.tile([P, 2, P], F32, name=f"late_sum{h}") for h in range(2)]
         sums = [[early_sum[:, h] for h in range(2)], [late_sums[h][:] for h in range(2)]]
 
-        def look_up(engine, j, b0, b1, picked=None):
-            if picked is None:
-                picked = keep.tile([P, (b1 - b0) * HALF], F32, name=f"picked{j}{b0}", align_bytes=64)[:]
+        def look_up(engine, j, b0, b1):
+            picked = keep.tile([P, (b1 - b0) * HALF], F32, name=f"picked{j}{b0}", align_bytes=64)[:]
             looked_up = single[j][:].indirect(offsets[:, b0 * COLS // 2 : b1 * COLS // 2])
             if engine == "vector":
                 nc.vector.tensor_copy(picked, looked_up)
@@ -116,7 +115,8 @@ def tile_picked_hash_lin_silu_sub_l_kernel(tc, xT, w, b, offs, out):
             return two[:, :V].bitcast(BF16), two[:, V:].bitcast(BF16)
 
         head = look_up("vector", 0, 0, 3)
-        pack(nc.vector.tensor_copy, 0, 0, T)
+        for lo, hi in HALVES:
+            pack(nc.vector.tensor_copy, 0, lo, hi)
         pack(nc.scalar.copy, 1, 0, T)
         w_grouped = [keep.tile([P, N, PACK], BF16, name="w_grouped0", align_bytes=64)]
         nc.gpsimd.tensor_scalar(w_grouped[0][:], w_raw[0][:].rearrange("p j n -> p n j"), 1.0, 0.0, MULT, ADD)
@@ -124,22 +124,23 @@ def tile_picked_hash_lin_silu_sub_l_kernel(tc, xT, w, b, offs, out):
         for g in range(2):
             nc.gpsimd.tensor_tensor(parts[:, 0, g, :], *gather(0, g), ADD)
         middle = look_up("vector", 1, 6, 8)
-        nc.gpsimd.tensor_tensor(parts[:, 1, 0, :], *gather(1, 0), ADD)
-        last_terms = gather(1, 1)
-        nc.gpsimd.tensor_tensor(parts[:, 1, 1, :SHARE], last_terms[0][:, :SHARE], last_terms[1][:, :SHARE], ADD)
+        for g in range(2):
+            nc.gpsimd.tensor_tensor(parts[:, 1, g, :], *gather(1, g), ADD)
 
         first = look_up("scalar", 0, 3, 5)
         add_turned(first + head)
         add_turned(look_up("scalar", 0, 5, 8))
-        add_turned(look_up("scalar", 1, 0, 4))
+        add_turned(look_up("scalar", 1, 0, 3))
+        add_turned(look_up("scalar", 1, 3, 6))
         add_turned(middle)
         add_turned(look_up("scalar", 2, 0, 4))
-        add_turned(look_up("scalar", 1, 4, 6, even[1][:, :V]))
         add_turned(look_up("scalar", 2, 4, 6))
         add_turned(look_up("scalar", 2, 6, 8))
-        add_turned(look_up("scalar", 3, 3, 6))
-        add_turned(look_up("vector", 3, 0, 3))
-        add_turned(sorted(look_up("scalar", 3, 6, 8), key=lambda block: block[1]))
+        add_turned(look_up("scalar", 3, 4, 6))
+        add_turned(look_up("vector", 3, 0, 2))
+        add_turned(look_up("scalar", 3, 6, 8))
+        add_turned(look_up("vector", 3, 2, 4))
+
         turned = [
             keep.tile([P, 2, 2 * P], BF16, name="turned0", tag="picked26", align_bytes=64),
             keep.tile([P, 2, 2 * P], BF16, name="turned1", align_bytes=64),
@@ -165,7 +166,7 @@ def tile_picked_hash_lin_silu_sub_l_kernel(tc, xT, w, b, offs, out):
         w_scales = keep.tile([P, PASSES * N], U8, name="w_scales", align_bytes=64)
         x_scales = keep.tile([P, PASSES * V], U8, name="x_scales", align_bytes=64)
         w_codes = [
-            keep.tile([P, N], U32, name="w_codes0", tag="two01", align_bytes=64),
+            keep.tile([P, N], U32, name="w_codes0", tag="two10", align_bytes=64),
             keep.tile([P, N], U32, name="w_codes1", tag="w_codes1", align_bytes=64),
         ]
         x_codes = [
@@ -187,9 +188,8 @@ def tile_picked_hash_lin_silu_sub_l_kernel(tc, xT, w, b, offs, out):
                 in_=grouped[c][:, h * PACK * HALF : (h + 1) * PACK * HALF],
             )
 
-        w_grouped.extend([keep.tile([P, N, PACK], BF16, name="w_grouped1", tag="two10", align_bytes=64)])
+        w_grouped.extend([keep.tile([P, N, PACK], BF16, name="w_grouped1", tag="two11", align_bytes=64)])
         nc.vector.tensor_copy(w_grouped[1][:], w_raw[1][:].rearrange("p j n -> p n j"))
-        nc.vector.tensor_tensor(parts[:, 1, 1, SHARE:], last_terms[0][:, SHARE:], last_terms[1][:, SHARE:], ADD)
         quantize_w(0)
         both = parts[:].rearrange("p u g (v e) -> p g v u e", e=2)
         for h in range(2):

@@ -136,28 +136,31 @@ def tile_picked_hash_lin_silu_sub_l_kernel(tc, xT, w, b, offs, out):
         add_turned(look_up("scalar", 2, 0, 4))
         add_turned(look_up("scalar", 2, 4, 6))
         add_turned(look_up("scalar", 2, 6, 8))
-        add_turned(look_up("scalar", 3, 4, 6))
-        add_turned(look_up("vector", 3, 0, 2))
-        add_turned(look_up("scalar", 3, 6, 8))
-        add_turned(look_up("vector", 3, 2, 4))
+        add_turned(look_up("scalar", 3, 3, 5)[::-1])
+        add_turned(look_up("scalar", 3, 5, 7)[::-1])
+        late = look_up("vector", 3, 0, 3)
+        add_turned(late[0::2] + late[1::2])
+        add_turned(look_up("scalar", 3, 7, 8))
 
         turned = [
-            keep.tile([P, 2, 2 * P], BF16, name="turned0", tag="picked26", align_bytes=64),
+            keep.tile([P, 2, 2 * P], BF16, name="turned0", tag="two01", align_bytes=64),
             keep.tile([P, 2, 2 * P], BF16, name="turned1", align_bytes=64),
         ]
-
-        nc.scalar.copy(
+        nc.vector.tensor_copy(
             turned[0][:].rearrange("v h (p e) -> v h p e", e=2), early_sum[:].rearrange("v h e p -> v h p e")
         )
+        w_grouped.extend([keep.tile([P, N, PACK], BF16, name="w_grouped1", tag="picked33", align_bytes=64)])
+        nc.scalar.copy(w_grouped[1][:], w_raw[1][:].rearrange("p j n -> p n j"))
+        backs = [psum.tile([P, 2, HALF], F32, name=f"back{h}", tag=f"last{h}") for h in range(2)]
+        for h in range(2):
+            nc.tensor.transpose(backs[h][:, 0, :], turned[0][:, h, :].bitcast(F32), identity[:])
         for h in range(2):
             nc.scalar.copy(
                 turned[1][:, h].rearrange("v (p e) -> v p e", e=2), late_sums[h][:].rearrange("v e p -> v p e")
             )
-        backs = [psum.tile([P, 2, HALF], F32, name=f"back{h}", tag=f"last{h}") for h in range(2)]
+            nc.tensor.transpose(backs[h][:, 1, :], turned[1][:, h, :].bitcast(F32), identity[:])
         grouped = [keep.tile([P, PACK * V], BF16, name=f"grouped{c}", align_bytes=64) for c in range(PASSES)]
         for h in range(2):
-            for u in (1, 0):
-                nc.tensor.transpose(backs[h][:, u, :], turned[u][:, h, :].bitcast(F32), identity[:])
             nc.scalar.copy(
                 grouped[0][:, h * PACK * HALF : (h + 1) * PACK * HALF].bitcast(F32).rearrange("p (v u) -> p v u", u=2),
                 backs[h][:].rearrange("p u v -> p v u"),
@@ -167,7 +170,7 @@ def tile_picked_hash_lin_silu_sub_l_kernel(tc, xT, w, b, offs, out):
         x_scales = keep.tile([P, PASSES * V], U8, name="x_scales", align_bytes=64)
         w_codes = [
             keep.tile([P, N], U32, name="w_codes0", tag="two10", align_bytes=64),
-            keep.tile([P, N], U32, name="w_codes1", tag="w_codes1", align_bytes=64),
+            keep.tile([P, N], U32, name="w_codes1", tag="two11", align_bytes=64),
         ]
         x_codes = [
             keep.tile([P, V], U32, name="x_codes0", tag="parts", align_bytes=64),
@@ -188,8 +191,6 @@ def tile_picked_hash_lin_silu_sub_l_kernel(tc, xT, w, b, offs, out):
                 in_=grouped[c][:, h * PACK * HALF : (h + 1) * PACK * HALF],
             )
 
-        w_grouped.extend([keep.tile([P, N, PACK], BF16, name="w_grouped1", tag="two11", align_bytes=64)])
-        nc.vector.tensor_copy(w_grouped[1][:], w_raw[1][:].rearrange("p j n -> p n j"))
         quantize_w(0)
         both = parts[:].rearrange("p u g (v e) -> p g v u e", e=2)
         for h in range(2):

@@ -46,17 +46,16 @@ def tile_picked_hash_lin_silu_sub_l_kernel(tc, xT, w, b, offs, out):
         def load_single(j):
             nc.sync.dma_start(single[j][:, :T], x_rows[0][:, j])
 
-        def load_pair(u, lo, hi):
+        def load_pair(u):
             rows = pair[u][:, : 2 * T].rearrange("p (e t) -> p e t", e=2)
-            nc.sync.dma_start(rows[:, :, lo:hi], x_rows[1][:, 2 * u : 2 * u + 2, lo:hi])
+            nc.sync.dma_start(rows, x_rows[1][:, 2 * u : 2 * u + 2])
 
         nc.sync.dma_start(offsets[:], offs)
         load_single(0)
-        for lo, hi in HALVES:
-            load_pair(0, lo, hi)
+        load_pair(0)
         load_single(1)
         nc.sync.dma_start(w_raw[0][:], w_rows[0])
-        load_pair(1, 0, T)
+        load_pair(1)
         load_single(2)
         load_single(3)
         nc.sync.dma_start(w_raw[1][:], w_rows[1])
@@ -115,11 +114,10 @@ def tile_picked_hash_lin_silu_sub_l_kernel(tc, xT, w, b, offs, out):
             return two[:, :V].bitcast(BF16), two[:, V:].bitcast(BF16)
 
         head = look_up("vector", 0, 0, 3)
-        for lo, hi in HALVES:
-            pack(nc.vector.tensor_copy, 0, lo, hi)
+        pack(nc.vector.tensor_copy, 0, 0, T)
         pack(nc.scalar.copy, 1, 0, T)
-        w_grouped = [keep.tile([P, N, PACK], BF16, name="w_grouped0", align_bytes=64)]
-        nc.gpsimd.tensor_scalar(w_grouped[0][:], w_raw[0][:].rearrange("p j n -> p n j"), 1.0, 0.0, MULT, ADD)
+        w_grouped = keep.tile([P, PASSES, N, PACK], BF16, name="w_grouped", align_bytes=64)
+        nc.gpsimd.tensor_scalar(w_grouped[:, 0], w_raw[0][:].rearrange("p j n -> p n j"), 1.0, 0.0, MULT, ADD)
         parts = keep.tile([P, 2, 2, 2 * V], F32, name="parts", tag="parts", align_bytes=64)
         for g in range(2):
             nc.gpsimd.tensor_tensor(parts[:, 0, g, :], *gather(0, g), ADD)
@@ -136,11 +134,10 @@ def tile_picked_hash_lin_silu_sub_l_kernel(tc, xT, w, b, offs, out):
         add_turned(look_up("scalar", 2, 0, 4))
         add_turned(look_up("scalar", 2, 4, 6))
         add_turned(look_up("scalar", 2, 6, 8))
-        add_turned(look_up("scalar", 3, 3, 5)[::-1])
-        add_turned(look_up("scalar", 3, 5, 7)[::-1])
-        late = look_up("vector", 3, 0, 3)
-        add_turned(late[0::2] + late[1::2])
-        add_turned(look_up("scalar", 3, 7, 8))
+        add_turned(look_up("scalar", 3, 4, 6))
+        add_turned(look_up("vector", 3, 0, 2))
+        add_turned(look_up("scalar", 3, 6, 8))
+        add_turned(look_up("vector", 3, 2, 4))
 
         turned = [
             keep.tile([P, 2, 2 * P], BF16, name="turned0", tag="two01", align_bytes=64),
@@ -149,8 +146,7 @@ def tile_picked_hash_lin_silu_sub_l_kernel(tc, xT, w, b, offs, out):
         nc.vector.tensor_copy(
             turned[0][:].rearrange("v h (p e) -> v h p e", e=2), early_sum[:].rearrange("v h e p -> v h p e")
         )
-        w_grouped.extend([keep.tile([P, N, PACK], BF16, name="w_grouped1", tag="picked33", align_bytes=64)])
-        nc.scalar.copy(w_grouped[1][:], w_raw[1][:].rearrange("p j n -> p n j"))
+        nc.scalar.copy(w_grouped[:, 1], w_raw[1][:].rearrange("p j n -> p n j"))
         backs = [psum.tile([P, 2, HALF], F32, name=f"back{h}", tag=f"last{h}") for h in range(2)]
         for h in range(2):
             nc.tensor.transpose(backs[h][:, 0, :], turned[0][:, h, :].bitcast(F32), identity[:])
@@ -168,43 +164,27 @@ def tile_picked_hash_lin_silu_sub_l_kernel(tc, xT, w, b, offs, out):
 
         w_scales = keep.tile([P, PASSES * N], U8, name="w_scales", align_bytes=64)
         x_scales = keep.tile([P, PASSES * V], U8, name="x_scales", align_bytes=64)
-        w_codes = [
-            keep.tile([P, N], U32, name="w_codes0", tag="two10", align_bytes=64),
-            keep.tile([P, N], U32, name="w_codes1", tag="two11", align_bytes=64),
-        ]
+        w_codes = keep.tile([P, PASSES * N], U32, name="w_codes", tag="two11", align_bytes=64)
         x_codes = [
             keep.tile([P, V], U32, name="x_codes0", tag="parts", align_bytes=64),
             keep.tile([P, V], U32, name="x_codes1", align_bytes=64),
         ]
 
-        def quantize_w(c):
+        def quantize_x(c, lo, hi):
             nc.vector.quantize_mx(
-                out=w_codes[c][:].bitcast(FP8X4),
-                scales=w_scales[:, c * N : (c + 1) * N],
-                in_=w_grouped[c][:].rearrange("p n j -> p (n j)"),
+                out=x_codes[c][:, lo:hi].bitcast(FP8X4),
+                scales=x_scales[:, c * V + lo : c * V + hi],
+                in_=grouped[c][:, PACK * lo : PACK * hi],
             )
 
-        def quantize_x(c, h):
-            nc.vector.quantize_mx(
-                out=x_codes[c][:, h * HALF : (h + 1) * HALF].bitcast(FP8X4),
-                scales=x_scales[:, c * V + h * HALF : c * V + (h + 1) * HALF],
-                in_=grouped[c][:, h * PACK * HALF : (h + 1) * PACK * HALF],
-            )
-
-        quantize_w(0)
         both = parts[:].rearrange("p u g (v e) -> p g v u e", e=2)
+        nc.vector.tensor_tensor(grouped[1][:].rearrange("p (v u e) -> p v u e", u=2, e=2), both[:, 0], both[:, 1], ADD)
+        nc.vector.quantize_mx(
+            out=w_codes[:].bitcast(FP8X4), scales=w_scales[:], in_=w_grouped[:].rearrange("p c n j -> p (c n j)")
+        )
+        quantize_x(1, 0, V)
         for h in range(2):
-            ids = slice(h * HALF, (h + 1) * HALF)
-            nc.vector.tensor_tensor(
-                grouped[1][:].rearrange("p (v u e) -> p v u e", u=2, e=2)[:, ids],
-                both[:, 0, ids],
-                both[:, 1, ids],
-                ADD,
-            )
-        quantize_w(1)
-        for h in range(2):
-            quantize_x(1, h)
-            quantize_x(0, h)
+            quantize_x(0, h * HALF, (h + 1) * HALF)
 
         acc = [psum.tile([P, HALF], F32, name=f"acc{h}", tag=f"last{h}") for h in range(2)]
         result = [keep.tile([P, HALF], F32, name=f"result{h}") for h in range(2)]
@@ -212,7 +192,7 @@ def tile_picked_hash_lin_silu_sub_l_kernel(tc, xT, w, b, offs, out):
             for c in (1, 0):
                 nc.tensor.matmul_mx(
                     out=acc[h][:],
-                    lhsT=w_codes[c][:].bitcast(FP8X4),
+                    lhsT=w_codes[:, c * N : (c + 1) * N].bitcast(FP8X4),
                     lhsT_scale=w_scales[:, c * N : (c + 1) * N],
                     rhs=x_codes[c][:, h * HALF : (h + 1) * HALF].bitcast(FP8X4),
                     rhs_scale=x_scales[:, c * V + h * HALF : c * V + (h + 1) * HALF],

@@ -21,10 +21,14 @@ P = 128
 PACK = 4
 PASSES = K // (P * PACK)
 HALF = V // 2
-COLS = V // 16
-HALVES = ((0, T // 2), (T // 2, T))
-WINDOW = 704
-SPARE = 16
+BLOCKS = D * V // HALF
+BLOCK_COLS = HALF // 16
+
+HEAD, MIDDLE, LATE = 3, 2, 4
+RUN = 2
+
+PAIR_WINDOW = 704
+ROW_WINDOWS = ((BLOCKS - HEAD) * HALF + 16, (BLOCKS - MIDDLE) * HALF + 16, 2 * RUN * HALF + 16, T)
 
 
 def tile_picked_hash_lin_silu_sub_l_kernel(tc, xT, w, b, offs, out):
@@ -33,12 +37,11 @@ def tile_picked_hash_lin_silu_sub_l_kernel(tc, xT, w, b, offs, out):
         keep = ctx.enter_context(tc.tile_pool(name="keep", bufs=1))
         psum = ctx.enter_context(tc.psum_pool(name="psum", bufs=1))
 
-        offsets = keep.tile([P, D * COLS], U16, name="offsets")
+        offsets = keep.tile([P, BLOCKS * BLOCK_COLS], U16, name="offsets")
         x_rows = xT.rearrange("(c p j) t -> c p j t", c=PASSES, p=P, j=PACK)
         w_rows = w.rearrange("(c p j) n -> c p j n", c=PASSES, p=P, j=PACK)
-        single = [keep.tile([P, T + SPARE], F32, name=f"single{j}", align_bytes=64) for j in range(PACK)]
-        pair = [keep.tile([P, T + WINDOW], F32, name=f"pair{u}", align_bytes=64) for u in range(2)]
-        even = [pair[u][:, :T] for u in range(2)]
+        single = [keep.tile([P, ROW_WINDOWS[j]], F32, name=f"single{j}", align_bytes=64) for j in range(PACK)]
+        pair = [keep.tile([P, T + PAIR_WINDOW], F32, name=f"pair{u}", align_bytes=64) for u in range(2)]
         table = [pair[u][:, T:] for u in range(2)]
         w_raw = [keep.tile([P, PACK, N], F32, name=f"w_raw{c}") for c in range(PASSES)]
         bias = keep.tile([P, 1], F32, name="bias")
@@ -61,15 +64,16 @@ def tile_picked_hash_lin_silu_sub_l_kernel(tc, xT, w, b, offs, out):
         nc.sync.dma_start(w_raw[1][:], w_rows[1])
         nc.sync.dma_start(bias[:], b)
 
-        warm = keep.tile([P, 1], F32, name="warm")
-        warm_out = keep.tile([P, 1], F32, name="warm_out")
-        nc.vector.memset(warm[:], 0.0)
-        nc.scalar.activation(warm_out[:], warm[:], SILU)
+        table_in = keep.tile([P, 1], F32, name="table_in")
+        table_out = keep.tile([P, 1], F32, name="table_out")
+        nc.vector.memset(table_in[:], 0.0)
+        nc.scalar.activation(table_out[:], table_in[:], SILU)
 
         identity = keep.tile([P, P], F32, name="identity")
         make_identity(nc, identity[:])
         for j in range(PACK):
-            nc.vector.memset(single[j][:, T:], 0.0)
+            if ROW_WINDOWS[j] > T:
+                nc.vector.memset(single[j][:, T:], 0.0)
         for u in range(2):
             nc.vector.memset(table[u][:, T:], 0.0)
 
@@ -77,77 +81,70 @@ def tile_picked_hash_lin_silu_sub_l_kernel(tc, xT, w, b, offs, out):
         late_sums = [psum.tile([P, 2, P], F32, name=f"late_sum{h}") for h in range(2)]
         sums = [[early_sum[:, h] for h in range(2)], [late_sums[h][:] for h in range(2)]]
 
-        def look_up(engine, j, b0, b1):
-            picked = keep.tile([P, (b1 - b0) * HALF], F32, name=f"picked{j}{b0}", align_bytes=64)[:]
-            looked_up = single[j][:].indirect(offsets[:, b0 * COLS // 2 : b1 * COLS // 2])
-            if engine == "vector":
-                nc.vector.tensor_copy(picked, looked_up)
+        def look_up(on_vector, j, first, end):
+            picked = keep.tile([P, (end - first) * HALF], F32, name=f"picked{j}{first}", align_bytes=64)
+            looked_up = single[j][:].indirect(offsets[:, first * BLOCK_COLS : end * BLOCK_COLS])
+            if on_vector:
+                nc.vector.tensor_copy(picked[:], looked_up)
             else:
-                nc.scalar.activation(picked, looked_up, COPY)
-            return [(j, block % 2, picked[:, (block - b0) * HALF : (block - b0 + 1) * HALF]) for block in range(b0, b1)]
+                nc.scalar.activation(picked[:], looked_up, COPY)
+            return [(j, i % 2, picked[:, (i - first) * HALF : (i - first + 1) * HALF]) for i in range(first, end)]
 
-        done = {}
+        added = {}
 
         def add_turned(blocks):
-            for j, h, block in blocks:
-                bank = (0, 0) if j < 2 else (1, h)
-                total = 4 * D if j < 2 else 2 * D
-                count = done.get(bank, 0)
+            for j, h, values in blocks:
+                bank, total = ("early", 2 * BLOCKS) if j < 2 else (h, BLOCKS)
+                count = added.get(bank, 0)
                 nc.tensor.matmul(
                     sums[j // 2][h][:, j % 2, :],
-                    lhsT=block,
+                    lhsT=values,
                     rhs=identity[:],
                     start=(count == 0),
                     stop=(count == total - 1),
                     is_transpose=True,
                 )
-                done.update({bank: count + 1})
+                added.update({bank: count + 1})
 
-        def pack(copy, u, lo, hi):
-            low = table[u][:, lo:hi].bitcast(BF16).rearrange("p (t h) -> p t h", h=2)[:, :, 0]
-            copy(low, even[u][:, lo:hi].bitcast(BF16).rearrange("p (t h) -> p t h", h=2)[:, :, 1])
+        def pack(copy, u):
+            halves = pair[u][:, : 2 * T].bitcast(BF16).rearrange("p (e t s) -> p e t s", e=2, s=2)
+            copy(halves[:, 1, :, 0], halves[:, 0, :, 1])
 
-        def gather(u, g):
+        def gather_words(u, g):
             two = keep.tile([P, 2 * V], U32, name=f"two{u}{g}", align_bytes=64)
-            window = table[u].bitcast(U32)
-            nc.vector.tensor_copy(two[:], window.indirect(offsets[:, 2 * g * COLS : 2 * (g + 1) * COLS]))
+            entries = offsets[:, 4 * g * BLOCK_COLS : 4 * (g + 1) * BLOCK_COLS]
+            nc.vector.tensor_copy(two[:], table[u].bitcast(U32).indirect(entries))
             return two[:, :V].bitcast(BF16), two[:, V:].bitcast(BF16)
 
-        head = look_up("vector", 0, 0, 3)
-        pack(nc.vector.tensor_copy, 0, 0, T)
-        pack(nc.scalar.copy, 1, 0, T)
+        head = look_up(True, 0, 0, HEAD)
+        pack(nc.vector.tensor_copy, 0)
+        pack(nc.scalar.copy, 1)
         w_grouped = keep.tile([P, PASSES, N, PACK], BF16, name="w_grouped", align_bytes=64)
         nc.gpsimd.tensor_scalar(w_grouped[:, 0], w_raw[0][:].rearrange("p j n -> p n j"), 1.0, 0.0, MULT, ADD)
-        parts = keep.tile([P, 2, 2, 2 * V], F32, name="parts", tag="parts", align_bytes=64)
+        inner = keep.tile([P, 2, 2, 2 * V], F32, name="inner", align_bytes=64)
         for g in range(2):
-            nc.gpsimd.tensor_tensor(parts[:, 0, g, :], *gather(0, g), ADD)
-        middle = look_up("vector", 1, 6, 8)
+            nc.gpsimd.tensor_tensor(inner[:, 0, g, :], *gather_words(0, g), ADD)
+        middle = look_up(True, 1, BLOCKS - MIDDLE, BLOCKS)
         for g in range(2):
-            nc.gpsimd.tensor_tensor(parts[:, 1, g, :], *gather(1, g), ADD)
+            nc.gpsimd.tensor_tensor(inner[:, 1, g, :], *gather_words(1, g), ADD)
 
-        first = look_up("scalar", 0, 3, 5)
-        add_turned(first + head)
-        add_turned(look_up("scalar", 0, 5, 8))
-        add_turned(look_up("scalar", 1, 0, 3))
-        add_turned(look_up("scalar", 1, 3, 6))
+        add_turned(head)
+        add_turned(look_up(False, 0, HEAD, BLOCKS))
+        add_turned(look_up(False, 1, 0, BLOCKS - MIDDLE))
         add_turned(middle)
-        add_turned(look_up("scalar", 2, 0, 4))
-        add_turned(look_up("scalar", 2, 4, 6))
-        add_turned(look_up("scalar", 2, 6, 8))
-        add_turned(look_up("scalar", 3, 4, 6))
-        add_turned(look_up("vector", 3, 0, 2))
-        add_turned(look_up("scalar", 3, 6, 8))
-        add_turned(look_up("vector", 3, 2, 4))
+        add_turned(look_up(False, 2, 0, 2 * RUN))
+        for first in range(2 * RUN, BLOCKS, RUN):
+            add_turned(look_up(False, 2, first, first + RUN))
+        for first in range(0, LATE, RUN):
+            add_turned(look_up(False, 3, LATE + first, LATE + first + RUN))
+            add_turned(look_up(True, 3, first, first + RUN))
 
-        turned = [
-            keep.tile([P, 2, 2 * P], BF16, name="turned0", tag="two01", align_bytes=64),
-            keep.tile([P, 2, 2 * P], BF16, name="turned1", align_bytes=64),
-        ]
-        nc.vector.tensor_copy(
+        turned = [keep.tile([P, 2, 2 * P], BF16, name=f"turned{u}", align_bytes=64) for u in range(2)]
+        nc.scalar.copy(
             turned[0][:].rearrange("v h (p e) -> v h p e", e=2), early_sum[:].rearrange("v h e p -> v h p e")
         )
         nc.scalar.copy(w_grouped[:, 1], w_raw[1][:].rearrange("p j n -> p n j"))
-        backs = [psum.tile([P, 2, HALF], F32, name=f"back{h}", tag=f"last{h}") for h in range(2)]
+        backs = [psum.tile([P, 2, HALF], F32, name=f"back{h}") for h in range(2)]
         for h in range(2):
             nc.tensor.transpose(backs[h][:, 0, :], turned[0][:, h, :].bitcast(F32), identity[:])
         for h in range(2):
@@ -166,18 +163,18 @@ def tile_picked_hash_lin_silu_sub_l_kernel(tc, xT, w, b, offs, out):
         x_scales = keep.tile([P, PASSES * V], U8, name="x_scales", align_bytes=64)
         w_codes = keep.tile([P, PASSES * N], U32, name="w_codes", tag="two11", align_bytes=64)
         x_codes = [
-            keep.tile([P, V], U32, name="x_codes0", tag="parts", align_bytes=64),
+            keep.tile([P, V], U32, name="x_codes0", tag="inner", align_bytes=64),
             keep.tile([P, V], U32, name="x_codes1", align_bytes=64),
         ]
 
-        def quantize_x(c, lo, hi):
+        def quantize_x(c, first, end):
             nc.vector.quantize_mx(
-                out=x_codes[c][:, lo:hi].bitcast(FP8X4),
-                scales=x_scales[:, c * V + lo : c * V + hi],
-                in_=grouped[c][:, PACK * lo : PACK * hi],
+                out=x_codes[c][:, first:end].bitcast(FP8X4),
+                scales=x_scales[:, c * V + first : c * V + end],
+                in_=grouped[c][:, PACK * first : PACK * end],
             )
 
-        both = parts[:].rearrange("p u g (v e) -> p g v u e", e=2)
+        both = inner[:].rearrange("p u g (v e) -> p g v u e", e=2)
         nc.vector.tensor_tensor(grouped[1][:].rearrange("p (v u e) -> p v u e", u=2, e=2), both[:, 0], both[:, 1], ADD)
         nc.vector.quantize_mx(
             out=w_codes[:].bitcast(FP8X4), scales=w_scales[:], in_=w_grouped[:].rearrange("p c n j -> p (c n j)")
@@ -186,12 +183,11 @@ def tile_picked_hash_lin_silu_sub_l_kernel(tc, xT, w, b, offs, out):
         for h in range(2):
             quantize_x(0, h * HALF, (h + 1) * HALF)
 
-        acc = [psum.tile([P, HALF], F32, name=f"acc{h}", tag=f"last{h}") for h in range(2)]
-        result = [keep.tile([P, HALF], F32, name=f"result{h}") for h in range(2)]
-        for h in range(2):
+        for h, bank in enumerate(("back0", "late_sum1")):
+            acc = psum.tile([P, HALF], F32, name=f"acc{h}", tag=bank)
             for c in (1, 0):
                 nc.tensor.matmul_mx(
-                    out=acc[h][:],
+                    out=acc[:],
                     lhsT=w_codes[:, c * N : (c + 1) * N].bitcast(FP8X4),
                     lhsT_scale=w_scales[:, c * N : (c + 1) * N],
                     rhs=x_codes[c][:, h * HALF : (h + 1) * HALF].bitcast(FP8X4),
@@ -199,5 +195,6 @@ def tile_picked_hash_lin_silu_sub_l_kernel(tc, xT, w, b, offs, out):
                     start=(c == 1),
                     stop=(c == 0),
                 )
-            nc.scalar.activation(result[h][:], acc[h][:], SILU, bias=bias[:])
-            nc.sync.dma_start(out[:, h * HALF : (h + 1) * HALF], result[h][:])
+            result = keep.tile([P, HALF], F32, name=f"result{h}")
+            nc.scalar.activation(result[:], acc[:], SILU, bias=bias[:])
+            nc.sync.dma_start(out[:, h * HALF : (h + 1) * HALF], result[:])

@@ -24,7 +24,7 @@ HALF = V // 2
 BLOCKS = D * V // HALF
 BLOCK_COLS = HALF // 16
 
-HEAD, MIDDLE, LATE = 3, 2, 4
+HEAD, MIDDLE, LATE = 3, 2, 3
 RUN = 2
 
 PAIR_WINDOW = 704
@@ -135,12 +135,16 @@ def tile_picked_hash_lin_silu_sub_l_kernel(tc, xT, w, b, offs, out):
         add_turned(look_up(False, 2, 0, 2 * RUN))
         for first in range(2 * RUN, BLOCKS, RUN):
             add_turned(look_up(False, 2, first, first + RUN))
-        for first in range(0, LATE, RUN):
-            add_turned(look_up(False, 3, LATE + first, LATE + first + RUN))
-            add_turned(look_up(True, 3, first, first + RUN))
+        for first in range(0, BLOCKS - LATE, RUN):
+            add_turned(look_up(False, 3, LATE + first, min(LATE + first + RUN, BLOCKS)))
+            if first < LATE:
+                add_turned(look_up(True, 3, first, min(first + RUN, LATE)))
 
-        turned = [keep.tile([P, 2, 2 * P], BF16, name=f"turned{u}", align_bytes=64) for u in range(2)]
-        nc.scalar.copy(
+        turned = [
+            keep.tile([P, 2, 2 * P], BF16, name="turned0", tag="two01", align_bytes=64),
+            keep.tile([P, 2, 2 * P], BF16, name="turned1", align_bytes=64),
+        ]
+        nc.vector.tensor_copy(
             turned[0][:].rearrange("v h (p e) -> v h p e", e=2), early_sum[:].rearrange("v h e p -> v h p e")
         )
         nc.scalar.copy(w_grouped[:, 1], w_raw[1][:].rearrange("p j n -> p n j"))

@@ -53,8 +53,8 @@ def tile_picked_hash_lin_silu_sub_l_kernel(tc, xT, w, b, offs, out):
             rows = pair[u][:, : 2 * T].rearrange("p (e t) -> p e t", e=2)
             nc.sync.dma_start(rows, x_rows[1][:, 2 * u : 2 * u + 2])
 
-        nc.sync.dma_start(offsets[:], offs)
         load_single(0)
+        nc.sync.dma_start(offsets[:], offs)
         load_pair(0)
         load_single(1)
         nc.sync.dma_start(w_raw[0][:], w_rows[0])

@@ -165,7 +165,18 @@ def tile_picked_hash_lin_silu_sub_l_kernel(tc, xT, w, b, offs, out):
 
         w_scales = keep.tile([P, PASSES * N], U8, name="w_scales", align_bytes=64)
         x_scales = keep.tile([P, PASSES * V], U8, name="x_scales", align_bytes=64)
-        w_codes = keep.tile([P, PASSES * N], U32, name="w_codes", tag="two11", align_bytes=64)
+        w_codes = [
+            keep.tile([P, N], U32, name="w_codes0", tag=f"picked1{BLOCKS - MIDDLE}", align_bytes=64),
+            keep.tile([P, N], U32, name="w_codes1", tag="two11", align_bytes=64),
+        ]
+
+        def quantize_w(c):
+            nc.vector.quantize_mx(
+                out=w_codes[c][:].bitcast(FP8X4),
+                scales=w_scales[:, c * N : (c + 1) * N],
+                in_=w_grouped[:, c].rearrange("p n j -> p (n j)"),
+            )
+
         x_codes = [
             keep.tile([P, V], U32, name="x_codes0", tag="inner", align_bytes=64),
             keep.tile([P, V], U32, name="x_codes1", align_bytes=64),
@@ -178,27 +189,27 @@ def tile_picked_hash_lin_silu_sub_l_kernel(tc, xT, w, b, offs, out):
                 in_=grouped[c][:, PACK * first : PACK * end],
             )
 
+        quantize_w(0)
         both = inner[:].rearrange("p u g (v e) -> p g v u e", e=2)
         nc.vector.tensor_tensor(grouped[1][:].rearrange("p (v u e) -> p v u e", u=2, e=2), both[:, 0], both[:, 1], ADD)
-        nc.vector.quantize_mx(
-            out=w_codes[:].bitcast(FP8X4), scales=w_scales[:], in_=w_grouped[:].rearrange("p c n j -> p (c n j)")
-        )
-        quantize_x(1, 0, V)
-        for h in range(2):
-            quantize_x(0, h * HALF, (h + 1) * HALF)
+        quantize_w(1)
+        for c in (1, 0):
+            for h in range(2):
+                quantize_x(c, h * HALF, (h + 1) * HALF)
 
-        for h, bank in enumerate(("back0", "late_sum1")):
-            acc = psum.tile([P, HALF], F32, name=f"acc{h}", tag=bank)
-            for c in (1, 0):
+        accs = [psum.tile([P, HALF], F32, name=f"acc{h}", tag=bank) for h, bank in enumerate(("back0", "late_sum1"))]
+        for c in (1, 0):
+            for h in range(2):
                 nc.tensor.matmul_mx(
-                    out=acc[:],
-                    lhsT=w_codes[:, c * N : (c + 1) * N].bitcast(FP8X4),
+                    out=accs[h][:],
+                    lhsT=w_codes[c][:].bitcast(FP8X4),
                     lhsT_scale=w_scales[:, c * N : (c + 1) * N],
                     rhs=x_codes[c][:, h * HALF : (h + 1) * HALF].bitcast(FP8X4),
                     rhs_scale=x_scales[:, c * V + h * HALF : c * V + (h + 1) * HALF],
                     start=(c == 1),
                     stop=(c == 0),
                 )
+        for h in range(2):
             result = keep.tile([P, HALF], F32, name=f"result{h}")
-            nc.scalar.activation(result[:], acc[:], SILU, bias=bias[:])
+            nc.scalar.activation(result[:], accs[h][:], SILU, bias=bias[:])
             nc.sync.dma_start(out[:, h * HALF : (h + 1) * HALF], result[:])

@@ -57,11 +57,11 @@ def tile_picked_hash_lin_silu_sub_l_kernel(tc, xT, w, b, offs, out):
         nc.sync.dma_start(offsets[:], offs)
         load_pair(0)
         load_single(1)
-        nc.sync.dma_start(w_raw[0][:], w_rows[0])
+        nc.sync.dma_start(w_raw[1][:], w_rows[1])
         load_pair(1)
         load_single(2)
         load_single(3)
-        nc.sync.dma_start(w_raw[1][:], w_rows[1])
+        nc.sync.dma_start(w_raw[0][:], w_rows[0])
         nc.sync.dma_start(bias[:], b)
 
         table_in = keep.tile([P, 1], F32, name="table_in")
@@ -81,13 +81,14 @@ def tile_picked_hash_lin_silu_sub_l_kernel(tc, xT, w, b, offs, out):
         late_sums = [psum.tile([P, 2, P], F32, name=f"late_sum{h}") for h in range(2)]
         sums = [[early_sum[:, h] for h in range(2)], [late_sums[h][:] for h in range(2)]]
 
-        def look_up(on_vector, j, first, end):
-            picked = keep.tile([P, (end - first) * HALF], F32, name=f"picked{j}{first}", align_bytes=64)
+        def look_up(on_vector, j, first, end, picked=None):
+            if picked is None:
+                picked = keep.tile([P, (end - first) * HALF], F32, name=f"picked{j}{first}", align_bytes=64)[:]
             looked_up = single[j][:].indirect(offsets[:, first * BLOCK_COLS : end * BLOCK_COLS])
             if on_vector:
-                nc.vector.tensor_copy(picked[:], looked_up)
+                nc.vector.tensor_copy(picked, looked_up)
             else:
-                nc.scalar.activation(picked[:], looked_up, COPY)
+                nc.scalar.activation(picked, looked_up, COPY)
             return [(j, i % 2, picked[:, (i - first) * HALF : (i - first + 1) * HALF]) for i in range(first, end)]
 
         added = {}
@@ -119,8 +120,9 @@ def tile_picked_hash_lin_silu_sub_l_kernel(tc, xT, w, b, offs, out):
         head = look_up(True, 0, 0, HEAD)
         pack(nc.vector.tensor_copy, 0)
         pack(nc.scalar.copy, 1)
-        w_grouped = keep.tile([P, PASSES, N, PACK], BF16, name="w_grouped", align_bytes=64)
-        nc.gpsimd.tensor_scalar(w_grouped[:, 0], w_raw[0][:].rearrange("p j n -> p n j"), 1.0, 0.0, MULT, ADD)
+        w_flat = keep.tile([P, PASSES * N * PACK], BF16, name="w_flat", align_bytes=64)
+        w_grouped = w_flat[:].rearrange("p (c n j) -> p c n j", c=PASSES, j=PACK)
+        nc.gpsimd.tensor_scalar(w_grouped[:, 1], w_raw[1][:].rearrange("p j n -> p n j"), 1.0, 0.0, MULT, ADD)
         inner = keep.tile([P, 2, 2, 2 * V], F32, name="inner", align_bytes=64)
         for g in range(2):
             nc.gpsimd.tensor_tensor(inner[:, 0, g, :], *gather_words(0, g), ADD)
@@ -135,10 +137,11 @@ def tile_picked_hash_lin_silu_sub_l_kernel(tc, xT, w, b, offs, out):
         add_turned(look_up(False, 2, 0, 2 * RUN))
         for first in range(2 * RUN, BLOCKS, RUN):
             add_turned(look_up(False, 2, first, first + RUN))
-        for first in range(0, BLOCKS - LATE, RUN):
-            add_turned(look_up(False, 3, LATE + first, min(LATE + first + RUN, BLOCKS)))
-            if first < LATE:
-                add_turned(look_up(True, 3, first, min(first + RUN, LATE)))
+        add_turned(look_up(False, 3, LATE, LATE + RUN))
+        add_turned(look_up(True, 3, 0, RUN))
+        second, first = look_up(False, 3, LATE + RUN, BLOCKS - 1)
+        add_turned([first] + look_up(True, 3, RUN, LATE) + [second])
+        add_turned(look_up(False, 3, BLOCKS - 1, BLOCKS, w_flat[:, N * PACK - 2 * HALF : N * PACK].bitcast(F32)))
 
         turned = [
             keep.tile([P, 2, 2 * P], BF16, name="turned0", tag="two01", align_bytes=64),
@@ -147,7 +150,8 @@ def tile_picked_hash_lin_silu_sub_l_kernel(tc, xT, w, b, offs, out):
         nc.vector.tensor_copy(
             turned[0][:].rearrange("v h (p e) -> v h p e", e=2), early_sum[:].rearrange("v h e p -> v h p e")
         )
-        nc.scalar.copy(w_grouped[:, 1], w_raw[1][:].rearrange("p j n -> p n j"))
+        w_turned = w_raw[0][:].rearrange("p j n -> p n j")
+        nc.scalar.copy(w_grouped[:, 0, : N // 2], w_turned[:, : N // 2])
         backs = [psum.tile([P, 2, HALF], F32, name=f"back{h}") for h in range(2)]
         for h in range(2):
             nc.tensor.transpose(backs[h][:, 0, :], turned[0][:, h, :].bitcast(F32), identity[:])
@@ -156,6 +160,7 @@ def tile_picked_hash_lin_silu_sub_l_kernel(tc, xT, w, b, offs, out):
                 turned[1][:, h].rearrange("v (p e) -> v p e", e=2), late_sums[h][:].rearrange("v e p -> v p e")
             )
             nc.tensor.transpose(backs[h][:, 1, :], turned[1][:, h, :].bitcast(F32), identity[:])
+        nc.scalar.copy(w_grouped[:, 0, N // 2 :], w_turned[:, N // 2 :])
         grouped = [keep.tile([P, PACK * V], BF16, name=f"grouped{c}", align_bytes=64) for c in range(PASSES)]
         for h in range(2):
             nc.scalar.copy(
@@ -166,15 +171,15 @@ def tile_picked_hash_lin_silu_sub_l_kernel(tc, xT, w, b, offs, out):
         w_scales = keep.tile([P, PASSES * N], U8, name="w_scales", align_bytes=64)
         x_scales = keep.tile([P, PASSES * V], U8, name="x_scales", align_bytes=64)
         w_codes = [
-            keep.tile([P, N], U32, name="w_codes0", tag=f"picked1{BLOCKS - MIDDLE}", align_bytes=64),
-            keep.tile([P, N], U32, name="w_codes1", tag="two11", align_bytes=64),
+            keep.tile([P, N], U32, name="w_codes0", tag="two11", align_bytes=64),
+            keep.tile([P, N], U32, name="w_codes1", tag=f"picked1{BLOCKS - MIDDLE}", align_bytes=64),
         ]
 
         def quantize_w(c):
             nc.vector.quantize_mx(
                 out=w_codes[c][:].bitcast(FP8X4),
                 scales=w_scales[:, c * N : (c + 1) * N],
-                in_=w_grouped[:, c].rearrange("p n j -> p (n j)"),
+                in_=w_flat[:, c * N * PACK : (c + 1) * N * PACK],
             )
 
         x_codes = [
@@ -189,13 +194,17 @@ def tile_picked_hash_lin_silu_sub_l_kernel(tc, xT, w, b, offs, out):
                 in_=grouped[c][:, PACK * first : PACK * end],
             )
 
-        quantize_w(0)
-        both = inner[:].rearrange("p u g (v e) -> p g v u e", e=2)
-        nc.vector.tensor_tensor(grouped[1][:].rearrange("p (v u e) -> p v u e", u=2, e=2), both[:, 0], both[:, 1], ADD)
         quantize_w(1)
-        for c in (1, 0):
-            for h in range(2):
-                quantize_x(c, h * HALF, (h + 1) * HALF)
+        both = inner[:].rearrange("p u g (v e) -> p g v u e", e=2)
+        summed = grouped[1][:].rearrange("p (v u e) -> p v u e", u=2, e=2)
+        for h in range(2):
+            ids = slice(h * HALF, (h + 1) * HALF)
+            nc.vector.tensor_tensor(summed[:, ids], both[:, 0, ids], both[:, 1, ids], ADD)
+        for h in range(2):
+            quantize_x(1, h * HALF, (h + 1) * HALF)
+        quantize_w(0)
+        for h in range(2):
+            quantize_x(0, h * HALF, (h + 1) * HALF)
 
         accs = [psum.tile([P, HALF], F32, name=f"acc{h}", tag=bank) for h, bank in enumerate(("back0", "late_sum1"))]
         for c in (1, 0):

@@ -25,6 +25,7 @@ BLOCKS = D * V // HALF
 BLOCK_COLS = HALF // 16
 
 HEAD, MIDDLE, LATE = 3, 2, 3
+SHARE = 128
 RUN = 2
 
 PAIR_WINDOW = 704
@@ -123,24 +124,27 @@ def tile_picked_hash_lin_silu_sub_l_kernel(tc, xT, w, b, offs, out):
         w_flat = keep.tile([P, PASSES * N * PACK], BF16, name="w_flat", align_bytes=64)
         w_grouped = w_flat[:].rearrange("p (c n j) -> p c n j", c=PASSES, j=PACK)
         nc.gpsimd.tensor_scalar(w_grouped[:, 1], w_raw[1][:].rearrange("p j n -> p n j"), 1.0, 0.0, MULT, ADD)
-        inner = keep.tile([P, 2, 2, 2 * V], F32, name="inner", align_bytes=64)
+        sums_flat = keep.tile([P, 8 * V + MIDDLE * HALF - SHARE], F32, name="sums_flat", align_bytes=64)
+        inner = sums_flat[:, : 8 * V].rearrange("p (u g x) -> p u g x", u=2, g=2)
         for g in range(2):
             nc.gpsimd.tensor_tensor(inner[:, 0, g, :], *gather_words(0, g), ADD)
-        middle = look_up(True, 1, BLOCKS - MIDDLE, BLOCKS)
-        for g in range(2):
-            nc.gpsimd.tensor_tensor(inner[:, 1, g, :], *gather_words(1, g), ADD)
+        middle = look_up(True, 1, BLOCKS - MIDDLE, BLOCKS, sums_flat[:, 8 * V - SHARE :])
+        nc.gpsimd.tensor_tensor(inner[:, 1, 0, :], *gather_words(1, 0), ADD)
+        last_terms = gather_words(1, 1)
+        cut = 2 * V - SHARE
+        nc.gpsimd.tensor_tensor(inner[:, 1, 1, :cut], last_terms[0][:, :cut], last_terms[1][:, :cut], ADD)
 
         add_turned(head)
         add_turned(look_up(False, 0, HEAD, BLOCKS))
         add_turned(look_up(False, 1, 0, BLOCKS - MIDDLE))
-        add_turned(middle)
+        add_turned(middle[::-1])
         add_turned(look_up(False, 2, 0, 2 * RUN))
         for first in range(2 * RUN, BLOCKS, RUN):
             add_turned(look_up(False, 2, first, first + RUN))
-        add_turned(look_up(False, 3, LATE, LATE + RUN))
-        add_turned(look_up(True, 3, 0, RUN))
-        second, first = look_up(False, 3, LATE + RUN, BLOCKS - 1)
-        add_turned([first] + look_up(True, 3, RUN, LATE) + [second])
+        for i, block in enumerate((3, 4, 6, 5)):
+            add_turned(look_up(False, 3, block, block + 1))
+            if i < LATE:
+                add_turned(look_up(True, 3, i, i + 1))
         add_turned(look_up(False, 3, BLOCKS - 1, BLOCKS, w_flat[:, N * PACK - 2 * HALF : N * PACK].bitcast(F32)))
 
         turned = [
@@ -150,8 +154,9 @@ def tile_picked_hash_lin_silu_sub_l_kernel(tc, xT, w, b, offs, out):
         nc.vector.tensor_copy(
             turned[0][:].rearrange("v h (p e) -> v h p e", e=2), early_sum[:].rearrange("v h e p -> v h p e")
         )
-        w_turned = w_raw[0][:].rearrange("p j n -> p n j")
-        nc.scalar.copy(w_grouped[:, 0, : N // 2], w_turned[:, : N // 2])
+        w_in = w_raw[0][:].rearrange("p j (s c i) -> p s c j i", s=2, i=4)
+        w_out = w_grouped[:, 0].rearrange("p (s c i) j -> p s c j i", s=2, i=4)
+        nc.scalar.copy(w_out[:, 0], w_in[:, 0])
         backs = [psum.tile([P, 2, HALF], F32, name=f"back{h}") for h in range(2)]
         for h in range(2):
             nc.tensor.transpose(backs[h][:, 0, :], turned[0][:, h, :].bitcast(F32), identity[:])
@@ -160,7 +165,7 @@ def tile_picked_hash_lin_silu_sub_l_kernel(tc, xT, w, b, offs, out):
                 turned[1][:, h].rearrange("v (p e) -> v p e", e=2), late_sums[h][:].rearrange("v e p -> v p e")
             )
             nc.tensor.transpose(backs[h][:, 1, :], turned[1][:, h, :].bitcast(F32), identity[:])
-        nc.scalar.copy(w_grouped[:, 0, N // 2 :], w_turned[:, N // 2 :])
+        nc.scalar.copy(w_out[:, 1], w_in[:, 1])
         grouped = [keep.tile([P, PACK * V], BF16, name=f"grouped{c}", align_bytes=64) for c in range(PASSES)]
         for h in range(2):
             nc.scalar.copy(
@@ -171,19 +176,19 @@ def tile_picked_hash_lin_silu_sub_l_kernel(tc, xT, w, b, offs, out):
         w_scales = keep.tile([P, PASSES * N], U8, name="w_scales", align_bytes=64)
         x_scales = keep.tile([P, PASSES * V], U8, name="x_scales", align_bytes=64)
         w_codes = [
-            keep.tile([P, N], U32, name="w_codes0", tag="two11", align_bytes=64),
-            keep.tile([P, N], U32, name="w_codes1", tag=f"picked1{BLOCKS - MIDDLE}", align_bytes=64),
+            keep.tile([P, N], U32, name="w_codes0", align_bytes=64)[:],
+            keep.tile([P, N], U32, name="w_codes1", tag="two11", align_bytes=64)[:],
         ]
 
         def quantize_w(c):
             nc.vector.quantize_mx(
-                out=w_codes[c][:].bitcast(FP8X4),
+                out=w_codes[c].bitcast(FP8X4),
                 scales=w_scales[:, c * N : (c + 1) * N],
                 in_=w_flat[:, c * N * PACK : (c + 1) * N * PACK],
             )
 
         x_codes = [
-            keep.tile([P, V], U32, name="x_codes0", tag="inner", align_bytes=64),
+            keep.tile([P, V], U32, name="x_codes0", align_bytes=64),
             keep.tile([P, V], U32, name="x_codes1", align_bytes=64),
         ]
 
@@ -194,14 +199,14 @@ def tile_picked_hash_lin_silu_sub_l_kernel(tc, xT, w, b, offs, out):
                 in_=grouped[c][:, PACK * first : PACK * end],
             )
 
-        quantize_w(1)
-        both = inner[:].rearrange("p u g (v e) -> p g v u e", e=2)
+        nc.vector.tensor_tensor(inner[:, 1, 1, cut:], last_terms[0][:, cut:], last_terms[1][:, cut:], ADD)
+        both = inner.rearrange("p u g (v e) -> p g v u e", e=2)
         summed = grouped[1][:].rearrange("p (v u e) -> p v u e", u=2, e=2)
         for h in range(2):
             ids = slice(h * HALF, (h + 1) * HALF)
             nc.vector.tensor_tensor(summed[:, ids], both[:, 0, ids], both[:, 1, ids], ADD)
-        for h in range(2):
-            quantize_x(1, h * HALF, (h + 1) * HALF)
+        quantize_w(1)
+        quantize_x(1, 0, V)
         quantize_w(0)
         for h in range(2):
             quantize_x(0, h * HALF, (h + 1) * HALF)
@@ -211,7 +216,7 @@ def tile_picked_hash_lin_silu_sub_l_kernel(tc, xT, w, b, offs, out):
             for h in range(2):
                 nc.tensor.matmul_mx(
                     out=accs[h][:],
-                    lhsT=w_codes[c][:].bitcast(FP8X4),
+                    lhsT=w_codes[c].bitcast(FP8X4),
                     lhsT_scale=w_scales[:, c * N : (c + 1) * N],
                     rhs=x_codes[c][:, h * HALF : (h + 1) * HALF].bitcast(FP8X4),
                     rhs_scale=x_scales[:, c * V + h * HALF : c * V + (h + 1) * HALF],

@@ -25,7 +25,8 @@ BLOCKS = D * V // HALF
 BLOCK_COLS = HALF // 16
 
 HEAD, MIDDLE, LATE = 3, 2, 3
-SHARE = 128
+SHARE = 256
+W_FIRST = 32
 RUN = 2
 
 PAIR_WINDOW = 704
@@ -78,9 +79,7 @@ def tile_picked_hash_lin_silu_sub_l_kernel(tc, xT, w, b, offs, out):
         for u in range(2):
             nc.vector.memset(table[u][:, T:], 0.0)
 
-        early_sum = psum.tile([P, 2, 2, P], F32, name="early_sum")
-        late_sums = [psum.tile([P, 2, P], F32, name=f"late_sum{h}") for h in range(2)]
-        sums = [[early_sum[:, h] for h in range(2)], [late_sums[h][:] for h in range(2)]]
+        sums = [[psum.tile([P, 2, P], F32, name=f"sum{u}{h}") for h in range(2)] for u in range(2)]
 
         def look_up(on_vector, j, first, end, picked=None):
             if picked is None:
@@ -96,14 +95,14 @@ def tile_picked_hash_lin_silu_sub_l_kernel(tc, xT, w, b, offs, out):
 
         def add_turned(blocks):
             for j, h, values in blocks:
-                bank, total = ("early", 2 * BLOCKS) if j < 2 else (h, BLOCKS)
+                bank = (j // 2, h)
                 count = added.get(bank, 0)
                 nc.tensor.matmul(
                     sums[j // 2][h][:, j % 2, :],
                     lhsT=values,
                     rhs=identity[:],
                     start=(count == 0),
-                    stop=(count == total - 1),
+                    stop=(count == BLOCKS - 1),
                     is_transpose=True,
                 )
                 added.update({bank: count + 1})
@@ -141,32 +140,42 @@ def tile_picked_hash_lin_silu_sub_l_kernel(tc, xT, w, b, offs, out):
         add_turned(look_up(False, 2, 0, 2 * RUN))
         for first in range(2 * RUN, BLOCKS, RUN):
             add_turned(look_up(False, 2, first, first + RUN))
-        for i, block in enumerate((3, 4, 6, 5)):
-            add_turned(look_up(False, 3, block, block + 1))
-            if i < LATE:
-                add_turned(look_up(True, 3, i, i + 1))
+        add_turned(look_up(False, 3, LATE, LATE + RUN))
+        add_turned(look_up(True, 3, 0, RUN))
+        second, first = look_up(False, 3, LATE + RUN, BLOCKS - 1)
+        add_turned([first] + look_up(True, 3, RUN, LATE) + [second])
         add_turned(look_up(False, 3, BLOCKS - 1, BLOCKS, w_flat[:, N * PACK - 2 * HALF : N * PACK].bitcast(F32)))
 
         turned = [
-            keep.tile([P, 2, 2 * P], BF16, name="turned0", tag="two01", align_bytes=64),
-            keep.tile([P, 2, 2 * P], BF16, name="turned1", align_bytes=64),
+            [
+                keep.tile([P, 2 * P], BF16, name=f"turned{u}{h}", tag="two01" if u + h == 0 else f"turned{u}{h}", align_bytes=64)
+                for h in range(2)
+            ]
+            for u in range(2)
         ]
-        nc.vector.tensor_copy(
-            turned[0][:].rearrange("v h (p e) -> v h p e", e=2), early_sum[:].rearrange("v h e p -> v h p e")
-        )
-        w_in = w_raw[0][:].rearrange("p j (s c i) -> p s c j i", s=2, i=4)
-        w_out = w_grouped[:, 0].rearrange("p (s c i) j -> p s c j i", s=2, i=4)
-        nc.scalar.copy(w_out[:, 0], w_in[:, 0])
         backs = [psum.tile([P, 2, HALF], F32, name=f"back{h}") for h in range(2)]
+
+        def empty(copy, u, h):
+            copy(turned[u][h][:].rearrange("v (p e) -> v p e", e=2), sums[u][h][:].rearrange("v e p -> v p e"))
+
+        def turn_back(u, h):
+            nc.tensor.transpose(backs[h][:, u, :], turned[u][h][:].bitcast(F32), identity[:])
+
+        w_in = w_raw[0][:].rearrange("p j (c i) -> p c j i", i=4)
+        w_out = w_grouped[:, 0].rearrange("p (c i) j -> p c j i", i=4)
+        empty(nc.vector.tensor_copy, 0, 0)
+        empty(nc.scalar.copy, 0, 1)
+        nc.scalar.copy(w_out[:, : W_FIRST // 4], w_in[:, : W_FIRST // 4])
         for h in range(2):
-            nc.tensor.transpose(backs[h][:, 0, :], turned[0][:, h, :].bitcast(F32), identity[:])
+            turn_back(0, h)
         for h in range(2):
-            nc.scalar.copy(
-                turned[1][:, h].rearrange("v (p e) -> v p e", e=2), late_sums[h][:].rearrange("v e p -> v p e")
-            )
-            nc.tensor.transpose(backs[h][:, 1, :], turned[1][:, h, :].bitcast(F32), identity[:])
-        nc.scalar.copy(w_out[:, 1], w_in[:, 1])
-        grouped = [keep.tile([P, PACK * V], BF16, name=f"grouped{c}", align_bytes=64) for c in range(PASSES)]
+            empty(nc.scalar.copy, 1, h)
+            turn_back(1, h)
+        nc.scalar.copy(w_out[:, W_FIRST // 4 :], w_in[:, W_FIRST // 4 :])
+        grouped = [
+            keep.tile([P, PACK * V], BF16, name="grouped0", align_bytes=64),
+            keep.tile([P, PACK * V], BF16, name="grouped1", tag="picked20", align_bytes=64),
+        ]
         for h in range(2):
             nc.scalar.copy(
                 grouped[0][:, h * PACK * HALF : (h + 1) * PACK * HALF].bitcast(F32).rearrange("p (v u) -> p v u", u=2),
@@ -211,7 +220,7 @@ def tile_picked_hash_lin_silu_sub_l_kernel(tc, xT, w, b, offs, out):
         for h in range(2):
             quantize_x(0, h * HALF, (h + 1) * HALF)
 
-        accs = [psum.tile([P, HALF], F32, name=f"acc{h}", tag=bank) for h, bank in enumerate(("back0", "late_sum1"))]
+        accs = [psum.tile([P, HALF], F32, name=f"acc{h}", tag=bank) for h, bank in enumerate(("back0", "sum11"))]
         for c in (1, 0):
             for h in range(2):
                 nc.tensor.matmul_mx(

from contextlib import ExitStack

import concourse.mybir as mybir
from concourse.masks import make_identity

K, T, D, V, N = 1024, 512, 4, 256, 128
FLOPS = 2 * K * N * V

F32 = mybir.dt.float32
BF16 = mybir.dt.bfloat16
U32 = mybir.dt.uint32
U16 = mybir.dt.uint16
U8 = mybir.dt.uint8
FP8X4 = mybir.dt.float8_e4m3fn_x4
ADD = mybir.AluOpType.add
MULT = mybir.AluOpType.mult
COPY = mybir.ActivationFunctionType.Copy
SILU = mybir.ActivationFunctionType.Silu

P = 128
PACK = 4
PASSES = K // (P * PACK)
HALF = V // 2
BLOCKS = D * V // HALF
BLOCK_COLS = HALF // 16

HEAD, MIDDLE, LATE = 3, 2, 3
SHARE = 256
W_FIRST = 32
RUN = 2

PAIR_WINDOW = 704
ROW_WINDOWS = ((BLOCKS - HEAD) * HALF + 16, (BLOCKS - MIDDLE) * HALF + 16, 2 * RUN * HALF + 16, T)


def tile_picked_hash_lin_silu_sub_l_kernel(tc, xT, w, b, offs, out):
    nc = tc.nc
    with ExitStack() as ctx:
        keep = ctx.enter_context(tc.tile_pool(name="keep", bufs=1))
        psum = ctx.enter_context(tc.psum_pool(name="psum", bufs=1))

        offsets = keep.tile([P, BLOCKS * BLOCK_COLS], U16, name="offsets")
        x_rows = xT.rearrange("(c p j) t -> c p j t", c=PASSES, p=P, j=PACK)
        w_rows = w.rearrange("(c p j) n -> c p j n", c=PASSES, p=P, j=PACK)
        single = [keep.tile([P, ROW_WINDOWS[j]], F32, name=f"single{j}", align_bytes=64) for j in range(PACK)]
        pair = [keep.tile([P, T + PAIR_WINDOW], F32, name=f"pair{u}", align_bytes=64) for u in range(2)]
        table = [pair[u][:, T:] for u in range(2)]
        w_raw = [keep.tile([P, PACK, N], F32, name=f"w_raw{c}") for c in range(PASSES)]
        bias = keep.tile([P, 1], F32, name="bias")

        def load_single(j):
            nc.sync.dma_start(single[j][:, :T], x_rows[0][:, j])

        def load_pair(u):
            rows = pair[u][:, : 2 * T].rearrange("p (e t) -> p e t", e=2)
            nc.sync.dma_start(rows, x_rows[1][:, 2 * u : 2 * u + 2])

        load_single(0)
        nc.sync.dma_start(offsets[:], offs)
        load_pair(0)
        load_single(1)
        nc.sync.dma_start(w_raw[1][:], w_rows[1])
        load_pair(1)
        load_single(2)
        load_single(3)
        nc.sync.dma_start(w_raw[0][:], w_rows[0])
        nc.sync.dma_start(bias[:], b)

        table_in = keep.tile([P, 1], F32, name="table_in")
        table_out = keep.tile([P, 1], F32, name="table_out")
        nc.vector.memset(table_in[:], 0.0)
        nc.scalar.activation(table_out[:], table_in[:], SILU)

        identity = keep.tile([P, P], F32, name="identity")
        make_identity(nc, identity[:])
        for j in range(PACK):
            if ROW_WINDOWS[j] > T:
                nc.vector.memset(single[j][:, T:], 0.0)
        for u in range(2):
            nc.vector.memset(table[u][:, T:], 0.0)

        sums = [[psum.tile([P, 2, P], F32, name=f"sum{u}{h}") for h in range(2)] for u in range(2)]

        def look_up(on_vector, j, first, end, picked=None):
            if picked is None:
                picked = keep.tile([P, (end - first) * HALF], F32, name=f"picked{j}{first}", align_bytes=64)[:]
            looked_up = single[j][:].indirect(offsets[:, first * BLOCK_COLS : end * BLOCK_COLS])
            if on_vector:
                nc.vector.tensor_copy(picked, looked_up)
            else:
                nc.scalar.activation(picked, looked_up, COPY)
            return [(j, i % 2, picked[:, (i - first) * HALF : (i - first + 1) * HALF]) for i in range(first, end)]

        added = {}

        def add_turned(blocks):
            for j, h, values in blocks:
                bank = (j // 2, h)
                count = added.get(bank, 0)
                nc.tensor.matmul(
                    sums[j // 2][h][:, j % 2, :],
                    lhsT=values,
                    rhs=identity[:],
                    start=(count == 0),
                    stop=(count == BLOCKS - 1),
                    is_transpose=True,
                )
                added.update({bank: count + 1})

        def pack(copy, u):
            halves = pair[u][:, : 2 * T].bitcast(BF16).rearrange("p (e t s) -> p e t s", e=2, s=2)
            copy(halves[:, 1, :, 0], halves[:, 0, :, 1])

        def gather_words(u, g):
            two = keep.tile([P, 2 * V], U32, name=f"two{u}{g}", align_bytes=64)
            entries = offsets[:, 4 * g * BLOCK_COLS : 4 * (g + 1) * BLOCK_COLS]
            nc.vector.tensor_copy(two[:], table[u].bitcast(U32).indirect(entries))
            return two[:, :V].bitcast(BF16), two[:, V:].bitcast(BF16)

        head = look_up(True, 0, 0, HEAD)
        pack(nc.vector.tensor_copy, 0)
        pack(nc.scalar.copy, 1)
        w_flat = keep.tile([P, PASSES * N * PACK], BF16, name="w_flat", align_bytes=64)
        w_grouped = w_flat[:].rearrange("p (c n j) -> p c n j", c=PASSES, j=PACK)
        nc.gpsimd.tensor_scalar(w_grouped[:, 1], w_raw[1][:].rearrange("p j n -> p n j"), 1.0, 0.0, MULT, ADD)
        sums_flat = keep.tile([P, 8 * V + MIDDLE * HALF - SHARE], F32, name="sums_flat", align_bytes=64)
        inner = sums_flat[:, : 8 * V].rearrange("p (u g x) -> p u g x", u=2, g=2)
        for g in range(2):
            nc.gpsimd.tensor_tensor(inner[:, 0, g, :], *gather_words(0, g), ADD)
        middle = look_up(True, 1, BLOCKS - MIDDLE, BLOCKS, sums_flat[:, 8 * V - SHARE :])
        nc.gpsimd.tensor_tensor(inner[:, 1, 0, :], *gather_words(1, 0), ADD)
        last_terms = gather_words(1, 1)
        cut = 2 * V - SHARE
        nc.gpsimd.tensor_tensor(inner[:, 1, 1, :cut], last_terms[0][:, :cut], last_terms[1][:, :cut], ADD)

        add_turned(head)
        add_turned(look_up(False, 0, HEAD, BLOCKS))
        add_turned(look_up(False, 1, 0, BLOCKS - MIDDLE))
        add_turned(middle[::-1])
        add_turned(look_up(False, 2, 0, 2 * RUN))
        for first in range(2 * RUN, BLOCKS, RUN):
            add_turned(look_up(False, 2, first, first + RUN))
        add_turned(look_up(False, 3, LATE, LATE + RUN))
        add_turned(look_up(True, 3, 0, RUN))
        second, first = look_up(False, 3, LATE + RUN, BLOCKS - 1)
        add_turned([first] + look_up(True, 3, RUN, LATE) + [second])
        add_turned(look_up(False, 3, BLOCKS - 1, BLOCKS, w_flat[:, N * PACK - 2 * HALF : N * PACK].bitcast(F32)))

        turned = [
            [
                keep.tile([P, 2 * P], BF16, name=f"turned{u}{h}", tag="two01" if u + h == 0 else f"turned{u}{h}", align_bytes=64)
                for h in range(2)
            ]
            for u in range(2)
        ]
        backs = [psum.tile([P, 2, HALF], F32, name=f"back{h}") for h in range(2)]

        def empty(copy, u, h):
            copy(turned[u][h][:].rearrange("v (p e) -> v p e", e=2), sums[u][h][:].rearrange("v e p -> v p e"))

        def turn_back(u, h):
            nc.tensor.transpose(backs[h][:, u, :], turned[u][h][:].bitcast(F32), identity[:])

        w_in = w_raw[0][:].rearrange("p j (c i) -> p c j i", i=4)
        w_out = w_grouped[:, 0].rearrange("p (c i) j -> p c j i", i=4)
        empty(nc.vector.tensor_copy, 0, 0)
        empty(nc.scalar.copy, 0, 1)
        nc.scalar.copy(w_out[:, : W_FIRST // 4], w_in[:, : W_FIRST // 4])
        for h in range(2):
            turn_back(0, h)
        for h in range(2):
            empty(nc.scalar.copy, 1, h)
            turn_back(1, h)
        nc.scalar.copy(w_out[:, W_FIRST // 4 :], w_in[:, W_FIRST // 4 :])
        grouped = [
            keep.tile([P, PACK * V], BF16, name="grouped0", align_bytes=64),
            keep.tile([P, PACK * V], BF16, name="grouped1", tag="picked20", align_bytes=64),
        ]
        for h in range(2):
            nc.scalar.copy(
                grouped[0][:, h * PACK * HALF : (h + 1) * PACK * HALF].bitcast(F32).rearrange("p (v u) -> p v u", u=2),
                backs[h][:].rearrange("p u v -> p v u"),
            )

        w_scales = keep.tile([P, PASSES * N], U8, name="w_scales", align_bytes=64)
        x_scales = keep.tile([P, PASSES * V], U8, name="x_scales", align_bytes=64)
        w_codes = [
            keep.tile([P, N], U32, name="w_codes0", align_bytes=64)[:],
            keep.tile([P, N], U32, name="w_codes1", tag="two11", align_bytes=64)[:],
        ]

        def quantize_w(c):
            nc.vector.quantize_mx(
                out=w_codes[c].bitcast(FP8X4),
                scales=w_scales[:, c * N : (c + 1) * N],
                in_=w_flat[:, c * N * PACK : (c + 1) * N * PACK],
            )

        x_codes = [
            keep.tile([P, V], U32, name="x_codes0", align_bytes=64),
            keep.tile([P, V], U32, name="x_codes1", align_bytes=64),
        ]

        def quantize_x(c, first, end):
            nc.vector.quantize_mx(
                out=x_codes[c][:, first:end].bitcast(FP8X4),
                scales=x_scales[:, c * V + first : c * V + end],
                in_=grouped[c][:, PACK * first : PACK * end],
            )

        nc.vector.tensor_tensor(inner[:, 1, 1, cut:], last_terms[0][:, cut:], last_terms[1][:, cut:], ADD)
        both = inner.rearrange("p u g (v e) -> p g v u e", e=2)
        summed = grouped[1][:].rearrange("p (v u e) -> p v u e", u=2, e=2)
        for h in range(2):
            ids = slice(h * HALF, (h + 1) * HALF)
            nc.vector.tensor_tensor(summed[:, ids], both[:, 0, ids], both[:, 1, ids], ADD)
        quantize_w(1)
        quantize_x(1, 0, V)
        quantize_w(0)
        for h in range(2):
            quantize_x(0, h * HALF, (h + 1) * HALF)

        accs = [psum.tile([P, HALF], F32, name=f"acc{h}", tag=bank) for h, bank in enumerate(("back0", "sum11"))]
        for c in (1, 0):
            for h in range(2):
                nc.tensor.matmul_mx(
                    out=accs[h][:],
                    lhsT=w_codes[c].bitcast(FP8X4),
                    lhsT_scale=w_scales[:, c * N : (c + 1) * N],
                    rhs=x_codes[c][:, h * HALF : (h + 1) * HALF].bitcast(FP8X4),
                    rhs_scale=x_scales[:, c * V + h * HALF : c * V + (h + 1) * HALF],
                    start=(c == 1),
                    stop=(c == 0),
                )
        for h in range(2):
            result = keep.tile([P, HALF], F32, name=f"result{h}")
            nc.scalar.activation(result[:], accs[h][:], SILU, bias=bias[:])
            nc.sync.dma_start(out[:, h * HALF : (h + 1) * HALF], result[:])
